import numpy as np
import ml_dtypes


def mxq(x, axis, fmt="e4m3"):
    dtype, down = {"e4m3": (ml_dtypes.float8_e4m3fn, 7), "e5m2": (ml_dtypes.float8_e5m2, 14)}[fmt]
    v = np.moveaxis(np.asarray(x, np.float32).astype(ml_dtypes.bfloat16).astype(np.float64), axis, -1)
    blocks = v.reshape(v.shape[:-1] + (-1, 32))
    amax = np.abs(blocks).max(-1, keepdims=True)
    byte = np.maximum(np.where(amax > 0, np.frexp(amax)[1] - 1 + 127, 0) - down, 1)
    scale = np.exp2(byte - 127.0)
    codes = (blocks / scale).astype(np.float32).astype(dtype).astype(np.float64)
    return np.moveaxis((codes * scale).reshape(v.shape), -1, axis)


WIDE = False


def mx_kscale(k):
    if not WIDE:
        return np.ones(k)
    levels = np.array([10, -10, 5, -5, 0])
    if k % 512:
        return np.exp2(np.random.permutation(np.resize(levels, k // 32))).repeat(32)
    a = np.empty((k // 512, 16))
    for p in range(k // 512):
        a[p, :8] = np.random.permutation(np.resize(levels, 8))
        for g in range(8):
            far = levels[np.abs(levels - a[p, g]) >= 10]
            a[p, g + 8] = far[np.random.randint(len(far))]
    return np.exp2(a.ravel()).repeat(32)


def f64(x):
    return np.asarray(x).astype(np.float64)


def striped(idx):
    return np.tile(idx.reshape(-1, 16).T, (8, 1)).astype(np.uint16)


def unstriped(offs):
    return offs[:16].T.reshape(-1).astype(np.int64)


E2M1 = np.array([0.0, 0.5, 1.0, 1.5, 2.0, 3.0, 4.0, 6.0, -0.0, -0.5, -1.0, -1.5, -2.0, -3.0, -4.0, -6.0])


def pack_weight(w, fmt):
    k, n = w.shape
    w = f64(np.asarray(w, np.float32).astype(ml_dtypes.bfloat16)).reshape(k // 32, 32, n)
    amax = np.abs(w).max(1)
    if fmt == "e4m3":
        byte = np.frexp(amax)[1] - 1 + 127 - 7
    else:
        mant, ex = np.frexp(amax / 6.0)
        byte = np.where(mant > 0.5, ex, ex - 1) + 127
    byte = np.clip(np.where(amax > 0, byte, 1), 1, 254)
    scaled = (w * np.exp2(127.0 - byte)[:, None, :]).reshape(k, n).astype(np.float32)
    by_word = np.ascontiguousarray(scaled.reshape(k // 512, 128, 4, n).transpose(0, 1, 3, 2))
    if fmt == "e4m3":
        words = by_word.astype(ml_dtypes.float8_e4m3fn).view(np.uint8)
    else:
        c = by_word.astype(ml_dtypes.float4_e2m1fn).view(np.uint8) & 0xF
        words = (c[..., 0::2] | (c[..., 1::2] << 4)).reshape(k // 512, 128, 2 * n)
    return np.ascontiguousarray(words), np.ascontiguousarray(byte.astype(np.uint8).reshape(k // 512, 16, n))


def unpack_weight(words, scales, fmt):
    g, _, n = scales.shape
    words = np.ascontiguousarray(words).reshape(g, 128, n, -1)
    if fmt == "e4m3":
        vals = words.view(ml_dtypes.float8_e4m3fn).astype(np.float64)
    else:
        nib = np.empty((g, 128, n, 4), np.uint8)
        nib[..., 0::2] = words & 0xF
        nib[..., 1::2] = words >> 4
        vals = E2M1[nib]
    vals = vals * np.repeat(np.exp2(scales.astype(np.float64) - 127.0), 8, axis=1)[..., None]
    return vals.transpose(0, 1, 3, 2).reshape(g * 512, n)


def gelu(v):
    return 0.5 * v * (1.0 + np.tanh(np.sqrt(2.0 / np.pi) * (v + 0.044715 * v**3)))


T, S, P, K, H, N = 4096, 1024, 512, 1024, 1536, 512

def setup_inputs():
    n = np.random.standard_normal
    s = mx_kscale(K)[:, None]
    u = mx_kscale(H)[:, None]
    tab_words, tab_scales = pack_weight(n((K, T)) * s, "e4m3")
    wf_words, wf_scales = pack_weight(n((K, H)) / np.sqrt(K) / s, "e2m1")
    return {
        "tab_words": tab_words, "tab_scales": tab_scales,
        "offs": striped(np.random.permutation(T)[:S]),
        "wf_words": wf_words, "wf_scales": wf_scales,
        "pos1": striped(np.random.permutation(S)[:P]),
        "pos2": striped(np.random.permutation(S)[:P]),
        "pos3": striped(np.random.permutation(S)[:P]),
        "gain": (np.random.uniform(0.5, 1.5, H) * u[:, 0]).astype(np.float32),
        "ws": (1.5 * n((H, N)) / np.sqrt(H) / u).astype(np.float32),
        "bo": (0.5 * n(N)).astype(np.float32),
        "lev": np.random.uniform(0.5, 2.0, P).astype(np.float32),
    }

def reference(tab_words, tab_scales, offs, wf_words, wf_scales, pos1, pos2, pos3, gain, ws, bo, lev):
    v = unpack_weight(tab_words, tab_scales, "e4m3")[:, unstriped(offs)]
    wf = unpack_weight(wf_words, wf_scales, "e2m1")
    h = wf.T @ v
    serve = h[:, unstriped(pos1)]
    ret = h[:, unstriped(pos2)]
    follow = h[:, unstriped(pos3)]
    gate = 1.0 / (1.0 + np.exp(-serve))
    z = gate * (ret - follow) * f64(gain)[:, None]
    y = mxq(f64(ws), 0, "e4m3").T @ mxq(z, 0, "e4m3")
    return (y + f64(bo)[:, None]) * f64(lev)[None, :]

@@ -1,0 +1,264 @@
+from contextlib import ExitStack
+
+import concourse.mybir as mybir
+
+T, S, M, K, H, N = 4096, 1024, 512, 1024, 1536, 512
+FLOPS = 2 * K * H * S + 2 * H * N * M
+
+F32 = mybir.dt.float32
+BF16 = mybir.dt.bfloat16
+I32 = mybir.dt.int32
+U32 = mybir.dt.uint32
+U16 = mybir.dt.uint16
+U8 = mybir.dt.uint8
+FP8X4 = mybir.dt.float8_e4m3fn_x4
+FP4X4 = mybir.dt.float4_e2m1fn_x4
+ALU = mybir.AluOpType
+ACT = mybir.ActivationFunctionType
+
+P = 128
+PACK = 4
+PASS = P * PACK
+BANK = 512
+KP = K // PASS
+HP = H // PASS
+SLICES = H // P
+HALF = M // 2
+
+
+def tile_list_rally_shot_scores_kernel(
+    tc, tab_words, tab_scales, offs, wf_words, wf_scales, pos1, pos2, pos3, gain, ws, bo, lev, out
+):
+    nc = tc.nc
+    with ExitStack() as ctx:
+        lists = ctx.enter_context(tc.tile_pool(name="lists", bufs=1))
+        keep = ctx.enter_context(tc.tile_pool(name="keep", bufs=1))
+        psum = ctx.enter_context(tc.psum_pool(name="psum", bufs=1))
+
+        offs_sb = lists.tile([P, S // 16], U16, name="offs_sb")
+        pos1_sb = lists.tile([P, M // 16], U16, name="pos1_sb")
+        pos2_sb = lists.tile([P, M // 16], U16, name="pos2_sb")
+        pos3_sb = lists.tile([P, M // 16], U16, name="pos3_sb")
+
+        tab_w = [keep.tile([P, T], I32, name=f"tab_w{a}", align_bytes=64) for a in range(KP)]
+        tab_s = keep.tile([P, T], U8, name="tab_s", align_bytes=64)
+        picked_s = keep.tile([P, S], U8, name="picked_s", align_bytes=64)
+        v_s = [keep.tile([P, S], U8, name=f"v_s{a}", align_bytes=64) for a in range(KP)]
+        v_w = [[keep.tile([P, BANK], U32, name=f"v_w{a}_{c}", align_bytes=64) for c in range(2)] for a in range(KP)]
+        wf_w_raw = keep.tile([P, KP, H // 2], I32, name="wf_w_raw", align_bytes=64)
+        wf_s_raw = keep.tile([P, KP, H], U8, name="wf_s_raw", align_bytes=64)
+        wf_w = [keep.tile([P, KP, PASS], U16, name=f"wf_w{b}", align_bytes=64) for b in range(HP)]
+        wf_s = [keep.tile([P, KP, PASS], U8, name=f"wf_s{b}", align_bytes=64) for b in range(HP)]
+        gain_sb = keep.tile([P, HP, PACK], F32, name="gain_sb")
+        bo_sb = keep.tile([P, N // P], F32, name="bo_sb")
+        lev_sb = keep.tile([P, M], F32, name="lev_sb")
+        ws_raw = [keep.tile([P, PACK, N], F32, name=f"ws_raw{b}") for b in range(HP)]
+        warm = keep.tile([P, 2], F32, name="warm")
+
+        nc.vector.memset(warm[:, 0:1], 0.0)
+        nc.scalar.activation(warm[:, 1:2], warm[:, 0:1], ACT.Sigmoid)
+        nc.vector.memset(wf_s_raw[:].rearrange("p a c -> p (a c)").bitcast(I32), 0)
+        nc.gpsimd.memset(tab_s[32:64, :].bitcast(I32), 0)
+        nc.gpsimd.memset(tab_s[64:128, :].bitcast(I32), 0)
+        for a in range(KP):
+            nc.gpsimd.memset(v_s[a][:].bitcast(I32), 0)
+
+        def load_words(a):
+            nc.sync.dma_start(out=tab_w[a][:], in_=tab_words[a].rearrange("p t i -> p (t i)").bitcast(I32))
+
+        nc.sync.dma_start(offs_sb[:], offs)
+        nc.sync.dma_start(out=tab_s[0:32, :].bitcast(I32), in_=tab_scales.rearrange("a q t -> (a q) t").bitcast(I32))
+        load_words(0)
+        nc.sync.dma_start(out=wf_w_raw[:], in_=wf_words.bitcast(I32).rearrange("a p c -> p a c"))
+        for q in range(4):
+            nc.sync.dma_start(
+                out=wf_s_raw[32 * q : 32 * q + 4].bitcast(I32),
+                in_=wf_scales[:, 4 * q : 4 * q + 4, :].bitcast(I32).rearrange("a r c -> r a c"),
+            )
+        load_words(1)
+        nc.sync.dma_start(pos3_sb[:], pos3)
+        nc.sync.dma_start(pos2_sb[:], pos2)
+        nc.sync.dma_start(pos1_sb[:], pos1)
+        nc.sync.dma_start(out=gain_sb[:], in_=gain.rearrange("(b p t) -> p b t", p=P, t=PACK))
+        for b in range(HP):
+            nc.sync.dma_start(
+                out=ws_raw[b][:], in_=ws[PASS * b : PASS * (b + 1), :].rearrange("(p t) n -> p t n", t=PACK)
+            )
+        nc.sync.dma_start(out=lev_sb[:], in_=lev.partition_broadcast(P))
+        with nc.allow_non_contiguous_dma(reason="one baseline for each partition"):
+            nc.sync.dma_start(out=bo_sb[:], in_=bo.rearrange("(j p) -> p j", p=P))
+
+        nc.vector.tensor_copy(picked_s[:], tab_s[:].indirect(offs_sb[:]))
+        for a in range(KP):
+            for q in range(4):
+                row = 16 * a + 4 * q
+                nc.scalar.dma_start(
+                    out=v_s[a][32 * q : 32 * q + 4, :].bitcast(I32), in_=picked_s[row : row + 4, :].bitcast(I32)
+                )
+
+        def gather_words(a, c):
+            cols = offs_sb[:, c * (BANK // 16) : (c + 1) * (BANK // 16)]
+            nc.vector.tensor_copy(v_w[a][c][:], tab_w[a][:].bitcast(U32).indirect(cols))
+
+        gather_words(0, 0)
+        gather_words(0, 1)
+        for b in range(HP):
+            cols = slice(PASS * b, PASS * (b + 1))
+            nc.vector.tensor_copy(
+                out=wf_w[b][:].rearrange("p a (t m) -> p a t m", t=PACK),
+                in_=wf_w_raw[:].bitcast(U16)[:, :, cols].rearrange("p a (m t) -> p a t m", t=PACK),
+            )
+            nc.vector.tensor_copy(
+                out=wf_s[b][:].rearrange("p a (t m) -> p a t m", t=PACK),
+                in_=wf_s_raw[:, :, cols].rearrange("p a (m t) -> p a t m", t=PACK),
+            )
+        gather_words(1, 0)
+        gather_words(1, 1)
+
+        h = [keep.tile([P, S], F32, name=f"h{s}") for s in range(SLICES)]
+        gate = [None] * SLICES
+
+        def first_product(s):
+            b, t = divmod(s, PACK)
+            for c in range(2):
+                acc = psum.tile([P, BANK], F32, name="acc", tag=f"bank{(2 * s + c) % 4}")
+                for a in range(KP):
+                    nc.tensor.matmul_mx(
+                        out=acc[:],
+                        lhsT=wf_w[b][:, a, P * t : P * (t + 1)].bitcast(FP4X4),
+                        lhsT_scale=wf_s[b][:, a, P * t : P * (t + 1)],
+                        rhs=v_w[a][c][:].bitcast(FP8X4),
+                        rhs_scale=v_s[a][:, BANK * c : BANK * (c + 1)],
+                        start=(a == 0),
+                        stop=(a == KP - 1),
+                    )
+                nc.scalar.copy(h[s][:, BANK * c : BANK * (c + 1)], acc[:])
+
+        def make_gate(s):
+            gate[s] = keep.tile([P, M], F32, name="gate", tag="gate", bufs=6)
+            nc.scalar.activation(gate[s][:], h[s][:].indirect(pos1_sb[:]), ACT.Sigmoid)
+
+        pieces = [(0, 0, M), (1, 0, M), (2, 0, HALF), (2, HALF, HALF)]
+        planes = [keep.tile([P, PACK, w], BF16, name=f"planes{i}") for i, (b, m0, w) in enumerate(pieces)]
+        z_w = [keep.tile([P, w], U32, name=f"z_w{i}", align_bytes=64) for i, (b, m0, w) in enumerate(pieces)]
+        z_s = [keep.tile([P, w], U8, name=f"z_s{i}", align_bytes=64) for i, (b, m0, w) in enumerate(pieces)]
+        follow = {}
+        diff = {}
+
+        def pick_follow(i, t):
+            b, m0, w = pieces[i]
+            follow[i, t] = keep.tile([P, w], F32, name="follow", tag="follow", bufs=3)
+            nc.vector.tensor_copy(follow[i, t][:], h[PACK * b + t][:].indirect(pos3_sb[:, m0 // 16 : (m0 + w) // 16]))
+
+        def pick_diff(i, t):
+            b, m0, w = pieces[i]
+            diff[i, t] = keep.tile([P, w], F32, name="diff", tag="diff", bufs=3)
+            nc.vector.tensor_tensor(
+                diff[i, t][:],
+                h[PACK * b + t][:].indirect(pos2_sb[:, m0 // 16 : (m0 + w) // 16]),
+                follow[i, t][:],
+                ALU.subtract,
+            )
+
+        def make_z(i, t):
+            b, m0, w = pieces[i]
+            nc.vector.scalar_tensor_tensor(
+                out=planes[i][:, t, :],
+                in0=diff[i, t][:],
+                scalar=gain_sb[:, b, t : t + 1],
+                in1=gate[PACK * b + t][:, m0 : m0 + w],
+                op0=ALU.mult,
+                op1=ALU.mult,
+            )
+
+        def weave(copy, src, w):
+            woven = keep.tile([P, w, PACK], BF16, name="woven", tag="woven", bufs=3, align_bytes=64)
+            copy(
+                woven[:].rearrange("p (c i) t -> p c t i", i=4),
+                src.rearrange("p t (c i) -> p c t i", i=4),
+            )
+            return woven
+
+        def quantize(codes, scales, woven):
+            nc.vector.quantize_mx(
+                out=codes[:].bitcast(FP8X4), scales=scales[:], in_=woven[:].rearrange("p w t -> p (w t)")
+            )
+
+        ws_w = [keep.tile([P, N], U32, name=f"ws_w{b}", align_bytes=64) for b in range(HP)]
+        ws_s = [keep.tile([P, N], U8, name=f"ws_s{b}", align_bytes=64) for b in range(HP)]
+
+        def prepare_ws(b, copy):
+            quantize(ws_w[b], ws_s[b], weave(copy, ws_raw[b][:], N))
+
+        def finish_z(i, copy):
+            quantize(z_w[i], z_s[i], weave(copy, planes[i][:], pieces[i][2]))
+
+        scores = {}
+
+        def second_product(half, j, b):
+            if b == 0:
+                scores[half, j] = psum.tile([P, HALF], F32, name="score", tag=f"bank{4 * (1 - half) + j}")
+            i = b if b < HP - 1 else b + half
+            cols = slice(HALF * half, HALF * (half + 1)) if b < HP - 1 else slice(0, HALF)
+            nc.tensor.matmul_mx(
+                out=scores[half, j][:],
+                lhsT=ws_w[b][:, P * j : P * (j + 1)].bitcast(FP8X4),
+                lhsT_scale=ws_s[b][:, P * j : P * (j + 1)],
+                rhs=z_w[i][:, cols].bitcast(FP8X4),
+                rhs_scale=z_s[i][:, cols],
+                start=(b == 0),
+                stop=(b == HP - 1),
+            )
+
+        def store(half, j):
+            cols = slice(HALF * half, HALF * (half + 1))
+            res = keep.tile([P, HALF], F32, name="res", tag="res", bufs=8)
+            nc.vector.scalar_tensor_tensor(
+                out=res[:],
+                in0=scores[half, j][:],
+                scalar=bo_sb[:, j : j + 1],
+                in1=lev_sb[:, cols],
+                op0=ALU.add,
+                op1=ALU.mult,
+            )
+            nc.sync.dma_start(out=out[P * j : P * (j + 1), cols], in_=res[:])
+
+        steps = [(i, t) for i in range(len(pieces)) for t in range(PACK)]
+        first_product(0)
+        pick_follow(0, 0)
+        pick_diff(0, 0)
+        for n, (i, t) in enumerate(steps):
+            if n + 1 < SLICES:
+                first_product(n + 1)
+            if n < SLICES:
+                make_gate(n)
+            if n + 1 < len(steps):
+                pick_follow(*steps[n + 1])
+            make_z(i, t)
+            if n + 1 < len(steps):
+                pick_diff(*steps[n + 1])
+            if n == 3:
+                prepare_ws(0, nc.vector.tensor_copy)
+            if n == 6:
+                finish_z(0, nc.scalar.copy)
+            if n == 10:
+                finish_z(1, nc.scalar.copy)
+            if n == 11:
+                prepare_ws(1, nc.scalar.copy)
+                prepare_ws(2, nc.scalar.copy)
+                for half in range(2):
+                    for b in range(HP - 1):
+                        for j in range(N // P):
+                            second_product(half, j, b)
+            if n == 12:
+                finish_z(2, nc.scalar.copy)
+                for j in range(N // P):
+                    second_product(0, j, HP - 1)
+            if n == 14:
+                for j in range(N // P):
+                    store(0, j)
+        finish_z(3, nc.vector.tensor_copy)
+        for j in range(N // P):
+            second_product(1, j, HP - 1)
+        for j in range(N // P):
+            store(1, j)

@@ -1,6 +1,7 @@
 from contextlib import ExitStack
 
 import concourse.mybir as mybir
+from concourse.masks import make_identity
 
 T, S, M, K, H, N = 4096, 1024, 512, 1024, 1536, 512
 FLOPS = 2 * K * H * S + 2 * H * N * M
@@ -45,54 +46,70 @@ def tile_list_rally_shot_scores_kernel(
         picked_s = keep.tile([P, S], U8, name="picked_s", align_bytes=64)
         v_s = [keep.tile([P, S], U8, name=f"v_s{a}", align_bytes=64) for a in range(KP)]
         v_w = [[keep.tile([P, BANK], U32, name=f"v_w{a}_{c}", align_bytes=64) for c in range(2)] for a in range(KP)]
-        wf_w_raw = keep.tile([P, KP, H // 2], I32, name="wf_w_raw", align_bytes=64)
-        wf_s_raw = keep.tile([P, KP, H], U8, name="wf_s_raw", align_bytes=64)
-        wf_w = [keep.tile([P, KP, PASS], U16, name=f"wf_w{b}", align_bytes=64) for b in range(HP)]
-        wf_s = [keep.tile([P, KP, PASS], U8, name=f"wf_s{b}", align_bytes=64) for b in range(HP)]
-        gain_sb = keep.tile([P, HP, PACK], F32, name="gain_sb")
-        bo_sb = keep.tile([P, N // P], F32, name="bo_sb")
+        parts = [(0, 1), (1, HP - 1)]
+        wf_w_raw = [keep.tile([P, KP, n * PASS // 2], I32, name=f"wf_w_raw{b}") for b, n in parts]
+        wf_s_raw = [keep.tile([P, KP, n * PASS // 4], I32, name=f"wf_s_raw{b}") for b, n in parts]
+        wf_w = [keep.tile([P, KP, PASS // 2], I32, name=f"wf_w{b}", align_bytes=64) for b in range(HP)]
+        wf_s = [keep.tile([P, KP, PASS // 4], I32, name=f"wf_s{b}", align_bytes=64) for b in range(HP)]
+        rows = keep.tile([P, P], F32, name="rows")
+        ident = keep.tile([P, P], F32, name="ident")
+        per_part = keep.tile([P, SLICES + N // P], F32, name="per_part")
         lev_sb = keep.tile([P, M], F32, name="lev_sb")
         ws_raw = [keep.tile([P, PACK, N], F32, name=f"ws_raw{b}") for b in range(HP)]
         warm = keep.tile([P, 2], F32, name="warm")
 
         nc.vector.memset(warm[:, 0:1], 0.0)
         nc.scalar.activation(warm[:, 1:2], warm[:, 0:1], ACT.Sigmoid)
-        nc.vector.memset(wf_s_raw[:].rearrange("p a c -> p (a c)").bitcast(I32), 0)
+        nc.vector.memset(wf_s_raw[0][:], 0)
+        nc.vector.memset(tab_s[64:128, :].bitcast(I32), 0)
+        nc.vector.memset(rows[:], 0.0)
+        nc.vector.memset(wf_s_raw[1][:], 0)
         nc.gpsimd.memset(tab_s[32:64, :].bitcast(I32), 0)
-        nc.gpsimd.memset(tab_s[64:128, :].bitcast(I32), 0)
         for a in range(KP):
             nc.gpsimd.memset(v_s[a][:].bitcast(I32), 0)
+        make_identity(nc, ident[:])
 
         def load_words(a):
             nc.sync.dma_start(out=tab_w[a][:], in_=tab_words[a].rearrange("p t i -> p (t i)").bitcast(I32))
 
-        nc.sync.dma_start(offs_sb[:], offs)
-        nc.sync.dma_start(out=tab_s[0:32, :].bitcast(I32), in_=tab_scales.rearrange("a q t -> (a q) t").bitcast(I32))
-        load_words(0)
-        nc.sync.dma_start(out=wf_w_raw[:], in_=wf_words.bitcast(I32).rearrange("a p c -> p a c"))
-        for q in range(4):
+        def load_wf(i):
+            b, n = parts[i]
             nc.sync.dma_start(
-                out=wf_s_raw[32 * q : 32 * q + 4].bitcast(I32),
-                in_=wf_scales[:, 4 * q : 4 * q + 4, :].bitcast(I32).rearrange("a r c -> r a c"),
+                out=wf_w_raw[i][:],
+                in_=wf_words[:, :, 2 * PASS * b : 2 * PASS * (b + n)].bitcast(I32).rearrange("a p c -> p a c"),
             )
+            for q in range(4):
+                nc.sync.dma_start(
+                    out=wf_s_raw[i][32 * q : 32 * q + 4],
+                    in_=wf_scales[:, 4 * q : 4 * q + 4, PASS * b : PASS * (b + n)].bitcast(I32).rearrange("a r c -> r a c"),
+                )
+
+        nc.sync.dma_start(out=tab_s[0:32, :].bitcast(I32), in_=tab_scales.rearrange("a q t -> (a q) t").bitcast(I32))
+        nc.sync.dma_start(offs_sb[:], offs)
+        load_words(0)
+        load_wf(0)
         load_words(1)
         nc.sync.dma_start(pos3_sb[:], pos3)
         nc.sync.dma_start(pos2_sb[:], pos2)
         nc.sync.dma_start(pos1_sb[:], pos1)
-        nc.sync.dma_start(out=gain_sb[:], in_=gain.rearrange("(b p t) -> p b t", p=P, t=PACK))
         for b in range(HP):
             nc.sync.dma_start(
-                out=ws_raw[b][:], in_=ws[PASS * b : PASS * (b + 1), :].rearrange("(p t) n -> p t n", t=PACK)
+                out=rows[PACK * b : PACK * (b + 1), :].rearrange("t (q e) -> t q e", e=8),
+                in_=gain[PASS * b : PASS * (b + 1)].rearrange("(q t e) -> t q e", t=PACK, e=8),
             )
+        nc.sync.dma_start(out=rows[SLICES : SLICES + N // P, :], in_=bo.rearrange("(j p) -> j p", p=P))
+        load_wf(1)
+        for b in range(HP):
+            by_slot = ws[PASS * b : PASS * (b + 1), :].rearrange("(q t e) n -> t q e n", t=PACK, e=8)
+            for t in range(PACK):
+                nc.sync.dma_start(out=ws_raw[b][:, t, :], in_=by_slot[t])
         nc.sync.dma_start(out=lev_sb[:], in_=lev.partition_broadcast(P))
-        with nc.allow_non_contiguous_dma(reason="one baseline for each partition"):
-            nc.sync.dma_start(out=bo_sb[:], in_=bo.rearrange("(j p) -> p j", p=P))
 
         nc.vector.tensor_copy(picked_s[:], tab_s[:].indirect(offs_sb[:]))
         for a in range(KP):
             for q in range(4):
                 row = 16 * a + 4 * q
-                nc.scalar.dma_start(
+                nc.gpsimd.dma_start(
                     out=v_s[a][32 * q : 32 * q + 4, :].bitcast(I32), in_=picked_s[row : row + 4, :].bitcast(I32)
                 )
 
@@ -100,22 +117,26 @@ def tile_list_rally_shot_scores_kernel(
             cols = offs_sb[:, c * (BANK // 16) : (c + 1) * (BANK // 16)]
             nc.vector.tensor_copy(v_w[a][c][:], tab_w[a][:].bitcast(U32).indirect(cols))
 
+        def order_wf(b):
+            i = min(b, 1)
+            first = b - parts[i][0]
+            for raw, ordered, width in ((wf_w_raw, wf_w, PASS // 2), (wf_s_raw, wf_s, PASS // 4)):
+                nc.vector.tensor_copy(
+                    out=ordered[b][:].rearrange("p a (t q e) -> p a t q e", t=PACK, q=16),
+                    in_=raw[i][:, :, width * first : width * (first + 1)].rearrange("p a (q t e) -> p a t q e", t=PACK, q=16),
+                )
+
         gather_words(0, 0)
         gather_words(0, 1)
-        for b in range(HP):
-            cols = slice(PASS * b, PASS * (b + 1))
-            nc.vector.tensor_copy(
-                out=wf_w[b][:].rearrange("p a (t m) -> p a t m", t=PACK),
-                in_=wf_w_raw[:].bitcast(U16)[:, :, cols].rearrange("p a (m t) -> p a t m", t=PACK),
-            )
-            nc.vector.tensor_copy(
-                out=wf_s[b][:].rearrange("p a (t m) -> p a t m", t=PACK),
-                in_=wf_s_raw[:, :, cols].rearrange("p a (m t) -> p a t m", t=PACK),
-            )
+        order_wf(0)
         gather_words(1, 0)
         gather_words(1, 1)
 
-        h = [keep.tile([P, S], F32, name=f"h{s}") for s in range(SLICES)]
+        turned = psum.tile([P, P], F32, name="turned", tag="bank4")
+        nc.tensor.transpose(turned[:], rows[:], ident[:])
+        nc.scalar.copy(per_part[:], turned[:, 0 : SLICES + N // P])
+
+        h = [keep.tile([P, S], F32, name=f"h{s}", tag=f"h{s}") for s in range(SLICES)]
         gate = [None] * SLICES
 
         def first_product(s):
@@ -125,8 +146,8 @@ def tile_list_rally_shot_scores_kernel(
                 for a in range(KP):
                     nc.tensor.matmul_mx(
                         out=acc[:],
-                        lhsT=wf_w[b][:, a, P * t : P * (t + 1)].bitcast(FP4X4),
-                        lhsT_scale=wf_s[b][:, a, P * t : P * (t + 1)],
+                        lhsT=wf_w[b][:, a, P // 2 * t : P // 2 * (t + 1)].bitcast(FP4X4),
+                        lhsT_scale=wf_s[b][:, a, P // 4 * t : P // 4 * (t + 1)].bitcast(U8),
                         rhs=v_w[a][c][:].bitcast(FP8X4),
                         rhs_scale=v_s[a][:, BANK * c : BANK * (c + 1)],
                         start=(a == 0),
@@ -135,38 +156,31 @@ def tile_list_rally_shot_scores_kernel(
                 nc.scalar.copy(h[s][:, BANK * c : BANK * (c + 1)], acc[:])
 
         def make_gate(s):
-            gate[s] = keep.tile([P, M], F32, name="gate", tag="gate", bufs=6)
+            gate[s] = keep.tile([P, M], F32, name="gate", tag="gate", bufs=4)
             nc.scalar.activation(gate[s][:], h[s][:].indirect(pos1_sb[:]), ACT.Sigmoid)
 
+        planes = [keep.tile([P, PACK, M], BF16, name=f"planes{b}") for b in range(HP)]
         pieces = [(0, 0, M), (1, 0, M), (2, 0, HALF), (2, HALF, HALF)]
-        planes = [keep.tile([P, PACK, w], BF16, name=f"planes{i}") for i, (b, m0, w) in enumerate(pieces)]
         z_w = [keep.tile([P, w], U32, name=f"z_w{i}", align_bytes=64) for i, (b, m0, w) in enumerate(pieces)]
         z_s = [keep.tile([P, w], U8, name=f"z_s{i}", align_bytes=64) for i, (b, m0, w) in enumerate(pieces)]
-        follow = {}
-        diff = {}
+        follow = [None] * SLICES
+        diff = [None] * SLICES
 
-        def pick_follow(i, t):
-            b, m0, w = pieces[i]
-            follow[i, t] = keep.tile([P, w], F32, name="follow", tag="follow", bufs=3)
-            nc.vector.tensor_copy(follow[i, t][:], h[PACK * b + t][:].indirect(pos3_sb[:, m0 // 16 : (m0 + w) // 16]))
+        def pick_follow(s):
+            follow[s] = keep.tile([P, M], F32, name="follow", tag="follow", bufs=3)
+            nc.vector.tensor_copy(follow[s][:], h[s][:].indirect(pos3_sb[:]))
 
-        def pick_diff(i, t):
-            b, m0, w = pieces[i]
-            diff[i, t] = keep.tile([P, w], F32, name="diff", tag="diff", bufs=3)
-            nc.vector.tensor_tensor(
-                diff[i, t][:],
-                h[PACK * b + t][:].indirect(pos2_sb[:, m0 // 16 : (m0 + w) // 16]),
-                follow[i, t][:],
-                ALU.subtract,
-            )
+        def pick_diff(s):
+            diff[s] = keep.tile([P, M], F32, name=f"diff{s}", tag=f"h{s - 1}")
+            nc.vector.tensor_tensor(diff[s][:], h[s][:].indirect(pos2_sb[:]), follow[s][:], ALU.subtract)
 
-        def make_z(i, t):
-            b, m0, w = pieces[i]
+        def make_z(s):
+            b, t = divmod(s, PACK)
             nc.vector.scalar_tensor_tensor(
-                out=planes[i][:, t, :],
-                in0=diff[i, t][:],
-                scalar=gain_sb[:, b, t : t + 1],
-                in1=gate[PACK * b + t][:, m0 : m0 + w],
+                out=planes[b][:, t, :],
+                in0=diff[s][:],
+                scalar=per_part[:, s : s + 1],
+                in1=gate[s][:],
                 op0=ALU.mult,
                 op1=ALU.mult,
             )
@@ -191,7 +205,8 @@ def tile_list_rally_shot_scores_kernel(
             quantize(ws_w[b], ws_s[b], weave(copy, ws_raw[b][:], N))
 
         def finish_z(i, copy):
-            quantize(z_w[i], z_s[i], weave(copy, planes[i][:], pieces[i][2]))
+            b, m0, w = pieces[i]
+            quantize(z_w[i], z_s[i], weave(copy, planes[b][:, :, m0 : m0 + w], w))
 
         scores = {}
 
@@ -216,49 +231,48 @@ def tile_list_rally_shot_scores_kernel(
             nc.vector.scalar_tensor_tensor(
                 out=res[:],
                 in0=scores[half, j][:],
-                scalar=bo_sb[:, j : j + 1],
+                scalar=per_part[:, SLICES + j : SLICES + j + 1],
                 in1=lev_sb[:, cols],
                 op0=ALU.add,
                 op1=ALU.mult,
             )
             nc.sync.dma_start(out=out[P * j : P * (j + 1), cols], in_=res[:])
 
-        steps = [(i, t) for i in range(len(pieces)) for t in range(PACK)]
         first_product(0)
-        pick_follow(0, 0)
-        pick_diff(0, 0)
-        for n, (i, t) in enumerate(steps):
+        pick_follow(0)
+        pick_diff(0)
+        for n in range(SLICES):
             if n + 1 < SLICES:
                 first_product(n + 1)
-            if n < SLICES:
-                make_gate(n)
-            if n + 1 < len(steps):
-                pick_follow(*steps[n + 1])
-            make_z(i, t)
-            if n + 1 < len(steps):
-                pick_diff(*steps[n + 1])
-            if n == 3:
+            make_gate(n)
+            if n + 1 < SLICES:
+                pick_follow(n + 1)
+            make_z(n)
+            if n + 1 < SLICES:
+                pick_diff(n + 1)
+            if n == 0:
+                order_wf(1)
+            if n == 1:
                 prepare_ws(0, nc.vector.tensor_copy)
+            if n == 2:
+                order_wf(2)
+            if n == 4:
+                prepare_ws(1, nc.scalar.copy)
             if n == 6:
                 finish_z(0, nc.scalar.copy)
+            if n == 8:
+                prepare_ws(2, nc.scalar.copy)
             if n == 10:
                 finish_z(1, nc.scalar.copy)
-            if n == 11:
-                prepare_ws(1, nc.scalar.copy)
-                prepare_ws(2, nc.scalar.copy)
-                for half in range(2):
-                    for b in range(HP - 1):
-                        for j in range(N // P):
-                            second_product(half, j, b)
-            if n == 12:
-                finish_z(2, nc.scalar.copy)
+        for half in range(2):
+            for b in range(HP - 1):
                 for j in range(N // P):
-                    second_product(0, j, HP - 1)
-            if n == 14:
-                for j in range(N // P):
-                    store(0, j)
-        finish_z(3, nc.vector.tensor_copy)
-        for j in range(N // P):
-            second_product(1, j, HP - 1)
-        for j in range(N // P):
-            store(1, j)
+                    second_product(half, j, b)
+        finish_z(2, nc.vector.tensor_copy)
+        finish_z(3, nc.scalar.copy)
+        for half in range(2):
+            for j in range(N // P):
+                second_product(half, j, HP - 1)
+        for half in range(2):
+            for j in range(N // P):
+                store(half, j)

@@ -34,6 +34,7 @@ def tile_list_rally_shot_scores_kernel(
     with ExitStack() as ctx:
         lists = ctx.enter_context(tc.tile_pool(name="lists", bufs=1))
         keep = ctx.enter_context(tc.tile_pool(name="keep", bufs=1))
+        shared = ctx.enter_context(tc.tile_pool(name="shared", bufs=1))
         psum = ctx.enter_context(tc.psum_pool(name="psum", bufs=1))
 
         offs_sb = lists.tile([P, S // 16], U16, name="offs_sb")
@@ -41,77 +42,60 @@ def tile_list_rally_shot_scores_kernel(
         pos2_sb = lists.tile([P, M // 16], U16, name="pos2_sb")
         pos3_sb = lists.tile([P, M // 16], U16, name="pos3_sb")
 
-        tab_w = [keep.tile([P, T], I32, name=f"tab_w{a}", align_bytes=64) for a in range(KP)]
-        tab_s = keep.tile([P, T], U8, name="tab_s", align_bytes=64)
-        picked_s = keep.tile([P, S], U8, name="picked_s", align_bytes=64)
-        v_s = [keep.tile([P, S], U8, name=f"v_s{a}", align_bytes=64) for a in range(KP)]
+        def reuse(tag, shape, dtype, name):
+            if isinstance(tag, int):
+                return shared.tile(shape, dtype, name=name, tag=name, align_bytes=64, offset=tag)
+            return keep.tile(shape, dtype, name=name, tag=tag, align_bytes=64)
+
+        tab_w = [None] * KP
+        tab_s = reuse("tab_s", [P, T], U8, "tab_s")
+        picked_s = reuse("slot_c", [P, S], U8, "picked_s")
+        v_s = [keep.tile([P, S // 4], I32, name=f"v_s{a}", align_bytes=64) for a in range(KP)]
         v_w = [[keep.tile([P, BANK], U32, name=f"v_w{a}_{c}", align_bytes=64) for c in range(2)] for a in range(KP)]
         parts = [(0, 1), (1, HP - 1)]
-        wf_w_raw = [keep.tile([P, KP, n * PASS // 2], I32, name=f"wf_w_raw{b}") for b, n in parts]
-        wf_s_raw = [keep.tile([P, KP, n * PASS // 4], I32, name=f"wf_s_raw{b}") for b, n in parts]
-        wf_w = [keep.tile([P, KP, PASS // 2], I32, name=f"wf_w{b}", align_bytes=64) for b in range(HP)]
-        wf_s = [keep.tile([P, KP, PASS // 4], I32, name=f"wf_s{b}", align_bytes=64) for b in range(HP)]
-        rows = keep.tile([P, P], F32, name="rows")
+        wf_w_raw = [None] * 2
+        wf_s_raw = [None] * 2
+        wf_w = [None] * HP
+        wf_s = [None] * HP
         ident = keep.tile([P, P], F32, name="ident")
         per_part = keep.tile([P, SLICES + N // P], F32, name="per_part")
-        lev_sb = keep.tile([P, M], F32, name="lev_sb")
-        ws_raw = [keep.tile([P, PACK, N], F32, name=f"ws_raw{b}") for b in range(HP)]
-        warm = keep.tile([P, 2], F32, name="warm")
+        ws_raw = [None] * HP
+        warm = reuse(0, [P, 2], F32, "warm")
 
-        nc.vector.memset(warm[:, 0:1], 0.0)
-        nc.scalar.activation(warm[:, 1:2], warm[:, 0:1], ACT.Sigmoid)
-        nc.vector.memset(wf_s_raw[0][:], 0)
-        nc.vector.memset(tab_s[64:128, :].bitcast(I32), 0)
-        nc.vector.memset(rows[:], 0.0)
-        nc.vector.memset(wf_s_raw[1][:], 0)
-        nc.gpsimd.memset(tab_s[32:64, :].bitcast(I32), 0)
-        for a in range(KP):
-            nc.gpsimd.memset(v_s[a][:].bitcast(I32), 0)
-        make_identity(nc, ident[:])
-
-        def load_words(a):
+        def load_words(a, tag):
+            tab_w[a] = reuse(tag, [P, T], I32, f"tab_w{a}")
             nc.sync.dma_start(out=tab_w[a][:], in_=tab_words[a].rearrange("p t i -> p (t i)").bitcast(I32))
 
-        def load_wf(i):
+        def load_wf_words(i):
             b, n = parts[i]
+            wf_w_raw[i] = reuse("slot_d", [P, KP, n * PASS // 2], I32, f"wf_w_raw{i}")
             nc.sync.dma_start(
                 out=wf_w_raw[i][:],
                 in_=wf_words[:, :, 2 * PASS * b : 2 * PASS * (b + n)].bitcast(I32).rearrange("a p c -> p a c"),
             )
-            for q in range(4):
+
+        def load_wf_scales(i, quadrants):
+            b, n = parts[i]
+            if quadrants[0] == 0:
+                wf_s_raw[i] = reuse(16384, [P, KP, n * PASS // 4], I32, f"wf_s_raw{i}")
+                nc.gpsimd.memset(wf_s_raw[i][:], 0)
+            for q in quadrants:
                 nc.sync.dma_start(
                     out=wf_s_raw[i][32 * q : 32 * q + 4],
                     in_=wf_scales[:, 4 * q : 4 * q + 4, PASS * b : PASS * (b + n)].bitcast(I32).rearrange("a r c -> r a c"),
                 )
 
-        nc.sync.dma_start(out=tab_s[0:32, :].bitcast(I32), in_=tab_scales.rearrange("a q t -> (a q) t").bitcast(I32))
-        nc.sync.dma_start(offs_sb[:], offs)
-        load_words(0)
-        load_wf(0)
-        load_words(1)
-        nc.sync.dma_start(pos3_sb[:], pos3)
-        nc.sync.dma_start(pos2_sb[:], pos2)
-        nc.sync.dma_start(pos1_sb[:], pos1)
-        for b in range(HP):
-            nc.sync.dma_start(
-                out=rows[PACK * b : PACK * (b + 1), :].rearrange("t (q e) -> t q e", e=8),
-                in_=gain[PASS * b : PASS * (b + 1)].rearrange("(q t e) -> t q e", t=PACK, e=8),
-            )
-        nc.sync.dma_start(out=rows[SLICES : SLICES + N // P, :], in_=bo.rearrange("(j p) -> j p", p=P))
-        load_wf(1)
-        for b in range(HP):
+        def load_ws(b, tag):
+            ws_raw[b] = reuse(tag, [P, PACK, N], F32, f"ws_raw{b}")
             by_slot = ws[PASS * b : PASS * (b + 1), :].rearrange("(q t e) n -> t q e n", t=PACK, e=8)
             for t in range(PACK):
                 nc.sync.dma_start(out=ws_raw[b][:, t, :], in_=by_slot[t])
-        nc.sync.dma_start(out=lev_sb[:], in_=lev.partition_broadcast(P))
 
-        nc.vector.tensor_copy(picked_s[:], tab_s[:].indirect(offs_sb[:]))
-        for a in range(KP):
-            for q in range(4):
-                row = 16 * a + 4 * q
-                nc.gpsimd.dma_start(
-                    out=v_s[a][32 * q : 32 * q + 4, :].bitcast(I32), in_=picked_s[row : row + 4, :].bitcast(I32)
-                )
+        def move_scales(a, q):
+            row = 16 * a + 4 * q
+            nc.sync.dma_start(
+                out=v_s[a][32 * q : 32 * q + 4, :], in_=picked_s[row : row + 4, :].bitcast(I32)
+            )
 
         def gather_words(a, c):
             cols = offs_sb[:, c * (BANK // 16) : (c + 1) * (BANK // 16)]
@@ -120,21 +104,57 @@ def tile_list_rally_shot_scores_kernel(
         def order_wf(b):
             i = min(b, 1)
             first = b - parts[i][0]
+            wf_w[b] = reuse(8192 + 3072 * (b - 1) if b else 26624, [P, KP, PASS // 2], I32, f"wf_w{b}")
+            wf_s[b] = reuse(10240 + 3072 * (b - 1) if b else 28672, [P, KP, PASS // 4], I32, f"wf_s{b}")
             for raw, ordered, width in ((wf_w_raw, wf_w, PASS // 2), (wf_s_raw, wf_s, PASS // 4)):
                 nc.vector.tensor_copy(
                     out=ordered[b][:].rearrange("p a (t q e) -> p a t q e", t=PACK, q=16),
                     in_=raw[i][:, :, width * first : width * (first + 1)].rearrange("p a (q t e) -> p a t q e", t=PACK, q=16),
                 )
 
+        nc.sync.dma_start(out=tab_s[0:32, :].bitcast(I32), in_=tab_scales.rearrange("a q t -> (a q) t").bitcast(I32))
+        nc.sync.dma_start(offs_sb[:], offs)
+        nc.sync.dma_start(pos3_sb[:], pos3)
+        nc.sync.dma_start(pos2_sb[:], pos2)
+        load_words(0, 18432)
+        load_wf_words(0)
+        load_wf_scales(0, [0, 1, 2, 3])
+        nc.sync.dma_start(pos1_sb[:], pos1)
+        nc.vector.memset(warm[:, 0:1], 0.0)
+        nc.scalar.activation(warm[:, 1:2], warm[:, 0:1], ACT.Sigmoid)
+        load_words(1, 0)
+
+        nc.vector.memset(tab_s[64:128, :].bitcast(I32), 0)
+        nc.vector.memset(tab_s[32:64, :].bitcast(I32), 0)
+        nc.gpsimd.memset(v_s[1][:], 0)
+        make_identity(nc, ident[:])
+
+        nc.vector.tensor_copy(picked_s[:], tab_s[:].indirect(offs_sb[:]))
+        moves = [(a, q) for a in range(KP) for q in range(4)]
+        nc.vector.tensor_copy(v_s[0][:], picked_s[:].bitcast(I32))
+        for a, q in moves[1:]:
+            move_scales(a, q)
+
         gather_words(0, 0)
         gather_words(0, 1)
         order_wf(0)
+
+        rows = reuse("slot_c", [P, P], F32, "rows")
+        nc.gpsimd.memset(rows[:], 0.0)
+        for b in range(HP):
+            nc.sync.dma_start(
+                out=rows[PACK * b : PACK * (b + 1), :].rearrange("t (q e) -> t q e", e=8),
+                in_=gain[PASS * b : PASS * (b + 1)].rearrange("(q t e) -> t q e", t=PACK, e=8),
+            )
+        nc.sync.dma_start(out=rows[SLICES : SLICES + N // P, :], in_=bo.rearrange("(j p) -> j p", p=P))
+        load_wf_words(1)
+        load_wf_scales(1, [0, 1, 2, 3])
+        load_ws(0, 18432)
+
         gather_words(1, 0)
         gather_words(1, 1)
+        load_ws(1, 0)
 
-        turned = psum.tile([P, P], F32, name="turned", tag="bank4")
-        nc.tensor.transpose(turned[:], rows[:], ident[:])
-        nc.scalar.copy(per_part[:], turned[:, 0 : SLICES + N // P])
 
         h = [keep.tile([P, S], F32, name=f"h{s}", tag=f"h{s}") for s in range(SLICES)]
         gate = [None] * SLICES
@@ -143,15 +163,16 @@ def tile_list_rally_shot_scores_kernel(
             b, t = divmod(s, PACK)
             for c in range(2):
                 acc = psum.tile([P, BANK], F32, name="acc", tag=f"bank{(2 * s + c) % 4}")
-                for a in range(KP):
+                order = (0, 1) if s == 0 else (1, 0)
+                for a in order:
                     nc.tensor.matmul_mx(
                         out=acc[:],
                         lhsT=wf_w[b][:, a, P // 2 * t : P // 2 * (t + 1)].bitcast(FP4X4),
                         lhsT_scale=wf_s[b][:, a, P // 4 * t : P // 4 * (t + 1)].bitcast(U8),
                         rhs=v_w[a][c][:].bitcast(FP8X4),
-                        rhs_scale=v_s[a][:, BANK * c : BANK * (c + 1)],
-                        start=(a == 0),
-                        stop=(a == KP - 1),
+                        rhs_scale=v_s[a][:, BANK // 4 * c : BANK // 4 * (c + 1)].bitcast(U8),
+                        start=(a == order[0]),
+                        stop=(a == order[-1]),
                     )
                 nc.scalar.copy(h[s][:, BANK * c : BANK * (c + 1)], acc[:])
 
@@ -241,6 +262,11 @@ def tile_list_rally_shot_scores_kernel(
         first_product(0)
         pick_follow(0)
         pick_diff(0)
+        turned = psum.tile([P, P], F32, name="turned", tag="bank1")
+        nc.tensor.transpose(turned[:], rows[:], ident[:])
+        nc.scalar.copy(per_part[:], turned[:, 0 : SLICES + N // P])
+        lev_sb = reuse("slot_c", [P, M], F32, "lev_sb")
+        nc.sync.dma_start(out=lev_sb[:], in_=lev.partition_broadcast(P))
         for n in range(SLICES):
             if n + 1 < SLICES:
                 first_product(n + 1)
@@ -256,6 +282,7 @@ def tile_list_rally_shot_scores_kernel(
                 prepare_ws(0, nc.vector.tensor_copy)
             if n == 2:
                 order_wf(2)
+                load_ws(2, "slot_d")
             if n == 4:
                 prepare_ws(1, nc.scalar.copy)
             if n == 6:

@@ -20,11 +20,27 @@ ACT = mybir.ActivationFunctionType
 P = 128
 PACK = 4
 PASS = P * PACK
+BLOCKS = 16
+RUN = 8
+QUADS = 4
+GROUP = 16
 BANK = 512
 KP = K // PASS
 HP = H // PASS
 SLICES = H // P
+N_TILES = N // P
 HALF = M // 2
+H_BANKS = 4
+
+TAB1_AT = 0
+WF_LATER_AT = 8192
+WF_SCALES_AT = 16384
+TAB0_AT = 18432
+WF_FIRST_AT = TAB0_AT + 8192
+WF_WORD_BYTES = 2048
+WF_BYTES = 3072
+SMALL_SLOT = "slot_c"
+WF_SLOT = "slot_d"
 
 
 def tile_list_rally_shot_scores_kernel(
@@ -37,92 +53,93 @@ def tile_list_rally_shot_scores_kernel(
         shared = ctx.enter_context(tc.tile_pool(name="shared", bufs=1))
         psum = ctx.enter_context(tc.psum_pool(name="psum", bufs=1))
 
-        offs_sb = lists.tile([P, S // 16], U16, name="offs_sb")
-        pos1_sb = lists.tile([P, M // 16], U16, name="pos1_sb")
-        pos2_sb = lists.tile([P, M // 16], U16, name="pos2_sb")
-        pos3_sb = lists.tile([P, M // 16], U16, name="pos3_sb")
+        offs_sb = lists.tile([P, S // GROUP], U16, name="offs_sb")
+        pos1_sb = lists.tile([P, M // GROUP], U16, name="pos1_sb")
+        pos2_sb = lists.tile([P, M // GROUP], U16, name="pos2_sb")
+        pos3_sb = lists.tile([P, M // GROUP], U16, name="pos3_sb")
 
-        def reuse(tag, shape, dtype, name):
-            if isinstance(tag, int):
-                return shared.tile(shape, dtype, name=name, tag=name, align_bytes=64, offset=tag)
+        def placed(offset, shape, dtype, name):
+            return shared.tile(shape, dtype, name=name, tag=name, align_bytes=64, offset=offset)
+
+        def tenant(tag, shape, dtype, name):
             return keep.tile(shape, dtype, name=name, tag=tag, align_bytes=64)
 
         tab_w = [None] * KP
-        tab_s = reuse("tab_s", [P, T], U8, "tab_s")
-        picked_s = reuse("slot_c", [P, S], U8, "picked_s")
+        tab_s = tenant("tab_s", [P, T], U8, "tab_s")
+        picked_s = tenant(SMALL_SLOT, [P, S], U8, "picked_s")
         v_s = [keep.tile([P, S // 4], I32, name=f"v_s{a}", align_bytes=64) for a in range(KP)]
         v_w = [[keep.tile([P, BANK], U32, name=f"v_w{a}_{c}", align_bytes=64) for c in range(2)] for a in range(KP)]
         parts = [(0, 1), (1, HP - 1)]
-        wf_w_raw = [None] * 2
-        wf_s_raw = [None] * 2
+        wf_w_raw = [None] * len(parts)
+        wf_s_raw = [None] * len(parts)
         wf_w = [None] * HP
         wf_s = [None] * HP
         ident = keep.tile([P, P], F32, name="ident")
-        per_part = keep.tile([P, SLICES + N // P], F32, name="per_part")
+        per_part = keep.tile([P, SLICES + N_TILES], F32, name="per_part")
         ws_raw = [None] * HP
-        warm = reuse(0, [P, 2], F32, "warm")
+        warm = placed(TAB1_AT, [P, 2], F32, "warm")
 
-        def load_words(a, tag):
-            tab_w[a] = reuse(tag, [P, T], I32, f"tab_w{a}")
+        def load_words(a, offset):
+            tab_w[a] = placed(offset, [P, T], I32, f"tab_w{a}")
             nc.sync.dma_start(out=tab_w[a][:], in_=tab_words[a].rearrange("p t i -> p (t i)").bitcast(I32))
 
         def load_wf_words(i):
-            b, n = parts[i]
-            wf_w_raw[i] = reuse("slot_d", [P, KP, n * PASS // 2], I32, f"wf_w_raw{i}")
+            b, count = parts[i]
+            wf_w_raw[i] = tenant(WF_SLOT, [P, KP, count * PASS // 2], I32, f"wf_w_raw{i}")
             nc.sync.dma_start(
                 out=wf_w_raw[i][:],
-                in_=wf_words[:, :, 2 * PASS * b : 2 * PASS * (b + n)].bitcast(I32).rearrange("a p c -> p a c"),
+                in_=wf_words[:, :, 2 * PASS * b : 2 * PASS * (b + count)].bitcast(I32).rearrange("a p c -> p a c"),
             )
 
-        def load_wf_scales(i, quadrants):
-            b, n = parts[i]
-            if quadrants[0] == 0:
-                wf_s_raw[i] = reuse(16384, [P, KP, n * PASS // 4], I32, f"wf_s_raw{i}")
-                nc.gpsimd.memset(wf_s_raw[i][:], 0)
-            for q in quadrants:
+        def load_wf_scales(i):
+            b, count = parts[i]
+            wf_s_raw[i] = placed(WF_SCALES_AT, [P, KP, count * PASS // 4], I32, f"wf_s_raw{i}")
+            nc.gpsimd.memset(wf_s_raw[i][:], 0)
+            for quad in range(QUADS):
+                live = wf_scales[:, 4 * quad : 4 * quad + 4, PASS * b : PASS * (b + count)]
                 nc.sync.dma_start(
-                    out=wf_s_raw[i][32 * q : 32 * q + 4],
-                    in_=wf_scales[:, 4 * q : 4 * q + 4, PASS * b : PASS * (b + n)].bitcast(I32).rearrange("a r c -> r a c"),
+                    out=wf_s_raw[i][32 * quad : 32 * quad + 4], in_=live.bitcast(I32).rearrange("a r c -> r a c")
                 )
 
-        def load_ws(b, tag):
-            ws_raw[b] = reuse(tag, [P, PACK, N], F32, f"ws_raw{b}")
-            by_slot = ws[PASS * b : PASS * (b + 1), :].rearrange("(q t e) n -> t q e n", t=PACK, e=8)
+        def load_ws(b, raw):
+            ws_raw[b] = raw
+            by_code = ws[PASS * b : PASS * (b + 1), :].rearrange("(q t e) n -> t q e n", t=PACK, e=RUN)
             for t in range(PACK):
-                nc.sync.dma_start(out=ws_raw[b][:, t, :], in_=by_slot[t])
+                nc.sync.dma_start(out=raw[:, t, :], in_=by_code[t])
 
-        def move_scales(a, q):
-            row = 16 * a + 4 * q
-            nc.sync.dma_start(
-                out=v_s[a][32 * q : 32 * q + 4, :], in_=picked_s[row : row + 4, :].bitcast(I32)
-            )
+        def move_scales(a, quad):
+            row = BLOCKS * a + 4 * quad
+            queue = nc.sync if a else nc.gpsimd
+            queue.dma_start(out=v_s[a][32 * quad : 32 * quad + 4, :], in_=picked_s[row : row + 4, :].bitcast(I32))
 
         def gather_words(a, c):
-            cols = offs_sb[:, c * (BANK // 16) : (c + 1) * (BANK // 16)]
-            nc.vector.tensor_copy(v_w[a][c][:], tab_w[a][:].bitcast(U32).indirect(cols))
+            entries = offs_sb[:, c * (BANK // GROUP) : (c + 1) * (BANK // GROUP)]
+            nc.vector.tensor_copy(v_w[a][c][:], tab_w[a][:].bitcast(U32).indirect(entries))
 
         def order_wf(b):
             i = min(b, 1)
             first = b - parts[i][0]
-            wf_w[b] = reuse(8192 + 3072 * (b - 1) if b else 26624, [P, KP, PASS // 2], I32, f"wf_w{b}")
-            wf_s[b] = reuse(10240 + 3072 * (b - 1) if b else 28672, [P, KP, PASS // 4], I32, f"wf_s{b}")
+            offset = WF_LATER_AT + WF_BYTES * (b - 1) if b else WF_FIRST_AT
+            wf_w[b] = placed(offset, [P, KP, PASS // 2], I32, f"wf_w{b}")
+            wf_s[b] = placed(offset + WF_WORD_BYTES, [P, KP, PASS // 4], I32, f"wf_s{b}")
             for raw, ordered, width in ((wf_w_raw, wf_w, PASS // 2), (wf_s_raw, wf_s, PASS // 4)):
+                source = raw[i][:, :, width * first : width * (first + 1)]
                 nc.vector.tensor_copy(
-                    out=ordered[b][:].rearrange("p a (t q e) -> p a t q e", t=PACK, q=16),
-                    in_=raw[i][:, :, width * first : width * (first + 1)].rearrange("p a (q t e) -> p a t q e", t=PACK, q=16),
+                    out=ordered[b][:].rearrange("p a (t q e) -> p a t q e", t=PACK, q=BLOCKS),
+                    in_=source.rearrange("p a (q t e) -> p a t q e", t=PACK, q=BLOCKS),
                 )
 
         nc.sync.dma_start(out=tab_s[0:32, :].bitcast(I32), in_=tab_scales.rearrange("a q t -> (a q) t").bitcast(I32))
         nc.sync.dma_start(offs_sb[:], offs)
         nc.sync.dma_start(pos3_sb[:], pos3)
         nc.sync.dma_start(pos2_sb[:], pos2)
-        load_words(0, 18432)
+        load_words(0, TAB0_AT)
         load_wf_words(0)
-        load_wf_scales(0, [0, 1, 2, 3])
+        load_wf_scales(0)
         nc.sync.dma_start(pos1_sb[:], pos1)
         nc.vector.memset(warm[:, 0:1], 0.0)
         nc.scalar.activation(warm[:, 1:2], warm[:, 0:1], ACT.Sigmoid)
-        load_words(1, 0)
+        load_words(1, TAB1_AT)
 
         nc.vector.memset(tab_s[64:128, :].bitcast(I32), 0)
         nc.vector.memset(tab_s[32:64, :].bitcast(I32), 0)
@@ -130,40 +147,39 @@ def tile_list_rally_shot_scores_kernel(
         make_identity(nc, ident[:])
 
         nc.vector.tensor_copy(picked_s[:], tab_s[:].indirect(offs_sb[:]))
-        moves = [(a, q) for a in range(KP) for q in range(4)]
         nc.vector.tensor_copy(v_s[0][:], picked_s[:].bitcast(I32))
-        for a, q in moves[1:]:
-            move_scales(a, q)
+        for a in range(KP):
+            for quad in range(0 if a else 1, QUADS):
+                move_scales(a, quad)
 
         gather_words(0, 0)
         gather_words(0, 1)
         order_wf(0)
 
-        rows = reuse("slot_c", [P, P], F32, "rows")
+        rows = tenant(SMALL_SLOT, [P, P], F32, "rows")
         nc.gpsimd.memset(rows[:], 0.0)
         for b in range(HP):
             nc.sync.dma_start(
-                out=rows[PACK * b : PACK * (b + 1), :].rearrange("t (q e) -> t q e", e=8),
-                in_=gain[PASS * b : PASS * (b + 1)].rearrange("(q t e) -> t q e", t=PACK, e=8),
+                out=rows[PACK * b : PACK * (b + 1), :].rearrange("t (q e) -> t q e", e=RUN),
+                in_=gain[PASS * b : PASS * (b + 1)].rearrange("(q t e) -> t q e", t=PACK, e=RUN),
             )
-        nc.sync.dma_start(out=rows[SLICES : SLICES + N // P, :], in_=bo.rearrange("(j p) -> j p", p=P))
+        nc.sync.dma_start(out=rows[SLICES : SLICES + N_TILES, :], in_=bo.rearrange("(j p) -> j p", p=P))
         load_wf_words(1)
-        load_wf_scales(1, [0, 1, 2, 3])
-        load_ws(0, 18432)
+        load_wf_scales(1)
+        load_ws(0, placed(TAB0_AT, [P, PACK, N], F32, "ws_raw0"))
 
         gather_words(1, 0)
         gather_words(1, 1)
-        load_ws(1, 0)
-
+        load_ws(1, placed(TAB1_AT, [P, PACK, N], F32, "ws_raw1"))
 
         h = [keep.tile([P, S], F32, name=f"h{s}", tag=f"h{s}") for s in range(SLICES)]
         gate = [None] * SLICES
 
         def first_product(s):
             b, t = divmod(s, PACK)
+            order = (0, 1) if s == 0 else (1, 0)
             for c in range(2):
-                acc = psum.tile([P, BANK], F32, name="acc", tag=f"bank{(2 * s + c) % 4}")
-                order = (0, 1) if s == 0 else (1, 0)
+                acc = psum.tile([P, BANK], F32, name="acc", tag=f"bank{(2 * s + c) % H_BANKS}")
                 for a in order:
                     nc.tensor.matmul_mx(
                         out=acc[:],
@@ -180,7 +196,7 @@ def tile_list_rally_shot_scores_kernel(
             gate[s] = keep.tile([P, M], F32, name="gate", tag="gate", bufs=4)
             nc.scalar.activation(gate[s][:], h[s][:].indirect(pos1_sb[:]), ACT.Sigmoid)
 
-        planes = [keep.tile([P, PACK, M], BF16, name=f"planes{b}") for b in range(HP)]
+        z_rows = [keep.tile([P, PACK, M], BF16, name=f"planes{b}") for b in range(HP)]
         pieces = [(0, 0, M), (1, 0, M), (2, 0, HALF), (2, HALF, HALF)]
         z_w = [keep.tile([P, w], U32, name=f"z_w{i}", align_bytes=64) for i, (b, m0, w) in enumerate(pieces)]
         z_s = [keep.tile([P, w], U8, name=f"z_s{i}", align_bytes=64) for i, (b, m0, w) in enumerate(pieces)]
@@ -198,7 +214,7 @@ def tile_list_rally_shot_scores_kernel(
         def make_z(s):
             b, t = divmod(s, PACK)
             nc.vector.scalar_tensor_tensor(
-                out=planes[b][:, t, :],
+                out=z_rows[b][:, t, :],
                 in0=diff[s][:],
                 scalar=per_part[:, s : s + 1],
                 in1=gate[s][:],
@@ -206,12 +222,15 @@ def tile_list_rally_shot_scores_kernel(
                 op1=ALU.mult,
             )
 
-        def weave(copy, src, w):
+        def weave(copies, src, w):
             woven = keep.tile([P, w, PACK], BF16, name="woven", tag="woven", bufs=3, align_bytes=64)
-            copy(
-                woven[:].rearrange("p (c i) t -> p c t i", i=4),
-                src.rearrange("p t (c i) -> p c t i", i=4),
-            )
+            share = w // len(copies)
+            for n, copy in enumerate(copies):
+                cols = slice(share * n, share * (n + 1))
+                copy(
+                    woven[:, cols, :].rearrange("p (c i) t -> p c t i", i=4),
+                    src[:, :, cols].rearrange("p t (c i) -> p c t i", i=4),
+                )
             return woven
 
         def quantize(codes, scales, woven):
@@ -222,20 +241,21 @@ def tile_list_rally_shot_scores_kernel(
         ws_w = [keep.tile([P, N], U32, name=f"ws_w{b}", align_bytes=64) for b in range(HP)]
         ws_s = [keep.tile([P, N], U8, name=f"ws_s{b}", align_bytes=64) for b in range(HP)]
 
-        def prepare_ws(b, copy):
-            quantize(ws_w[b], ws_s[b], weave(copy, ws_raw[b][:], N))
+        def prepare_ws(b, *copies):
+            quantize(ws_w[b], ws_s[b], weave(copies, ws_raw[b][:], N))
 
         def finish_z(i, copy):
             b, m0, w = pieces[i]
-            quantize(z_w[i], z_s[i], weave(copy, planes[b][:, :, m0 : m0 + w], w))
+            quantize(z_w[i], z_s[i], weave([copy], z_rows[b][:, :, m0 : m0 + w], w))
 
         scores = {}
 
         def second_product(half, j, b):
             if b == 0:
-                scores[half, j] = psum.tile([P, HALF], F32, name="score", tag=f"bank{4 * (1 - half) + j}")
-            i = b if b < HP - 1 else b + half
-            cols = slice(HALF * half, HALF * (half + 1)) if b < HP - 1 else slice(0, HALF)
+                scores[half, j] = psum.tile([P, HALF], F32, name="score", tag=f"bank{H_BANKS * (1 - half) + j}")
+            last = b == HP - 1
+            i = b + half if last else b
+            cols = slice(0, HALF) if last else slice(HALF * half, HALF * (half + 1))
             nc.tensor.matmul_mx(
                 out=scores[half, j][:],
                 lhsT=ws_w[b][:, P * j : P * (j + 1)].bitcast(FP8X4),
@@ -243,12 +263,12 @@ def tile_list_rally_shot_scores_kernel(
                 rhs=z_w[i][:, cols].bitcast(FP8X4),
                 rhs_scale=z_s[i][:, cols],
                 start=(b == 0),
-                stop=(b == HP - 1),
+                stop=last,
             )
 
         def store(half, j):
             cols = slice(HALF * half, HALF * (half + 1))
-            res = keep.tile([P, HALF], F32, name="res", tag="res", bufs=8)
+            res = keep.tile([P, HALF], F32, name="res", tag="res", bufs=2 * N_TILES)
             nc.vector.scalar_tensor_tensor(
                 out=res[:],
                 in0=scores[half, j][:],
@@ -259,47 +279,50 @@ def tile_list_rally_shot_scores_kernel(
             )
             nc.sync.dma_start(out=out[P * j : P * (j + 1), cols], in_=res[:])
 
+        def order_last_wf():
+            order_wf(2)
+            load_ws(2, tenant(WF_SLOT, [P, PACK, N], F32, "ws_raw2"))
+
+        beside = {
+            0: lambda: order_wf(1),
+            1: lambda: prepare_ws(0, nc.vector.tensor_copy, nc.scalar.copy),
+            2: order_last_wf,
+            4: lambda: prepare_ws(1, nc.scalar.copy),
+            6: lambda: finish_z(0, nc.scalar.copy),
+            8: lambda: prepare_ws(2, nc.scalar.copy),
+            10: lambda: finish_z(1, nc.scalar.copy),
+        }
+
         first_product(0)
         pick_follow(0)
         pick_diff(0)
         turned = psum.tile([P, P], F32, name="turned", tag="bank1")
         nc.tensor.transpose(turned[:], rows[:], ident[:])
-        nc.scalar.copy(per_part[:], turned[:, 0 : SLICES + N // P])
-        lev_sb = reuse("slot_c", [P, M], F32, "lev_sb")
+        nc.scalar.copy(per_part[:], turned[:, 0 : SLICES + N_TILES])
+        lev_sb = tenant(SMALL_SLOT, [P, M], F32, "lev_sb")
         nc.sync.dma_start(out=lev_sb[:], in_=lev.partition_broadcast(P))
-        for n in range(SLICES):
-            if n + 1 < SLICES:
-                first_product(n + 1)
-            make_gate(n)
-            if n + 1 < SLICES:
-                pick_follow(n + 1)
-            make_z(n)
-            if n + 1 < SLICES:
-                pick_diff(n + 1)
-            if n == 0:
-                order_wf(1)
-            if n == 1:
-                prepare_ws(0, nc.vector.tensor_copy)
-            if n == 2:
-                order_wf(2)
-                load_ws(2, "slot_d")
-            if n == 4:
-                prepare_ws(1, nc.scalar.copy)
-            if n == 6:
-                finish_z(0, nc.scalar.copy)
-            if n == 8:
-                prepare_ws(2, nc.scalar.copy)
-            if n == 10:
-                finish_z(1, nc.scalar.copy)
+        for s in range(SLICES):
+            more = s + 1 < SLICES
+            if more:
+                first_product(s + 1)
+            make_gate(s)
+            if more:
+                pick_follow(s + 1)
+            make_z(s)
+            if more:
+                pick_diff(s + 1)
+            if s in beside:
+                beside[s]()
+
         for half in range(2):
             for b in range(HP - 1):
-                for j in range(N // P):
+                for j in range(N_TILES):
                     second_product(half, j, b)
         finish_z(2, nc.vector.tensor_copy)
         finish_z(3, nc.scalar.copy)
         for half in range(2):
-            for j in range(N // P):
+            for j in range(N_TILES):
                 second_product(half, j, HP - 1)
         for half in range(2):
-            for j in range(N // P):
+            for j in range(N_TILES):
                 store(half, j)

@@ -30,6 +30,7 @@ HP = H // PASS
 SLICES = H // P
 N_TILES = N // P
 HALF = M // 2
+VECTOR_FOLLOW_EVERY = 3
 H_BANKS = 4
 
 TAB1_AT = 0
@@ -193,7 +194,7 @@ def tile_list_rally_shot_scores_kernel(
                 nc.scalar.copy(h[s][:, BANK * c : BANK * (c + 1)], acc[:])
 
         def make_gate(s):
-            gate[s] = keep.tile([P, M], F32, name="gate", tag="gate", bufs=4)
+            gate[s] = keep.tile([P, M], F32, name=f"gate{s}")
             nc.scalar.activation(gate[s][:], h[s][:].indirect(pos1_sb[:]), ACT.Sigmoid)
 
         z_rows = [keep.tile([P, PACK, M], BF16, name=f"planes{b}") for b in range(HP)]
@@ -204,11 +205,14 @@ def tile_list_rally_shot_scores_kernel(
         diff = [None] * SLICES
 
         def pick_follow(s):
-            follow[s] = keep.tile([P, M], F32, name="follow", tag="follow", bufs=3)
-            nc.vector.tensor_copy(follow[s][:], h[s][:].indirect(pos3_sb[:]))
+            follow[s] = keep.tile([P, M], F32, name=f"follow{s}")
+            if s % VECTOR_FOLLOW_EVERY == 0:
+                nc.vector.tensor_copy(follow[s][:], h[s][:].indirect(pos3_sb[:]))
+            else:
+                nc.scalar.activation(follow[s][:], h[s][:].indirect(pos3_sb[:]), ACT.Copy)
 
         def pick_diff(s):
-            diff[s] = keep.tile([P, M], F32, name=f"diff{s}", tag=f"h{s - 1}")
+            diff[s] = keep.tile([P, M], F32, name="diff", tag="diff", bufs=3)
             nc.vector.tensor_tensor(diff[s][:], h[s][:].indirect(pos2_sb[:]), follow[s][:], ALU.subtract)
 
         def make_z(s):
@@ -285,12 +289,12 @@ def tile_list_rally_shot_scores_kernel(
 
         beside = {
             0: lambda: order_wf(1),
-            1: lambda: prepare_ws(0, nc.vector.tensor_copy, nc.scalar.copy),
+            1: lambda: prepare_ws(0, nc.vector.tensor_copy),
             2: order_last_wf,
-            4: lambda: prepare_ws(1, nc.scalar.copy),
-            6: lambda: finish_z(0, nc.scalar.copy),
-            8: lambda: prepare_ws(2, nc.scalar.copy),
-            10: lambda: finish_z(1, nc.scalar.copy),
+            4: lambda: finish_z(0, nc.vector.tensor_copy),
+            5: lambda: prepare_ws(1, nc.vector.tensor_copy),
+            7: lambda: prepare_ws(2, nc.vector.tensor_copy),
+            8: lambda: finish_z(1, nc.vector.tensor_copy),
         }
 
         first_product(0)
@@ -308,9 +312,8 @@ def tile_list_rally_shot_scores_kernel(
             make_gate(s)
             if more:
                 pick_follow(s + 1)
-            make_z(s)
-            if more:
                 pick_diff(s + 1)
+            make_z(s)
             if s in beside:
                 beside[s]()
 

@@ -30,18 +30,20 @@ HP = H // PASS
 SLICES = H // P
 N_TILES = N // P
 HALF = M // 2
-VECTOR_FOLLOW_EVERY = 3
-H_BANKS = 4
+VECTOR_FOLLOWS = 4
+BANKS = 8
 
 TAB1_AT = 0
 WF_LATER_AT = 8192
-WF_SCALES_AT = 16384
-TAB0_AT = 18432
+TAB0_AT = 16384
 WF_FIRST_AT = TAB0_AT + 8192
-WF_WORD_BYTES = 2048
-WF_BYTES = 3072
-SMALL_SLOT = "slot_c"
-WF_SLOT = "slot_d"
+ROWS_AT = TAB0_AT + 12288
+WF_RAW_AT = 32768
+Z1_WOVEN_AT = 40960
+WF_BYTES = 2048
+H_BYTES = 4 * S
+V_SCALES = S // 4
+WF_SCALES = H // 4
 
 
 def tile_list_rally_shot_scores_kernel(
@@ -52,6 +54,7 @@ def tile_list_rally_shot_scores_kernel(
         lists = ctx.enter_context(tc.tile_pool(name="lists", bufs=1))
         keep = ctx.enter_context(tc.tile_pool(name="keep", bufs=1))
         shared = ctx.enter_context(tc.tile_pool(name="shared", bufs=1))
+        rows_of_h = ctx.enter_context(tc.tile_pool(name="rows_of_h", bufs=1))
         psum = ctx.enter_context(tc.psum_pool(name="psum", bufs=1))
 
         offs_sb = lists.tile([P, S // GROUP], U16, name="offs_sb")
@@ -62,45 +65,30 @@ def tile_list_rally_shot_scores_kernel(
         def placed(offset, shape, dtype, name):
             return shared.tile(shape, dtype, name=name, tag=name, align_bytes=64, offset=offset)
 
-        def tenant(tag, shape, dtype, name):
-            return keep.tile(shape, dtype, name=name, tag=tag, align_bytes=64)
+        def after_h(s, shape, dtype, name, at=0):
+            return rows_of_h.tile(shape, dtype, name=name, tag=name, align_bytes=64, offset=H_BYTES * s + at)
 
         tab_w = [None] * KP
-        tab_s = tenant("tab_s", [P, T], U8, "tab_s")
-        picked_s = tenant(SMALL_SLOT, [P, S], U8, "picked_s")
-        v_s = [keep.tile([P, S // 4], I32, name=f"v_s{a}", align_bytes=64) for a in range(KP)]
+        tab_s = keep.tile([P, T], U8, name="tab_s", align_bytes=64)
+        picked_s = keep.tile([P, S], U8, name="picked_s", align_bytes=64)
+        planes = [keep.tile([P, V_SCALES + WF_SCALES], I32, name=f"plane{a}", align_bytes=64) for a in range(KP)]
         v_w = [[keep.tile([P, BANK], U32, name=f"v_w{a}_{c}", align_bytes=64) for c in range(2)] for a in range(KP)]
-        parts = [(0, 1), (1, HP - 1)]
-        wf_w_raw = [None] * len(parts)
-        wf_s_raw = [None] * len(parts)
+        wf_s_raw = keep.tile([KP * BLOCKS, WF_SCALES], I32, name="wf_s_raw")
         wf_w = [None] * HP
-        wf_s = [None] * HP
         ident = keep.tile([P, P], F32, name="ident")
         per_part = keep.tile([P, SLICES + N_TILES], F32, name="per_part")
         ws_raw = [None] * HP
-        warm = placed(TAB1_AT, [P, 2], F32, "warm")
+        warm = keep.tile([P, 2], F32, name="warm")
 
         def load_words(a, offset):
             tab_w[a] = placed(offset, [P, T], I32, f"tab_w{a}")
             nc.sync.dma_start(out=tab_w[a][:], in_=tab_words[a].rearrange("p t i -> p (t i)").bitcast(I32))
 
-        def load_wf_words(i):
-            b, count = parts[i]
-            wf_w_raw[i] = tenant(WF_SLOT, [P, KP, count * PASS // 2], I32, f"wf_w_raw{i}")
+        def load_wf_words(raw, b, count):
             nc.sync.dma_start(
-                out=wf_w_raw[i][:],
+                out=raw[:],
                 in_=wf_words[:, :, 2 * PASS * b : 2 * PASS * (b + count)].bitcast(I32).rearrange("a p c -> p a c"),
             )
-
-        def load_wf_scales(i):
-            b, count = parts[i]
-            wf_s_raw[i] = placed(WF_SCALES_AT, [P, KP, count * PASS // 4], I32, f"wf_s_raw{i}")
-            nc.gpsimd.memset(wf_s_raw[i][:], 0)
-            for quad in range(QUADS):
-                live = wf_scales[:, 4 * quad : 4 * quad + 4, PASS * b : PASS * (b + count)]
-                nc.sync.dma_start(
-                    out=wf_s_raw[i][32 * quad : 32 * quad + 4], in_=live.bitcast(I32).rearrange("a r c -> r a c")
-                )
 
         def load_ws(b, raw):
             ws_raw[b] = raw
@@ -108,56 +96,60 @@ def tile_list_rally_shot_scores_kernel(
             for t in range(PACK):
                 nc.sync.dma_start(out=raw[:, t, :], in_=by_code[t])
 
-        def move_scales(a, quad):
+        def move_scales(a, quad, queue):
             row = BLOCKS * a + 4 * quad
-            queue = nc.sync if a else nc.gpsimd
-            queue.dma_start(out=v_s[a][32 * quad : 32 * quad + 4, :], in_=picked_s[row : row + 4, :].bitcast(I32))
+            queue.dma_start(out=planes[a][32 * quad : 32 * quad + 4, :], in_=planes[0][row : row + 4, :])
 
         def gather_words(a, c):
             entries = offs_sb[:, c * (BANK // GROUP) : (c + 1) * (BANK // GROUP)]
             nc.vector.tensor_copy(v_w[a][c][:], tab_w[a][:].bitcast(U32).indirect(entries))
 
-        def order_wf(b):
-            i = min(b, 1)
-            first = b - parts[i][0]
+        def order_wf(b, raw):
             offset = WF_LATER_AT + WF_BYTES * (b - 1) if b else WF_FIRST_AT
             wf_w[b] = placed(offset, [P, KP, PASS // 2], I32, f"wf_w{b}")
-            wf_s[b] = placed(offset + WF_WORD_BYTES, [P, KP, PASS // 4], I32, f"wf_s{b}")
-            for raw, ordered, width in ((wf_w_raw, wf_w, PASS // 2), (wf_s_raw, wf_s, PASS // 4)):
-                source = raw[i][:, :, width * first : width * (first + 1)]
-                nc.vector.tensor_copy(
-                    out=ordered[b][:].rearrange("p a (t q e) -> p a t q e", t=PACK, q=BLOCKS),
-                    in_=source.rearrange("p a (q t e) -> p a t q e", t=PACK, q=BLOCKS),
-                )
+            nc.vector.tensor_copy(
+                out=wf_w[b][:].rearrange("p a (t q e) -> p a t q e", t=PACK, q=BLOCKS),
+                in_=raw.rearrange("p a (q t e) -> p a t q e", t=PACK, q=BLOCKS),
+            )
 
-        nc.sync.dma_start(out=tab_s[0:32, :].bitcast(I32), in_=tab_scales.rearrange("a q t -> (a q) t").bitcast(I32))
+        rows32 = slice(0, KP * BLOCKS)
+        nc.sync.dma_start(out=tab_s[rows32, :].bitcast(I32), in_=tab_scales.rearrange("a q t -> (a q) t").bitcast(I32))
         nc.sync.dma_start(offs_sb[:], offs)
+        nc.sync.dma_start(out=wf_s_raw[:], in_=wf_scales.rearrange("a q c -> (a q) c").bitcast(I32))
         nc.sync.dma_start(pos3_sb[:], pos3)
         nc.sync.dma_start(pos2_sb[:], pos2)
-        load_words(0, TAB0_AT)
-        load_wf_words(0)
-        load_wf_scales(0)
         nc.sync.dma_start(pos1_sb[:], pos1)
+        load_words(0, TAB0_AT)
+        wf_first = keep.tile([P, KP, PASS // 2], I32, name="wf_first")
+        load_wf_words(wf_first, 0, 1)
         nc.vector.memset(warm[:, 0:1], 0.0)
         nc.scalar.activation(warm[:, 1:2], warm[:, 0:1], ACT.Sigmoid)
         load_words(1, TAB1_AT)
+        wf_later = placed(WF_RAW_AT, [P, KP, PASS], I32, "wf_later")
+        load_wf_words(wf_later, 1, HP - 1)
 
         nc.vector.memset(tab_s[64:128, :].bitcast(I32), 0)
         nc.vector.memset(tab_s[32:64, :].bitcast(I32), 0)
-        nc.gpsimd.memset(v_s[1][:], 0)
+        for a in range(KP):
+            nc.gpsimd.memset(planes[a][:], 0)
         make_identity(nc, ident[:])
 
         nc.vector.tensor_copy(picked_s[:], tab_s[:].indirect(offs_sb[:]))
-        nc.vector.tensor_copy(v_s[0][:], picked_s[:].bitcast(I32))
+        nc.vector.tensor_copy(
+            out=planes[0][rows32, V_SCALES:].rearrange("p (b t q e) -> p b t q e", b=HP, t=PACK, q=BLOCKS),
+            in_=wf_s_raw[:].rearrange("p (b q t e) -> p b t q e", b=HP, t=PACK, q=BLOCKS),
+        )
+        nc.vector.tensor_copy(planes[0][rows32, 0:V_SCALES], picked_s[rows32, :].bitcast(I32))
         for a in range(KP):
             for quad in range(0 if a else 1, QUADS):
-                move_scales(a, quad)
+                move_scales(a, quad, nc.gpsimd if (a, quad) == (KP - 1, QUADS - 1) else nc.scalar)
 
         gather_words(0, 0)
         gather_words(0, 1)
-        order_wf(0)
+        order_wf(0, wf_first[:])
 
-        rows = tenant(SMALL_SLOT, [P, P], F32, "rows")
+        load_ws(0, placed(TAB0_AT, [P, PACK, N], F32, "ws_raw0"))
+        rows = placed(ROWS_AT, [P, P], F32, "rows")
         nc.gpsimd.memset(rows[:], 0.0)
         for b in range(HP):
             nc.sync.dma_start(
@@ -165,98 +157,120 @@ def tile_list_rally_shot_scores_kernel(
                 in_=gain[PASS * b : PASS * (b + 1)].rearrange("(q t e) -> t q e", t=PACK, e=RUN),
             )
         nc.sync.dma_start(out=rows[SLICES : SLICES + N_TILES, :], in_=bo.rearrange("(j p) -> j p", p=P))
-        load_wf_words(1)
-        load_wf_scales(1)
-        load_ws(0, placed(TAB0_AT, [P, PACK, N], F32, "ws_raw0"))
 
         gather_words(1, 0)
         gather_words(1, 1)
         load_ws(1, placed(TAB1_AT, [P, PACK, N], F32, "ws_raw1"))
 
-        h = [keep.tile([P, S], F32, name=f"h{s}", tag=f"h{s}") for s in range(SLICES)]
-        gate = [None] * SLICES
+        h = [after_h(s, [P, S], F32, f"h{s}") for s in range(SLICES)]
+        acc = {}
+
+        def first_pass(s, c, a, start, stop):
+            b, t = divmod(s, PACK)
+            if start:
+                acc[s, c] = psum.tile([P, BANK], F32, name="acc", tag=f"bank{(2 * s + c) % BANKS}")
+            nc.tensor.matmul_mx(
+                out=acc[s, c][:],
+                lhsT=wf_w[b][:, a, P // 2 * t : P // 2 * (t + 1)].bitcast(FP4X4),
+                lhsT_scale=planes[a][:, V_SCALES + P // 4 * s : V_SCALES + P // 4 * (s + 1)].bitcast(U8),
+                rhs=v_w[a][c][:].bitcast(FP8X4),
+                rhs_scale=planes[a][:, BANK // 4 * c : BANK // 4 * (c + 1)].bitcast(U8),
+                start=start,
+                stop=stop,
+            )
+
+        def empty_bank(s, c, copy):
+            copy(h[s][:, BANK * c : BANK * (c + 1)], acc[s, c][:])
 
         def first_product(s):
-            b, t = divmod(s, PACK)
-            order = (0, 1) if s == 0 else (1, 0)
             for c in range(2):
-                acc = psum.tile([P, BANK], F32, name="acc", tag=f"bank{(2 * s + c) % H_BANKS}")
-                for a in order:
-                    nc.tensor.matmul_mx(
-                        out=acc[:],
-                        lhsT=wf_w[b][:, a, P // 2 * t : P // 2 * (t + 1)].bitcast(FP4X4),
-                        lhsT_scale=wf_s[b][:, a, P // 4 * t : P // 4 * (t + 1)].bitcast(U8),
-                        rhs=v_w[a][c][:].bitcast(FP8X4),
-                        rhs_scale=v_s[a][:, BANK // 4 * c : BANK // 4 * (c + 1)].bitcast(U8),
-                        start=(a == order[0]),
-                        stop=(a == order[-1]),
-                    )
-                nc.scalar.copy(h[s][:, BANK * c : BANK * (c + 1)], acc[:])
+                if s >= PACK:
+                    first_pass(s, c, 0, True, False)
+                first_pass(s, c, 1, False, True)
+                empty_bank(s, c, nc.scalar.copy)
 
-        def make_gate(s):
-            gate[s] = keep.tile([P, M], F32, name=f"gate{s}")
-            nc.scalar.activation(gate[s][:], h[s][:].indirect(pos1_sb[:]), ACT.Sigmoid)
-
-        z_rows = [keep.tile([P, PACK, M], BF16, name=f"planes{b}") for b in range(HP)]
+        whole = SLICES - PACK
+        units = [(s, 0, M) for s in range(whole)]
+        units = units + [(s, m0, HALF) for m0 in (0, HALF) for s in range(whole, SLICES)]
         pieces = [(0, 0, M), (1, 0, M), (2, 0, HALF), (2, HALF, HALF)]
-        z_w = [keep.tile([P, w], U32, name=f"z_w{i}", align_bytes=64) for i, (b, m0, w) in enumerate(pieces)]
-        z_s = [keep.tile([P, w], U8, name=f"z_s{i}", align_bytes=64) for i, (b, m0, w) in enumerate(pieces)]
-        follow = [None] * SLICES
-        diff = [None] * SLICES
+        z_rows = [keep.tile([P, PACK, w], BF16, name=f"z_rows{i}") for i, (b, m0, w) in enumerate(pieces)]
+        gate = [None] * len(units)
+        follow = [None] * len(units)
+        diff = [None] * len(units)
 
-        def pick_follow(s):
-            follow[s] = keep.tile([P, M], F32, name=f"follow{s}")
-            if s % VECTOR_FOLLOW_EVERY == 0:
-                nc.vector.tensor_copy(follow[s][:], h[s][:].indirect(pos3_sb[:]))
+        def picked(u, pos_sb):
+            s, m0, w = units[u]
+            return h[s][:].indirect(pos_sb[:, m0 // GROUP : (m0 + w) // GROUP])
+
+        def make_gate(u):
+            gate[u] = keep.tile([P, units[u][2]], F32, name=f"gate{u}")
+            nc.scalar.activation(gate[u][:], picked(u, pos1_sb), ACT.Sigmoid)
+
+        def pick_follow(u):
+            if u == whole + 1:
+                follow[u] = placed(Z1_WOVEN_AT, [P, units[u][2]], F32, f"follow{u}")
             else:
-                nc.scalar.activation(follow[s][:], h[s][:].indirect(pos3_sb[:]), ACT.Copy)
+                follow[u] = keep.tile([P, units[u][2]], F32, name=f"follow{u}")
+            if u < VECTOR_FOLLOWS:
+                nc.vector.tensor_copy(follow[u][:], picked(u, pos3_sb))
+            else:
+                nc.scalar.activation(follow[u][:], picked(u, pos3_sb), ACT.Copy)
 
-        def pick_diff(s):
-            diff[s] = keep.tile([P, M], F32, name="diff", tag="diff", bufs=3)
-            nc.vector.tensor_tensor(diff[s][:], h[s][:].indirect(pos2_sb[:]), follow[s][:], ALU.subtract)
+        def pick_diff(u):
+            if 2 <= u < VECTOR_FOLLOWS:
+                diff[u] = after_h(u - 2, [P, M], F32, f"diff{u}")
+            else:
+                diff[u] = keep.tile([P, units[u][2]], F32, name="diff", tag="diff", bufs=4)
+            nc.vector.tensor_tensor(diff[u][:], picked(u, pos2_sb), follow[u][:], ALU.subtract)
 
-        def make_z(s):
-            b, t = divmod(s, PACK)
+        def make_z(u):
+            s = units[u][0]
             nc.vector.scalar_tensor_tensor(
-                out=z_rows[b][:, t, :],
-                in0=diff[s][:],
+                out=z_rows[u // PACK][:, u % PACK, :],
+                in0=diff[u][:],
                 scalar=per_part[:, s : s + 1],
-                in1=gate[s][:],
+                in1=gate[u][:],
                 op0=ALU.mult,
                 op1=ALU.mult,
             )
 
-        def weave(copies, src, w):
-            woven = keep.tile([P, w, PACK], BF16, name="woven", tag="woven", bufs=3, align_bytes=64)
-            share = w // len(copies)
-            for n, copy in enumerate(copies):
-                cols = slice(share * n, share * (n + 1))
-                copy(
-                    woven[:, cols, :].rearrange("p (c i) t -> p c t i", i=4),
-                    src[:, :, cols].rearrange("p t (c i) -> p c t i", i=4),
-                )
-            return woven
+        def weave(woven, src):
+            nc.vector.tensor_copy(
+                woven[:].rearrange("p (c i) t -> p c t i", i=4), src.rearrange("p t (c i) -> p c t i", i=4)
+            )
 
         def quantize(codes, scales, woven):
             nc.vector.quantize_mx(
                 out=codes[:].bitcast(FP8X4), scales=scales[:], in_=woven[:].rearrange("p w t -> p (w t)")
             )
 
-        ws_w = [keep.tile([P, N], U32, name=f"ws_w{b}", align_bytes=64) for b in range(HP)]
+        ws_woven = [keep.tile([P, N, PACK], BF16, name=f"ws_woven{b}", align_bytes=64) for b in range(HP)]
+        ws_w = [None] * HP
         ws_s = [keep.tile([P, N], U8, name=f"ws_s{b}", align_bytes=64) for b in range(HP)]
+        z_woven = [None] * len(pieces)
+        z_w = [None] * len(pieces)
+        z_s = [keep.tile([P, w], U8, name=f"z_s{i}", align_bytes=64) for i, (b, m0, w) in enumerate(pieces)]
 
-        def prepare_ws(b, *copies):
-            quantize(ws_w[b], ws_s[b], weave(copies, ws_raw[b][:], N))
+        def weave_ws(b):
+            weave(ws_woven[b], ws_raw[b][:])
 
-        def finish_z(i, copy):
-            b, m0, w = pieces[i]
-            quantize(z_w[i], z_s[i], weave([copy], z_rows[b][:, :, m0 : m0 + w], w))
+        def quantize_ws(b, s):
+            ws_w[b] = after_h(s, [P, N], U32, f"ws_w{b}")
+            quantize(ws_w[b], ws_s[b], ws_woven[b])
+
+        def weave_z(i, woven):
+            z_woven[i] = woven
+            weave(woven, z_rows[i][:])
+
+        def quantize_z(i, codes):
+            z_w[i] = codes
+            quantize(codes, z_s[i], z_woven[i])
 
         scores = {}
 
         def second_product(half, j, b):
             if b == 0:
-                scores[half, j] = psum.tile([P, HALF], F32, name="score", tag=f"bank{H_BANKS * (1 - half) + j}")
+                scores[half, j] = psum.tile([P, HALF], F32, name="score", tag=f"bank{N_TILES * half + j}")
             last = b == HP - 1
             i = b + half if last else b
             cols = slice(0, HALF) if last else slice(HALF * half, HALF * (half + 1))
@@ -272,7 +286,10 @@ def tile_list_rally_shot_scores_kernel(
 
         def store(half, j):
             cols = slice(HALF * half, HALF * (half + 1))
-            res = keep.tile([P, HALF], F32, name="res", tag="res", bufs=2 * N_TILES)
+            if half == 0:
+                res = after_h(SLICES - 1, [P, HALF], F32, f"res{j}", at=4 * HALF * j)
+            else:
+                res = keep.tile([P, HALF], F32, name="res", tag="res", bufs=N_TILES)
             nc.vector.scalar_tensor_tensor(
                 out=res[:],
                 in0=scores[half, j][:],
@@ -283,49 +300,69 @@ def tile_list_rally_shot_scores_kernel(
             )
             nc.sync.dma_start(out=out[P * j : P * (j + 1), cols], in_=res[:])
 
-        def order_last_wf():
-            order_wf(2)
-            load_ws(2, tenant(WF_SLOT, [P, PACK, N], F32, "ws_raw2"))
+        def order_later_wf():
+            for b in range(1, HP):
+                order_wf(b, wf_later[:, :, PASS // 2 * (b - 1) : PASS // 2 * b])
+            load_ws(2, placed(WF_RAW_AT, [P, PACK, N], F32, "ws_raw2"))
+
+        def products(half, passes):
+            for b in passes:
+                for j in range(N_TILES):
+                    second_product(half, j, b)
 
         beside = {
-            0: lambda: order_wf(1),
-            1: lambda: prepare_ws(0, nc.vector.tensor_copy),
-            2: order_last_wf,
-            4: lambda: finish_z(0, nc.vector.tensor_copy),
-            5: lambda: prepare_ws(1, nc.vector.tensor_copy),
-            7: lambda: prepare_ws(2, nc.vector.tensor_copy),
-            8: lambda: finish_z(1, nc.vector.tensor_copy),
+            0: [lambda: weave_ws(0)],
+            1: [lambda: weave_ws(1)],
+            2: [lambda: quantize_ws(0, 2), lambda: weave_ws(2)],
+            3: [lambda: quantize_ws(1, 3)],
+            4: [lambda: weave_z(0, after_h(4, [P, M, PACK], BF16, "z_woven0"))],
+            5: [lambda: quantize_z(0, after_h(5, [P, M], U32, "z_w0"))],
+            6: [lambda: quantize_ws(2, 6)],
+            8: [lambda: weave_z(1, placed(Z1_WOVEN_AT, [P, M, PACK], BF16, "z_woven1"))],
+            9: [lambda: quantize_z(1, keep.tile([P, M], U32, name="z_w1", align_bytes=64))],
+            12: [lambda: weave_z(2, after_h(8, [P, HALF, PACK], BF16, "z_woven2"))],
+            13: [lambda: quantize_z(2, after_h(9, [P, HALF], U32, "z_w2"))],
         }
 
-        first_product(0)
+        for s in range(PACK):
+            for c in range(2):
+                first_pass(s, c, 0, True, False)
+        for c in range(2):
+            for s in range(2):
+                first_pass(s, c, 1, False, True)
+                empty_bank(s, c, nc.vector.tensor_copy if (s, c) == (0, 1) else nc.scalar.copy)
+        order_later_wf()
         pick_follow(0)
+        pick_follow(1)
         pick_diff(0)
         turned = psum.tile([P, P], F32, name="turned", tag="bank1")
         nc.tensor.transpose(turned[:], rows[:], ident[:])
         nc.scalar.copy(per_part[:], turned[:, 0 : SLICES + N_TILES])
-        lev_sb = tenant(SMALL_SLOT, [P, M], F32, "lev_sb")
-        nc.sync.dma_start(out=lev_sb[:], in_=lev.partition_broadcast(P))
-        for s in range(SLICES):
-            more = s + 1 < SLICES
-            if more:
-                first_product(s + 1)
-            make_gate(s)
-            if more:
-                pick_follow(s + 1)
-                pick_diff(s + 1)
-            make_z(s)
-            if s in beside:
-                beside[s]()
+        for u in range(len(units)):
+            if u + 2 < SLICES:
+                first_product(u + 2)
+            ahead = u + 2 if u + 2 < VECTOR_FOLLOWS else u + 1
+            if VECTOR_FOLLOWS <= u + 1 < len(units) or 2 <= u + 2 < VECTOR_FOLLOWS:
+                pick_follow(ahead)
+            make_gate(u)
+            if VECTOR_FOLLOWS <= u + 1 < len(units) or u == 0:
+                pick_diff(u + 1)
+            make_z(u)
+            if 2 <= u + 2 < VECTOR_FOLLOWS:
+                pick_diff(u + 2)
+            for work in beside.get(u, []):
+                work()
 
-        for half in range(2):
-            for b in range(HP - 1):
-                for j in range(N_TILES):
-                    second_product(half, j, b)
-        finish_z(2, nc.vector.tensor_copy)
-        finish_z(3, nc.scalar.copy)
-        for half in range(2):
-            for j in range(N_TILES):
-                second_product(half, j, HP - 1)
-        for half in range(2):
-            for j in range(N_TILES):
-                store(half, j)
+        lev_sb = placed(TAB0_AT, [P, M], F32, "lev_sb")
+        nc.sync.dma_start(out=lev_sb[:], in_=lev.partition_broadcast(P))
+        products(0, range(HP))
+        products(1, range(HP - 1))
+        store(0, 0)
+        weave_z(3, keep.tile([P, HALF, PACK], BF16, name="z_woven3", align_bytes=64))
+        store(0, 1)
+        quantize_z(3, keep.tile([P, HALF], U32, name="z_w3", align_bytes=64))
+        products(1, [HP - 1])
+        store(0, 2)
+        store(0, 3)
+        for j in range(N_TILES):
+            store(1, j)

@@ -30,7 +30,8 @@ HP = H // PASS
 SLICES = H // P
 N_TILES = N // P
 HALF = M // 2
-VECTOR_FOLLOWS = 4
+VECTOR_FOLLOWS = 3
+LAST_SPLIT = 128
 BANKS = 8
 
 TAB1_AT = 0
@@ -38,7 +39,7 @@ WF_LATER_AT = 8192
 TAB0_AT = 16384
 WF_FIRST_AT = TAB0_AT + 8192
 ROWS_AT = TAB0_AT + 12288
-WF_RAW_AT = 32768
+WF_RAW_AT = TAB0_AT + 12800
 Z1_WOVEN_AT = 40960
 WF_BYTES = 2048
 H_BYTES = 4 * S
@@ -70,7 +71,7 @@ def tile_list_rally_shot_scores_kernel(
 
         tab_w = [None] * KP
         tab_s = keep.tile([P, T], U8, name="tab_s", align_bytes=64)
-        picked_s = keep.tile([P, S], U8, name="picked_s", align_bytes=64)
+        picked_s = placed(TAB1_AT, [P, S], U8, "picked_s")
         planes = [keep.tile([P, V_SCALES + WF_SCALES], I32, name=f"plane{a}", align_bytes=64) for a in range(KP)]
         v_w = [[keep.tile([P, BANK], U32, name=f"v_w{a}_{c}", align_bytes=64) for c in range(2)] for a in range(KP)]
         wf_s_raw = keep.tile([KP * BLOCKS, WF_SCALES], I32, name="wf_s_raw")
@@ -117,18 +118,15 @@ def tile_list_rally_shot_scores_kernel(
         nc.sync.dma_start(offs_sb[:], offs)
         nc.sync.dma_start(out=wf_s_raw[:], in_=wf_scales.rearrange("a q c -> (a q) c").bitcast(I32))
         nc.sync.dma_start(pos3_sb[:], pos3)
-        nc.sync.dma_start(pos2_sb[:], pos2)
-        nc.sync.dma_start(pos1_sb[:], pos1)
         load_words(0, TAB0_AT)
         wf_first = keep.tile([P, KP, PASS // 2], I32, name="wf_first")
         load_wf_words(wf_first, 0, 1)
+        nc.sync.dma_start(pos2_sb[:], pos2)
+        nc.sync.dma_start(pos1_sb[:], pos1)
         nc.vector.memset(warm[:, 0:1], 0.0)
         nc.scalar.activation(warm[:, 1:2], warm[:, 0:1], ACT.Sigmoid)
-        load_words(1, TAB1_AT)
-        wf_later = placed(WF_RAW_AT, [P, KP, PASS], I32, "wf_later")
-        load_wf_words(wf_later, 1, HP - 1)
 
-        nc.vector.memset(tab_s[64:128, :].bitcast(I32), 0)
+        nc.gpsimd.memset(tab_s[64:128, :].bitcast(I32), 0)
         nc.vector.memset(tab_s[32:64, :].bitcast(I32), 0)
         for a in range(KP):
             nc.gpsimd.memset(planes[a][:], 0)
@@ -140,14 +138,18 @@ def tile_list_rally_shot_scores_kernel(
             in_=wf_s_raw[:].rearrange("p (b q t e) -> p b t q e", b=HP, t=PACK, q=BLOCKS),
         )
         nc.vector.tensor_copy(planes[0][rows32, 0:V_SCALES], picked_s[rows32, :].bitcast(I32))
-        for a in range(KP):
-            for quad in range(0 if a else 1, QUADS):
-                move_scales(a, quad, nc.gpsimd if (a, quad) == (KP - 1, QUADS - 1) else nc.scalar)
+        for quad in range(1, QUADS):
+            move_scales(0, quad, nc.sync)
+        load_words(1, TAB1_AT)
+        for quad in range(QUADS):
+            move_scales(1, quad, nc.sync)
 
         gather_words(0, 0)
         gather_words(0, 1)
         order_wf(0, wf_first[:])
 
+        wf_later = placed(WF_RAW_AT, [P, KP, PASS], I32, "wf_later")
+        load_wf_words(wf_later, 1, HP - 1)
         load_ws(0, placed(TAB0_AT, [P, PACK, N], F32, "ws_raw0"))
         rows = placed(ROWS_AT, [P, P], F32, "rows")
         nc.gpsimd.memset(rows[:], 0.0)
@@ -179,14 +181,17 @@ def tile_list_rally_shot_scores_kernel(
                 stop=stop,
             )
 
+        def fill_bank(s, c):
+            if s >= PACK:
+                first_pass(s, c, 0, True, False)
+            first_pass(s, c, 1, False, True)
+
         def empty_bank(s, c, copy):
             copy(h[s][:, BANK * c : BANK * (c + 1)], acc[s, c][:])
 
         def first_product(s):
             for c in range(2):
-                if s >= PACK:
-                    first_pass(s, c, 0, True, False)
-                first_pass(s, c, 1, False, True)
+                fill_bank(s, c)
                 empty_bank(s, c, nc.scalar.copy)
 
         whole = SLICES - PACK
@@ -234,10 +239,8 @@ def tile_list_rally_shot_scores_kernel(
                 op1=ALU.mult,
             )
 
-        def weave(woven, src):
-            nc.vector.tensor_copy(
-                woven[:].rearrange("p (c i) t -> p c t i", i=4), src.rearrange("p t (c i) -> p c t i", i=4)
-            )
+        def weave(woven, src, copy=nc.vector.tensor_copy):
+            copy(woven.rearrange("p (c i) t -> p c t i", i=4), src.rearrange("p t (c i) -> p c t i", i=4))
 
         def quantize(codes, scales, woven):
             nc.vector.quantize_mx(
@@ -252,7 +255,7 @@ def tile_list_rally_shot_scores_kernel(
         z_s = [keep.tile([P, w], U8, name=f"z_s{i}", align_bytes=64) for i, (b, m0, w) in enumerate(pieces)]
 
         def weave_ws(b):
-            weave(ws_woven[b], ws_raw[b][:])
+            weave(ws_woven[b][:], ws_raw[b][:])
 
         def quantize_ws(b, s):
             ws_w[b] = after_h(s, [P, N], U32, f"ws_w{b}")
@@ -260,7 +263,7 @@ def tile_list_rally_shot_scores_kernel(
 
         def weave_z(i, woven):
             z_woven[i] = woven
-            weave(woven, z_rows[i][:])
+            weave(woven[:], z_rows[i][:])
 
         def quantize_z(i, codes):
             z_w[i] = codes
@@ -328,8 +331,8 @@ def tile_list_rally_shot_scores_kernel(
             for c in range(2):
                 first_pass(s, c, 0, True, False)
         for c in range(2):
-            for s in range(2):
-                first_pass(s, c, 1, False, True)
+            for s in range(3):
+                fill_bank(s, c)
                 empty_bank(s, c, nc.vector.tensor_copy if (s, c) == (0, 1) else nc.scalar.copy)
         order_later_wf()
         pick_follow(0)
@@ -339,7 +342,7 @@ def tile_list_rally_shot_scores_kernel(
         nc.tensor.transpose(turned[:], rows[:], ident[:])
         nc.scalar.copy(per_part[:], turned[:, 0 : SLICES + N_TILES])
         for u in range(len(units)):
-            if u + 2 < SLICES:
+            if 2 < u + 2 < SLICES:
                 first_product(u + 2)
             ahead = u + 2 if u + 2 < VECTOR_FOLLOWS else u + 1
             if VECTOR_FOLLOWS <= u + 1 < len(units) or 2 <= u + 2 < VECTOR_FOLLOWS:
@@ -358,7 +361,9 @@ def tile_list_rally_shot_scores_kernel(
         products(0, range(HP))
         products(1, range(HP - 1))
         store(0, 0)
-        weave_z(3, keep.tile([P, HALF, PACK], BF16, name="z_woven3", align_bytes=64))
+        z_woven[3] = keep.tile([P, HALF, PACK], BF16, name="z_woven3", align_bytes=64)
+        weave(z_woven[3][:, 0:LAST_SPLIT, :], z_rows[3][:, :, 0:LAST_SPLIT], nc.scalar.copy)
+        weave(z_woven[3][:, LAST_SPLIT:, :], z_rows[3][:, :, LAST_SPLIT:])
         store(0, 1)
         quantize_z(3, keep.tile([P, HALF], U32, name="z_w3", align_bytes=64))
         products(1, [HP - 1])

@@ -31,7 +31,7 @@ SLICES = H // P
 N_TILES = N // P
 HALF = M // 2
 VECTOR_FOLLOWS = 3
-LAST_SPLIT = 128
+QUARTER = M // 4
 BANKS = 8
 
 TAB1_AT = 0
@@ -41,6 +41,7 @@ WF_FIRST_AT = TAB0_AT + 8192
 ROWS_AT = TAB0_AT + 12288
 WF_RAW_AT = TAB0_AT + 12800
 Z1_WOVEN_AT = 40960
+Z3_WOVEN_AT = 45056
 WF_BYTES = 2048
 H_BYTES = 4 * S
 V_SCALES = S // 4
@@ -209,7 +210,14 @@ def tile_list_rally_shot_scores_kernel(
 
         def make_gate(u):
             gate[u] = keep.tile([P, units[u][2]], F32, name=f"gate{u}")
-            nc.scalar.activation(gate[u][:], picked(u, pos1_sb), ACT.Sigmoid)
+            if u < len(units) - 1:
+                nc.scalar.activation(gate[u][:], picked(u, pos1_sb), ACT.Sigmoid)
+                return
+            gate[u] = [keep.tile([P, QUARTER], F32, name=f"last_gate{k}") for k in range(2)]
+            for k in range(2):
+                m0 = HALF + QUARTER * k
+                entries = pos1_sb[:, m0 // GROUP : (m0 + QUARTER) // GROUP]
+                nc.scalar.activation(gate[u][k][:], h[SLICES - 1][:].indirect(entries), ACT.Sigmoid)
 
         def pick_follow(u):
             if u == whole + 1:
@@ -230,14 +238,18 @@ def tile_list_rally_shot_scores_kernel(
 
         def make_z(u):
             s = units[u][0]
-            nc.vector.scalar_tensor_tensor(
-                out=z_rows[u // PACK][:, u % PACK, :],
-                in0=diff[u][:],
-                scalar=per_part[:, s : s + 1],
-                in1=gate[u][:],
-                op0=ALU.mult,
-                op1=ALU.mult,
-            )
+            parts = [(slice(0, units[u][2]), gate[u])]
+            if u == len(units) - 1:
+                parts = [(slice(QUARTER * k, QUARTER * (k + 1)), gate[u][k]) for k in range(2)]
+            for cols, part in parts:
+                nc.vector.scalar_tensor_tensor(
+                    out=z_rows[u // PACK][:, u % PACK, cols],
+                    in0=diff[u][:, cols],
+                    scalar=per_part[:, s : s + 1],
+                    in1=part[:],
+                    op0=ALU.mult,
+                    op1=ALU.mult,
+                )
 
         def weave(woven, src, copy=nc.vector.tensor_copy):
             copy(woven.rearrange("p (c i) t -> p c t i", i=4), src.rearrange("p t (c i) -> p c t i", i=4))
@@ -303,6 +315,13 @@ def tile_list_rally_shot_scores_kernel(
             )
             nc.sync.dma_start(out=out[P * j : P * (j + 1), cols], in_=res[:])
 
+        def store_beside(j):
+            biased = keep.tile([P, HALF], F32, name=f"biased{j}")
+            nc.scalar.activation(biased[:], scores[0, j][:], ACT.Identity, bias=per_part[:, SLICES + j : SLICES + j + 1])
+            res = placed(Z3_WOVEN_AT + 4 * HALF * (j % 2), [P, HALF], F32, f"res_beside{j}")
+            nc.gpsimd.tensor_tensor(res[:], biased[:], lev_sb[:, 0:HALF], ALU.mult)
+            nc.scalar.dma_start(out=out[P * j : P * (j + 1), 0:HALF], in_=res[:])
+
         def order_later_wf():
             for b in range(1, HP):
                 order_wf(b, wf_later[:, :, PASS // 2 * (b - 1) : PASS // 2 * b])
@@ -333,7 +352,7 @@ def tile_list_rally_shot_scores_kernel(
         for c in range(2):
             for s in range(3):
                 fill_bank(s, c)
-                empty_bank(s, c, nc.vector.tensor_copy if (s, c) == (0, 1) else nc.scalar.copy)
+                empty_bank(s, c, nc.vector.tensor_copy if c == 1 and s < 2 else nc.scalar.copy)
         order_later_wf()
         pick_follow(0)
         pick_follow(1)
@@ -359,15 +378,55 @@ def tile_list_rally_shot_scores_kernel(
         lev_sb = placed(TAB0_AT, [P, M], F32, "lev_sb")
         nc.sync.dma_start(out=lev_sb[:], in_=lev.partition_broadcast(P))
         products(0, range(HP))
-        products(1, range(HP - 1))
+        ends = [psum.tile([P, N_TILES, QUARTER], F32, name=f"end{k}", tag=f"bank{N_TILES + k}") for k in range(2)]
+        end_w = [keep.tile([P, QUARTER], U32, name=f"end_w{k}", align_bytes=64) for k in range(2)]
+        end_s = [keep.tile([P, QUARTER], U8, name=f"end_s{k}", align_bytes=64) for k in range(2)]
+        end_woven = [placed(Z3_WOVEN_AT + (512 if k else 2048), [P, QUARTER, PACK], BF16, f"end_woven{k}") for k in range(2)]
+        end_res = [keep.tile([P, 2, QUARTER], F32, name=f"end_res{k}") for k in range(4)]
+
+        def end_products(k, b):
+            cols = slice(HALF + QUARTER * k, HALF + QUARTER * (k + 1))
+            last = b == HP - 1
+            for j in range(N_TILES):
+                nc.tensor.matmul_mx(
+                    out=ends[k][:, j, :],
+                    lhsT=ws_w[b][:, P * j : P * (j + 1)].bitcast(FP8X4),
+                    lhsT_scale=ws_s[b][:, P * j : P * (j + 1)],
+                    rhs=(end_w[k][:] if last else z_w[b][:, cols]).bitcast(FP8X4),
+                    rhs_scale=end_s[k][:] if last else z_s[b][:, cols],
+                    start=(b == 0 and j == 0),
+                    stop=(last and j == N_TILES - 1),
+                )
+
+        def end_store(k):
+            cols = slice(HALF + QUARTER * k, HALF + QUARTER * (k + 1))
+            for pair in range(2):
+                res = end_res[2 * k + pair]
+                for i in range(2):
+                    j = 2 * pair + i
+                    nc.vector.scalar_tensor_tensor(
+                        out=res[:, i, :],
+                        in0=ends[k][:, j, :],
+                        scalar=per_part[:, SLICES + j : SLICES + j + 1],
+                        in1=lev_sb[:, cols],
+                        op0=ALU.add,
+                        op1=ALU.mult,
+                    )
+                rows_out = out[2 * P * pair : 2 * P * (pair + 1), cols]
+                nc.sync.dma_start(out=rows_out.rearrange("(i p) m -> p i m", p=P), in_=res[:])
+
+        for k in range(2):
+            for b in range(HP - 1):
+                end_products(k, b)
         store(0, 0)
-        z_woven[3] = keep.tile([P, HALF, PACK], BF16, name="z_woven3", align_bytes=64)
-        weave(z_woven[3][:, 0:LAST_SPLIT, :], z_rows[3][:, :, 0:LAST_SPLIT], nc.scalar.copy)
-        weave(z_woven[3][:, LAST_SPLIT:, :], z_rows[3][:, :, LAST_SPLIT:])
+        weave(end_woven[0][:], z_rows[3][:, :, 0:QUARTER])
+        weave(end_woven[1][:], z_rows[3][:, :, QUARTER:], nc.scalar.copy)
+        quantize(end_w[0], end_s[0], end_woven[0])
+        end_products(0, HP - 1)
         store(0, 1)
-        quantize_z(3, keep.tile([P, HALF], U32, name="z_w3", align_bytes=64))
-        products(1, [HP - 1])
-        store(0, 2)
-        store(0, 3)
-        for j in range(N_TILES):
-            store(1, j)
+        quantize(end_w[1], end_s[1], end_woven[1])
+        end_products(1, HP - 1)
+        store_beside(2)
+        store_beside(3)
+        end_store(0)
+        end_store(1)

@@ -109,7 +109,7 @@ def tile_list_rally_shot_scores_kernel(
         def order_wf(b, raw):
             offset = WF_LATER_AT + WF_BYTES * (b - 1) if b else WF_FIRST_AT
             wf_w[b] = placed(offset, [P, KP, PASS // 2], I32, f"wf_w{b}")
-            nc.vector.tensor_copy(
+            (nc.gpsimd if b else nc.vector).tensor_copy(
                 out=wf_w[b][:].rearrange("p a (t q e) -> p a t q e", t=PACK, q=BLOCKS),
                 in_=raw.rearrange("p a (q t e) -> p a t q e", t=PACK, q=BLOCKS),
             )
@@ -352,7 +352,7 @@ def tile_list_rally_shot_scores_kernel(
         for c in range(2):
             for s in range(3):
                 fill_bank(s, c)
-                empty_bank(s, c, nc.vector.tensor_copy if c == 1 and s < 2 else nc.scalar.copy)
+                empty_bank(s, c, nc.vector.tensor_copy if (s, c) in ((2, 0), (0, 1)) else nc.scalar.copy)
         order_later_wf()
         pick_follow(0)
         pick_follow(1)

@@ -378,7 +378,7 @@ def tile_list_rally_shot_scores_kernel(
         lev_sb = placed(TAB0_AT, [P, M], F32, "lev_sb")
         nc.sync.dma_start(out=lev_sb[:], in_=lev.partition_broadcast(P))
         products(0, range(HP))
-        ends = [psum.tile([P, N_TILES, QUARTER], F32, name=f"end{k}", tag=f"bank{N_TILES + k}") for k in range(2)]
+        ends = [psum.tile([P, 2, QUARTER], F32, name=f"end{k}", tag=f"bank{N_TILES + k}") for k in range(4)]
         end_w = [keep.tile([P, QUARTER], U32, name=f"end_w{k}", align_bytes=64) for k in range(2)]
         end_s = [keep.tile([P, QUARTER], U8, name=f"end_s{k}", align_bytes=64) for k in range(2)]
         end_woven = [placed(Z3_WOVEN_AT + (512 if k else 2048), [P, QUARTER, PACK], BF16, f"end_woven{k}") for k in range(2)]
@@ -389,13 +389,13 @@ def tile_list_rally_shot_scores_kernel(
             last = b == HP - 1
             for j in range(N_TILES):
                 nc.tensor.matmul_mx(
-                    out=ends[k][:, j, :],
+                    out=ends[2 * k + j // 2][:, j % 2, :],
                     lhsT=ws_w[b][:, P * j : P * (j + 1)].bitcast(FP8X4),
                     lhsT_scale=ws_s[b][:, P * j : P * (j + 1)],
                     rhs=(end_w[k][:] if last else z_w[b][:, cols]).bitcast(FP8X4),
                     rhs_scale=end_s[k][:] if last else z_s[b][:, cols],
-                    start=(b == 0 and j == 0),
-                    stop=(last and j == N_TILES - 1),
+                    start=(b == 0 and j % 2 == 0),
+                    stop=(last and j % 2 == 1),
                 )
 
         def end_store(k):
@@ -406,14 +406,17 @@ def tile_list_rally_shot_scores_kernel(
                     j = 2 * pair + i
                     nc.vector.scalar_tensor_tensor(
                         out=res[:, i, :],
-                        in0=ends[k][:, j, :],
+                        in0=ends[2 * k + pair][:, i, :],
                         scalar=per_part[:, SLICES + j : SLICES + j + 1],
                         in1=lev_sb[:, cols],
                         op0=ALU.add,
                         op1=ALU.mult,
                     )
-                rows_out = out[2 * P * pair : 2 * P * (pair + 1), cols]
-                nc.sync.dma_start(out=rows_out.rearrange("(i p) m -> p i m", p=P), in_=res[:])
+                    if k == 1 and pair == 1:
+                        nc.sync.dma_start(out=out[P * j : P * (j + 1), cols], in_=res[:, i, :])
+                if k == 0 or pair == 0:
+                    rows_out = out[2 * P * pair : 2 * P * (pair + 1), cols]
+                    nc.sync.dma_start(out=rows_out.rearrange("(i p) m -> p i m", p=P), in_=res[:])
 
         for k in range(2):
             for b in range(HP - 1):

@@ -42,6 +42,7 @@ ROWS_AT = TAB0_AT + 12288
 WF_RAW_AT = TAB0_AT + 12800
 Z1_WOVEN_AT = 40960
 Z3_WOVEN_AT = 45056
+END_AT = 49152
 WF_BYTES = 2048
 H_BYTES = 4 * S
 V_SCALES = S // 4
@@ -199,29 +200,32 @@ def tile_list_rally_shot_scores_kernel(
         units = [(s, 0, M) for s in range(whole)]
         units = units + [(s, m0, HALF) for m0 in (0, HALF) for s in range(whole, SLICES)]
         pieces = [(0, 0, M), (1, 0, M), (2, 0, HALF), (2, HALF, HALF)]
-        z_rows = [keep.tile([P, PACK, w], BF16, name=f"z_rows{i}") for i, (b, m0, w) in enumerate(pieces)]
-        gate = [None] * len(units)
+        gates = [keep.tile([P, PACK, w], F32, name=f"gates{i}") for i, (b, m0, w) in enumerate(pieces[:-1])]
+        end_gates = [keep.tile([P, PACK, QUARTER], F32, name=f"end_gates{k}") for k in range(2)]
+        diffs = [keep.tile([P, PACK, w], F32, name=f"diffs{i}") for i, (b, m0, w) in enumerate(pieces)]
         follow = [None] * len(units)
-        diff = [None] * len(units)
+        first_end = len(units) - PACK
 
         def picked(u, pos_sb):
             s, m0, w = units[u]
             return h[s][:].indirect(pos_sb[:, m0 // GROUP : (m0 + w) // GROUP])
 
         def make_gate(u):
-            gate[u] = keep.tile([P, units[u][2]], F32, name=f"gate{u}")
-            if u < len(units) - 1:
-                nc.scalar.activation(gate[u][:], picked(u, pos1_sb), ACT.Sigmoid)
-                return
-            gate[u] = [keep.tile([P, QUARTER], F32, name=f"last_gate{k}") for k in range(2)]
-            for k in range(2):
-                m0 = HALF + QUARTER * k
-                entries = pos1_sb[:, m0 // GROUP : (m0 + QUARTER) // GROUP]
-                nc.scalar.activation(gate[u][k][:], h[SLICES - 1][:].indirect(entries), ACT.Sigmoid)
+            if u < first_end:
+                nc.scalar.activation(gates[u // PACK][:, u % PACK, :], picked(u, pos1_sb), ACT.Sigmoid)
+            else:
+                make_end_gate(u, 0)
+
+        def make_end_gate(u, k):
+            m0 = HALF + QUARTER * k
+            entries = pos1_sb[:, m0 // GROUP : (m0 + QUARTER) // GROUP]
+            nc.scalar.activation(end_gates[k][:, u % PACK, :], h[units[u][0]][:].indirect(entries), ACT.Sigmoid)
 
         def pick_follow(u):
             if u == whole + 1:
                 follow[u] = placed(Z1_WOVEN_AT, [P, units[u][2]], F32, f"follow{u}")
+            elif u >= first_end:
+                follow[u] = placed(END_AT + 2048 * (u - first_end), [P, units[u][2]], F32, f"follow{u}")
             else:
                 follow[u] = keep.tile([P, units[u][2]], F32, name=f"follow{u}")
             if u < VECTOR_FOLLOWS:
@@ -230,26 +234,20 @@ def tile_list_rally_shot_scores_kernel(
                 nc.scalar.activation(follow[u][:], picked(u, pos3_sb), ACT.Copy)
 
         def pick_diff(u):
-            if 2 <= u < VECTOR_FOLLOWS:
-                diff[u] = after_h(u - 2, [P, M], F32, f"diff{u}")
-            else:
-                diff[u] = keep.tile([P, units[u][2]], F32, name="diff", tag="diff", bufs=4)
-            nc.vector.tensor_tensor(diff[u][:], picked(u, pos2_sb), follow[u][:], ALU.subtract)
+            nc.vector.tensor_tensor(diffs[u // PACK][:, u % PACK, :], picked(u, pos2_sb), follow[u][:], ALU.subtract)
 
-        def make_z(u):
+        def apply_gain(u):
             s = units[u][0]
-            parts = [(slice(0, units[u][2]), gate[u])]
-            if u == len(units) - 1:
-                parts = [(slice(QUARTER * k, QUARTER * (k + 1)), gate[u][k]) for k in range(2)]
-            for cols, part in parts:
-                nc.vector.scalar_tensor_tensor(
-                    out=z_rows[u // PACK][:, u % PACK, cols],
-                    in0=diff[u][:, cols],
-                    scalar=per_part[:, s : s + 1],
-                    in1=part[:],
-                    op0=ALU.mult,
-                    op1=ALU.mult,
-                )
+            rows_u = (gates if u < first_end else diffs)[u // PACK][:, u % PACK, :]
+            nc.vector.tensor_scalar(rows_u, rows_u, per_part[:, s : s + 1], None, ALU.mult)
+
+        def make_z(woven, gate4, diff4):
+            nc.vector.tensor_tensor(
+                woven.rearrange("p (c i) t -> p c t i", i=2),
+                diff4.rearrange("p t (c i) -> p c t i", i=2),
+                gate4.rearrange("p t (c i) -> p c t i", i=2),
+                ALU.mult,
+            )
 
         def weave(woven, src, copy=nc.vector.tensor_copy):
             copy(woven.rearrange("p (c i) t -> p c t i", i=4), src.rearrange("p t (c i) -> p c t i", i=4))
@@ -275,7 +273,7 @@ def tile_list_rally_shot_scores_kernel(
 
         def weave_z(i, woven):
             z_woven[i] = woven
-            weave(woven[:], z_rows[i][:])
+            make_z(woven[:], gates[i][:], diffs[i][:])
 
         def quantize_z(i, codes):
             z_w[i] = codes
@@ -302,7 +300,7 @@ def tile_list_rally_shot_scores_kernel(
         def store(half, j):
             cols = slice(HALF * half, HALF * (half + 1))
             if half == 0:
-                res = after_h(SLICES - 1, [P, HALF], F32, f"res{j}", at=4 * HALF * j)
+                res = placed(END_AT + 3 * 2048 - 2 * HALF + 4 * HALF * j, [P, HALF], F32, f"res{j}")
             else:
                 res = keep.tile([P, HALF], F32, name="res", tag="res", bufs=N_TILES)
             nc.vector.scalar_tensor_tensor(
@@ -342,8 +340,8 @@ def tile_list_rally_shot_scores_kernel(
             6: [lambda: quantize_ws(2, 6)],
             8: [lambda: weave_z(1, placed(Z1_WOVEN_AT, [P, M, PACK], BF16, "z_woven1"))],
             9: [lambda: quantize_z(1, keep.tile([P, M], U32, name="z_w1", align_bytes=64))],
-            12: [lambda: weave_z(2, after_h(8, [P, HALF, PACK], BF16, "z_woven2"))],
-            13: [lambda: quantize_z(2, after_h(9, [P, HALF], U32, "z_w2"))],
+            12: [lambda: weave_z(2, placed(END_AT, [P, HALF, PACK], BF16, "z_woven2"))],
+            13: [lambda: quantize_z(2, placed(END_AT + 2048, [P, HALF], U32, "z_w2"))],
         }
 
         for s in range(PACK):
@@ -369,11 +367,14 @@ def tile_list_rally_shot_scores_kernel(
             make_gate(u)
             if VECTOR_FOLLOWS <= u + 1 < len(units) or u == 0:
                 pick_diff(u + 1)
-            make_z(u)
+            apply_gain(u)
             if 2 <= u + 2 < VECTOR_FOLLOWS:
                 pick_diff(u + 2)
             for work in beside.get(u, []):
                 work()
+
+        for u in range(first_end, len(units)):
+            make_end_gate(u, 1)
 
         lev_sb = placed(TAB0_AT, [P, M], F32, "lev_sb")
         nc.sync.dma_start(out=lev_sb[:], in_=lev.partition_broadcast(P))
@@ -421,11 +422,11 @@ def tile_list_rally_shot_scores_kernel(
         for k in range(2):
             for b in range(HP - 1):
                 end_products(k, b)
+        make_z(end_woven[0][:], end_gates[0][:], diffs[3][:, :, 0:QUARTER])
         store(0, 0)
-        weave(end_woven[0][:], z_rows[3][:, :, 0:QUARTER])
-        weave(end_woven[1][:], z_rows[3][:, :, QUARTER:], nc.scalar.copy)
         quantize(end_w[0], end_s[0], end_woven[0])
         end_products(0, HP - 1)
+        make_z(end_woven[1][:], end_gates[1][:], diffs[3][:, :, QUARTER:])
         store(0, 1)
         quantize(end_w[1], end_s[1], end_woven[1])
         end_products(1, HP - 1)

@@ -197,49 +197,31 @@ def tile_list_rally_shot_scores_kernel(
                 empty_bank(s, c, nc.scalar.copy)
 
         whole = SLICES - PACK
-        units = [(s, 0, M) for s in range(whole)]
-        units = units + [(s, m0, HALF) for m0 in (0, HALF) for s in range(whole, SLICES)]
-        pieces = [(0, 0, M), (1, 0, M), (2, 0, HALF), (2, HALF, HALF)]
+        pieces = [(0, 0, M), (1, 0, M), (2, 0, HALF), (2, HALF, QUARTER), (2, HALF + QUARTER, QUARTER)]
         gates = [keep.tile([P, PACK, w], F32, name=f"gates{i}") for i, (b, m0, w) in enumerate(pieces[:-1])]
-        end_gates = [keep.tile([P, PACK, QUARTER], F32, name=f"end_gates{k}") for k in range(2)]
-        diffs = [keep.tile([P, PACK, w], F32, name=f"diffs{i}") for i, (b, m0, w) in enumerate(pieces)]
-        follow = [None] * len(units)
-        first_end = len(units) - PACK
+        gates = gates + [placed(END_AT, [P, PACK, QUARTER], F32, "gates4")]
+        diffs = [keep.tile([P, PACK, M], F32, name=f"diffs{b}") for b in range(HP)]
+        follow = [None] * SLICES
 
-        def picked(u, pos_sb):
-            s, m0, w = units[u]
-            return h[s][:].indirect(pos_sb[:, m0 // GROUP : (m0 + w) // GROUP])
+        def make_gate(i, t):
+            b, m0, w = pieces[i]
+            entries = pos1_sb[:, m0 // GROUP : (m0 + w) // GROUP]
+            nc.scalar.activation(gates[i][:, t, :], h[PACK * b + t][:].indirect(entries), ACT.Sigmoid)
 
-        def make_gate(u):
-            if u < first_end:
-                nc.scalar.activation(gates[u // PACK][:, u % PACK, :], picked(u, pos1_sb), ACT.Sigmoid)
+        def pick_follow(s):
+            follow[s] = keep.tile([P, M], F32, name=f"follow{s}")
+            if s < VECTOR_FOLLOWS:
+                nc.vector.tensor_copy(follow[s][:], h[s][:].indirect(pos3_sb[:]))
             else:
-                make_end_gate(u, 0)
+                nc.scalar.activation(follow[s][:], h[s][:].indirect(pos3_sb[:]), ACT.Copy)
 
-        def make_end_gate(u, k):
-            m0 = HALF + QUARTER * k
-            entries = pos1_sb[:, m0 // GROUP : (m0 + QUARTER) // GROUP]
-            nc.scalar.activation(end_gates[k][:, u % PACK, :], h[units[u][0]][:].indirect(entries), ACT.Sigmoid)
+        def pick_diff(s):
+            nc.vector.tensor_tensor(diffs[s // PACK][:, s % PACK, :], h[s][:].indirect(pos2_sb[:]), follow[s][:], ALU.subtract)
 
-        def pick_follow(u):
-            if u == whole + 1:
-                follow[u] = placed(Z1_WOVEN_AT, [P, units[u][2]], F32, f"follow{u}")
-            elif u >= first_end:
-                follow[u] = placed(END_AT + 2048 * (u - first_end), [P, units[u][2]], F32, f"follow{u}")
-            else:
-                follow[u] = keep.tile([P, units[u][2]], F32, name=f"follow{u}")
-            if u < VECTOR_FOLLOWS:
-                nc.vector.tensor_copy(follow[u][:], picked(u, pos3_sb))
-            else:
-                nc.scalar.activation(follow[u][:], picked(u, pos3_sb), ACT.Copy)
-
-        def pick_diff(u):
-            nc.vector.tensor_tensor(diffs[u // PACK][:, u % PACK, :], picked(u, pos2_sb), follow[u][:], ALU.subtract)
-
-        def apply_gain(u):
-            s = units[u][0]
-            rows_u = (gates if u < first_end else diffs)[u // PACK][:, u % PACK, :]
-            nc.vector.tensor_scalar(rows_u, rows_u, per_part[:, s : s + 1], None, ALU.mult)
+        def apply_gain(s):
+            b, t = divmod(s, PACK)
+            row = (gates if s < whole else diffs)[b][:, t, :]
+            nc.vector.tensor_scalar(row, row, per_part[:, s : s + 1], None, ALU.mult)
 
         def make_z(woven, gate4, diff4):
             nc.vector.tensor_tensor(
@@ -257,7 +239,8 @@ def tile_list_rally_shot_scores_kernel(
                 out=codes[:].bitcast(FP8X4), scales=scales[:], in_=woven[:].rearrange("p w t -> p (w t)")
             )
 
-        ws_woven = [keep.tile([P, N, PACK], BF16, name=f"ws_woven{b}", align_bytes=64) for b in range(HP)]
+        ws_woven = [keep.tile([P, N, PACK], BF16, name=f"ws_woven{b}", align_bytes=64) for b in range(HP - 1)]
+        ws_woven = ws_woven + [after_h(whole + 2, [P, N, PACK], BF16, "ws_woven2")]
         ws_w = [None] * HP
         ws_s = [keep.tile([P, N], U8, name=f"ws_s{b}", align_bytes=64) for b in range(HP)]
         z_woven = [None] * len(pieces)
@@ -273,7 +256,8 @@ def tile_list_rally_shot_scores_kernel(
 
         def weave_z(i, woven):
             z_woven[i] = woven
-            make_z(woven[:], gates[i][:], diffs[i][:])
+            b, m0, w = pieces[i]
+            make_z(woven[:], gates[i][:], diffs[b][:, :, m0 : m0 + w])
 
         def quantize_z(i, codes):
             z_w[i] = codes
@@ -299,10 +283,7 @@ def tile_list_rally_shot_scores_kernel(
 
         def store(half, j):
             cols = slice(HALF * half, HALF * (half + 1))
-            if half == 0:
-                res = placed(END_AT + 3 * 2048 - 2 * HALF + 4 * HALF * j, [P, HALF], F32, f"res{j}")
-            else:
-                res = keep.tile([P, HALF], F32, name="res", tag="res", bufs=N_TILES)
+            res = keep.tile([P, HALF], F32, name=f"res{j}")
             nc.vector.scalar_tensor_tensor(
                 out=res[:],
                 in0=scores[half, j][:],
@@ -313,10 +294,10 @@ def tile_list_rally_shot_scores_kernel(
             )
             nc.sync.dma_start(out=out[P * j : P * (j + 1), cols], in_=res[:])
 
-        def store_beside(j):
+        def store_beside(j, offset):
             biased = keep.tile([P, HALF], F32, name=f"biased{j}")
             nc.scalar.activation(biased[:], scores[0, j][:], ACT.Identity, bias=per_part[:, SLICES + j : SLICES + j + 1])
-            res = placed(Z3_WOVEN_AT + 4 * HALF * (j % 2), [P, HALF], F32, f"res_beside{j}")
+            res = placed(offset, [P, HALF], F32, f"res_beside{j}")
             nc.gpsimd.tensor_tensor(res[:], biased[:], lev_sb[:, 0:HALF], ALU.mult)
             nc.scalar.dma_start(out=out[P * j : P * (j + 1), 0:HALF], in_=res[:])
 
@@ -338,10 +319,6 @@ def tile_list_rally_shot_scores_kernel(
             4: [lambda: weave_z(0, after_h(4, [P, M, PACK], BF16, "z_woven0"))],
             5: [lambda: quantize_z(0, after_h(5, [P, M], U32, "z_w0"))],
             6: [lambda: quantize_ws(2, 6)],
-            8: [lambda: weave_z(1, placed(Z1_WOVEN_AT, [P, M, PACK], BF16, "z_woven1"))],
-            9: [lambda: quantize_z(1, keep.tile([P, M], U32, name="z_w1", align_bytes=64))],
-            12: [lambda: weave_z(2, placed(END_AT, [P, HALF, PACK], BF16, "z_woven2"))],
-            13: [lambda: quantize_z(2, placed(END_AT + 2048, [P, HALF], U32, "z_w2"))],
         }
 
         for s in range(PACK):
@@ -358,31 +335,51 @@ def tile_list_rally_shot_scores_kernel(
         turned = psum.tile([P, P], F32, name="turned", tag="bank1")
         nc.tensor.transpose(turned[:], rows[:], ident[:])
         nc.scalar.copy(per_part[:], turned[:, 0 : SLICES + N_TILES])
-        for u in range(len(units)):
-            if 2 < u + 2 < SLICES:
+        for u in range(whole - 1):
+            if u > 0:
                 first_product(u + 2)
-            ahead = u + 2 if u + 2 < VECTOR_FOLLOWS else u + 1
-            if VECTOR_FOLLOWS <= u + 1 < len(units) or 2 <= u + 2 < VECTOR_FOLLOWS:
-                pick_follow(ahead)
-            make_gate(u)
-            if VECTOR_FOLLOWS <= u + 1 < len(units) or u == 0:
+            if u == 0:
+                pick_follow(2)
+            elif u > 1:
+                pick_follow(u + 1)
+            make_gate(*divmod(u, PACK))
+            if u != 1:
                 pick_diff(u + 1)
             apply_gain(u)
-            if 2 <= u + 2 < VECTOR_FOLLOWS:
-                pick_diff(u + 2)
+            if u == 0:
+                pick_diff(2)
             for work in beside.get(u, []):
                 work()
-
-        for u in range(first_end, len(units)):
-            make_end_gate(u, 1)
+        make_gate(1, PACK - 1)
+        apply_gain(whole - 1)
+        first_product(whole + 1)
+        pick_follow(whole)
+        for c in range(2):
+            fill_bank(whole + 2, c)
+            empty_bank(whole + 2, c, nc.vector.tensor_copy if c else nc.scalar.copy)
+        weave_z(1, keep.tile([P, M, PACK], BF16, name="z_woven1", align_bytes=64))
+        pick_diff(whole)
+        quantize_z(1, keep.tile([P, M], U32, name="z_w1", align_bytes=64))
+        pick_follow(whole + 1)
+        first_product(whole + 3)
+        pick_follow(whole + 2)
+        pick_follow(whole + 3)
+        for s in range(whole + 1, SLICES):
+            pick_diff(s)
+            apply_gain(s - 1)
+        apply_gain(SLICES - 1)
+        for i in range(HP - 1, len(pieces)):
+            for t in range(PACK):
+                make_gate(i, t)
+        weave_z(2, keep.tile([P, HALF, PACK], BF16, name="z_woven2", align_bytes=64))
+        weave_z(3, placed(Z3_WOVEN_AT + 2048, [P, QUARTER, PACK], BF16, "z_woven3"))
+        quantize_z(2, keep.tile([P, HALF], U32, name="z_w2", align_bytes=64))
+        quantize_z(3, keep.tile([P, QUARTER], U32, name="z_w3", align_bytes=64))
 
         lev_sb = placed(TAB0_AT, [P, M], F32, "lev_sb")
         nc.sync.dma_start(out=lev_sb[:], in_=lev.partition_broadcast(P))
         products(0, range(HP))
         ends = [psum.tile([P, 2, QUARTER], F32, name=f"end{k}", tag=f"bank{N_TILES + k}") for k in range(4)]
-        end_w = [keep.tile([P, QUARTER], U32, name=f"end_w{k}", align_bytes=64) for k in range(2)]
-        end_s = [keep.tile([P, QUARTER], U8, name=f"end_s{k}", align_bytes=64) for k in range(2)]
-        end_woven = [placed(Z3_WOVEN_AT + (512 if k else 2048), [P, QUARTER, PACK], BF16, f"end_woven{k}") for k in range(2)]
         end_res = [keep.tile([P, 2, QUARTER], F32, name=f"end_res{k}") for k in range(4)]
 
         def end_products(k, b):
@@ -393,8 +390,8 @@ def tile_list_rally_shot_scores_kernel(
                     out=ends[2 * k + j // 2][:, j % 2, :],
                     lhsT=ws_w[b][:, P * j : P * (j + 1)].bitcast(FP8X4),
                     lhsT_scale=ws_s[b][:, P * j : P * (j + 1)],
-                    rhs=(end_w[k][:] if last else z_w[b][:, cols]).bitcast(FP8X4),
-                    rhs_scale=end_s[k][:] if last else z_s[b][:, cols],
+                    rhs=(z_w[HP + k][:] if last else z_w[b][:, cols]).bitcast(FP8X4),
+                    rhs_scale=z_s[HP + k][:] if last else z_s[b][:, cols],
                     start=(b == 0 and j % 2 == 0),
                     stop=(last and j % 2 == 1),
                 )
@@ -422,15 +419,13 @@ def tile_list_rally_shot_scores_kernel(
         for k in range(2):
             for b in range(HP - 1):
                 end_products(k, b)
-        make_z(end_woven[0][:], end_gates[0][:], diffs[3][:, :, 0:QUARTER])
-        store(0, 0)
-        quantize(end_w[0], end_s[0], end_woven[0])
         end_products(0, HP - 1)
-        make_z(end_woven[1][:], end_gates[1][:], diffs[3][:, :, QUARTER:])
+        weave_z(4, placed(Z3_WOVEN_AT + 512, [P, QUARTER, PACK], BF16, "z_woven4"))
+        store_beside(0, END_AT)
         store(0, 1)
-        quantize(end_w[1], end_s[1], end_woven[1])
+        store(0, 2)
+        quantize_z(4, keep.tile([P, QUARTER], U32, name="z_w4", align_bytes=64))
         end_products(1, HP - 1)
-        store_beside(2)
-        store_beside(3)
+        store_beside(3, Z3_WOVEN_AT)
         end_store(0)
         end_store(1)

@@ -30,7 +30,7 @@ HP = H // PASS
 SLICES = H // P
 N_TILES = N // P
 HALF = M // 2
-VECTOR_FOLLOWS = 3
+VECTOR_FOLLOWS = 2
 QUARTER = M // 4
 BANKS = 8
 
@@ -38,7 +38,6 @@ TAB1_AT = 0
 WF_LATER_AT = 8192
 TAB0_AT = 16384
 WF_FIRST_AT = TAB0_AT + 8192
-ROWS_AT = TAB0_AT + 12288
 WF_RAW_AT = TAB0_AT + 12800
 Z1_WOVEN_AT = 40960
 Z3_WOVEN_AT = 45056
@@ -79,7 +78,7 @@ def tile_list_rally_shot_scores_kernel(
         wf_s_raw = keep.tile([KP * BLOCKS, WF_SCALES], I32, name="wf_s_raw")
         wf_w = [None] * HP
         ident = keep.tile([P, P], F32, name="ident")
-        per_part = keep.tile([P, SLICES + N_TILES], F32, name="per_part")
+        per_part = keep.tile([P, PACK, 2, HP], F32, name="per_part")
         ws_raw = [None] * HP
         warm = keep.tile([P, 2], F32, name="warm")
 
@@ -123,8 +122,9 @@ def tile_list_rally_shot_scores_kernel(
         load_words(0, TAB0_AT)
         wf_first = keep.tile([P, KP, PASS // 2], I32, name="wf_first")
         load_wf_words(wf_first, 0, 1)
-        nc.sync.dma_start(pos2_sb[:], pos2)
-        nc.sync.dma_start(pos1_sb[:], pos1)
+        raw_rows = keep.tile([P, PASS], F32, name="raw_rows")
+        nc.sync.dma_start(out=raw_rows[0:HP, :], in_=gain.rearrange("(b r) -> b r", b=HP))
+        nc.sync.dma_start(out=raw_rows[32:33, :], in_=bo.rearrange("(o n) -> o n", o=1))
         nc.vector.memset(warm[:, 0:1], 0.0)
         nc.scalar.activation(warm[:, 1:2], warm[:, 0:1], ACT.Sigmoid)
 
@@ -133,6 +133,17 @@ def tile_list_rally_shot_scores_kernel(
         for a in range(KP):
             nc.gpsimd.memset(planes[a][:], 0)
         make_identity(nc, ident[:])
+        rows = keep.tile([P, PACK, P], F32, name="rows")
+        nc.gpsimd.memset(rows[:], 0.0)
+        nc.gpsimd.tensor_copy(
+            rows[0:HP].rearrange("b t (q e) -> b t q e", e=RUN),
+            raw_rows[0:HP, :].rearrange("b (q t e) -> b t q e", t=PACK, e=RUN),
+        )
+        nc.gpsimd.tensor_copy(rows[32:33].rearrange("o j p -> o (j p)"), raw_rows[32:33, :])
+        turned = psum.tile([P, PACK, P], F32, name="turned", tag=f"bank{BANKS - 1}")
+        for t in range(PACK):
+            nc.tensor.transpose(turned[:, t, :], rows[:, t, :], ident[:])
+        nc.scalar.copy(per_part[:], turned[:].rearrange("p t (g x) -> p t g x", x=32)[:, :, 0:2, 0:HP])
 
         nc.vector.tensor_copy(picked_s[:], tab_s[:].indirect(offs_sb[:]))
         nc.vector.tensor_copy(
@@ -150,18 +161,11 @@ def tile_list_rally_shot_scores_kernel(
         gather_words(0, 1)
         order_wf(0, wf_first[:])
 
+        nc.sync.dma_start(pos1_sb[:], pos1)
+        nc.sync.dma_start(pos2_sb[:], pos2)
         wf_later = placed(WF_RAW_AT, [P, KP, PASS], I32, "wf_later")
         load_wf_words(wf_later, 1, HP - 1)
         load_ws(0, placed(TAB0_AT, [P, PACK, N], F32, "ws_raw0"))
-        rows = placed(ROWS_AT, [P, P], F32, "rows")
-        nc.gpsimd.memset(rows[:], 0.0)
-        for b in range(HP):
-            nc.sync.dma_start(
-                out=rows[PACK * b : PACK * (b + 1), :].rearrange("t (q e) -> t q e", e=RUN),
-                in_=gain[PASS * b : PASS * (b + 1)].rearrange("(q t e) -> t q e", t=PACK, e=RUN),
-            )
-        nc.sync.dma_start(out=rows[SLICES : SLICES + N_TILES, :], in_=bo.rearrange("(j p) -> j p", p=P))
-
         gather_words(1, 0)
         gather_words(1, 1)
         load_ws(1, placed(TAB1_AT, [P, PACK, N], F32, "ws_raw1"))
@@ -198,18 +202,24 @@ def tile_list_rally_shot_scores_kernel(
 
         whole = SLICES - PACK
         pieces = [(0, 0, M), (1, 0, M), (2, 0, HALF), (2, HALF, QUARTER), (2, HALF + QUARTER, QUARTER)]
-        gates = [keep.tile([P, PACK, w], F32, name=f"gates{i}") for i, (b, m0, w) in enumerate(pieces[:-1])]
-        gates = gates + [placed(END_AT, [P, PACK, QUARTER], F32, "gates4")]
+        gate = [keep.tile([P, M], F32, name=f"gate{s}") for s in range(whole)]
+        gates = {i: keep.tile([P, PACK, pieces[i][2]], F32, name=f"gates{i}") for i in (2, 3)}
+        gates[4] = placed(END_AT + 2048, [P, PACK, QUARTER], F32, "gates4")
         diffs = [keep.tile([P, PACK, M], F32, name=f"diffs{b}") for b in range(HP)]
+        z_rows = [keep.tile([P, PACK, M], BF16, name=f"z_rows{b}") for b in range(HP - 1)]
         follow = [None] * SLICES
 
         def make_gate(i, t):
             b, m0, w = pieces[i]
             entries = pos1_sb[:, m0 // GROUP : (m0 + w) // GROUP]
-            nc.scalar.activation(gates[i][:, t, :], h[PACK * b + t][:].indirect(entries), ACT.Sigmoid)
+            dst = gate[PACK * b + t][:] if b < HP - 1 else gates[i][:, t, :]
+            nc.scalar.activation(dst, h[PACK * b + t][:].indirect(entries), ACT.Sigmoid)
 
         def pick_follow(s):
-            follow[s] = keep.tile([P, M], F32, name=f"follow{s}")
+            if s == SLICES - 1:
+                follow[s] = placed(END_AT, [P, M], F32, f"follow{s}")
+            else:
+                follow[s] = keep.tile([P, M], F32, name=f"follow{s}")
             if s < VECTOR_FOLLOWS:
                 nc.vector.tensor_copy(follow[s][:], h[s][:].indirect(pos3_sb[:]))
             else:
@@ -220,8 +230,18 @@ def tile_list_rally_shot_scores_kernel(
 
         def apply_gain(s):
             b, t = divmod(s, PACK)
-            row = (gates if s < whole else diffs)[b][:, t, :]
-            nc.vector.tensor_scalar(row, row, per_part[:, s : s + 1], None, ALU.mult)
+            row = diffs[b][:, t, :]
+            if s < whole:
+                nc.vector.scalar_tensor_tensor(
+                    out=z_rows[b][:, t, :],
+                    in0=row,
+                    scalar=per_part[:, t, 0, b : b + 1],
+                    in1=gate[s][:],
+                    op0=ALU.mult,
+                    op1=ALU.mult,
+                )
+            else:
+                nc.vector.tensor_scalar(row, row, per_part[:, t, 0, b : b + 1], None, ALU.mult)
 
         def make_z(woven, gate4, diff4):
             nc.vector.tensor_tensor(
@@ -239,8 +259,7 @@ def tile_list_rally_shot_scores_kernel(
                 out=codes[:].bitcast(FP8X4), scales=scales[:], in_=woven[:].rearrange("p w t -> p (w t)")
             )
 
-        ws_woven = [keep.tile([P, N, PACK], BF16, name=f"ws_woven{b}", align_bytes=64) for b in range(HP - 1)]
-        ws_woven = ws_woven + [after_h(whole + 2, [P, N, PACK], BF16, "ws_woven2")]
+        ws_woven = [keep.tile([P, N, PACK], BF16, name=f"ws_woven{b}", align_bytes=64) for b in range(HP)]
         ws_w = [None] * HP
         ws_s = [keep.tile([P, N], U8, name=f"ws_s{b}", align_bytes=64) for b in range(HP)]
         z_woven = [None] * len(pieces)
@@ -257,7 +276,10 @@ def tile_list_rally_shot_scores_kernel(
         def weave_z(i, woven):
             z_woven[i] = woven
             b, m0, w = pieces[i]
-            make_z(woven[:], gates[i][:], diffs[b][:, :, m0 : m0 + w])
+            if b < HP - 1:
+                weave(woven[:], z_rows[b][:])
+            else:
+                make_z(woven[:], gates[i][:], diffs[b][:, :, m0 : m0 + w])
 
         def quantize_z(i, codes):
             z_w[i] = codes
@@ -283,11 +305,11 @@ def tile_list_rally_shot_scores_kernel(
 
         def store(half, j):
             cols = slice(HALF * half, HALF * (half + 1))
-            res = keep.tile([P, HALF], F32, name=f"res{j}")
+            res = after_h(SLICES - 1, [P, HALF], F32, f"res{j}", at=4 * HALF * (j - 1))
             nc.vector.scalar_tensor_tensor(
                 out=res[:],
                 in0=scores[half, j][:],
-                scalar=per_part[:, SLICES + j : SLICES + j + 1],
+                scalar=per_part[:, j, 1, 0:1],
                 in1=lev_sb[:, cols],
                 op0=ALU.add,
                 op1=ALU.mult,
@@ -296,7 +318,7 @@ def tile_list_rally_shot_scores_kernel(
 
         def store_beside(j, offset):
             biased = keep.tile([P, HALF], F32, name=f"biased{j}")
-            nc.scalar.activation(biased[:], scores[0, j][:], ACT.Identity, bias=per_part[:, SLICES + j : SLICES + j + 1])
+            nc.scalar.activation(biased[:], scores[0, j][:], ACT.Identity, bias=per_part[:, j, 1, 0:1])
             res = placed(offset, [P, HALF], F32, f"res_beside{j}")
             nc.gpsimd.tensor_tensor(res[:], biased[:], lev_sb[:, 0:HALF], ALU.mult)
             nc.scalar.dma_start(out=out[P * j : P * (j + 1), 0:HALF], in_=res[:])
@@ -324,50 +346,43 @@ def tile_list_rally_shot_scores_kernel(
         for s in range(PACK):
             for c in range(2):
                 first_pass(s, c, 0, True, False)
-        for c in range(2):
-            for s in range(3):
-                fill_bank(s, c)
-                empty_bank(s, c, nc.vector.tensor_copy if (s, c) in ((2, 0), (0, 1)) else nc.scalar.copy)
+        for s, c in ((0, 0), (1, 0), (2, 0), (3, 0), (0, 1), (1, 1)):
+            fill_bank(s, c)
+            empty_bank(s, c, nc.vector.tensor_copy if c or s == 2 else nc.scalar.copy)
         order_later_wf()
         pick_follow(0)
         pick_follow(1)
         pick_diff(0)
-        turned = psum.tile([P, P], F32, name="turned", tag="bank1")
-        nc.tensor.transpose(turned[:], rows[:], ident[:])
-        nc.scalar.copy(per_part[:], turned[:, 0 : SLICES + N_TILES])
-        for u in range(whole - 1):
-            if u > 0:
-                first_product(u + 2)
-            if u == 0:
-                pick_follow(2)
+        for u in range(whole):
+            if u == 1:
+                for s in (2, 3):
+                    fill_bank(s, 1)
+                    empty_bank(s, 1, nc.scalar.copy)
             elif u > 1:
+                first_product(u + 2)
+            if u > 0:
                 pick_follow(u + 1)
             make_gate(*divmod(u, PACK))
-            if u != 1:
-                pick_diff(u + 1)
+            pick_diff(u + 1)
             apply_gain(u)
-            if u == 0:
-                pick_diff(2)
             for work in beside.get(u, []):
                 work()
-        make_gate(1, PACK - 1)
-        apply_gain(whole - 1)
-        first_product(whole + 1)
-        pick_follow(whole)
-        for c in range(2):
-            fill_bank(whole + 2, c)
-            empty_bank(whole + 2, c, nc.vector.tensor_copy if c else nc.scalar.copy)
+        apply_gain(whole)
         weave_z(1, keep.tile([P, M, PACK], BF16, name="z_woven1", align_bytes=64))
-        pick_diff(whole)
-        quantize_z(1, keep.tile([P, M], U32, name="z_w1", align_bytes=64))
+        first_product(whole + 2)
         pick_follow(whole + 1)
+        pick_diff(whole + 1)
+        z_w[1] = keep.tile([P, HALF], U32, name="z_w1", align_bytes=64)
+        quantize(z_w[1], z_s[1][:, 0:HALF], z_woven[1][:, 0:HALF, :])
         first_product(whole + 3)
         pick_follow(whole + 2)
         pick_follow(whole + 3)
-        for s in range(whole + 1, SLICES):
+        for s in range(whole + 2, SLICES):
             pick_diff(s)
             apply_gain(s - 1)
         apply_gain(SLICES - 1)
+        late_w = placed(END_AT, [P, HALF], U32, "late_w")
+        quantize(late_w, z_s[1][:, HALF:], z_woven[1][:, HALF:, :])
         for i in range(HP - 1, len(pieces)):
             for t in range(PACK):
                 make_gate(i, t)
@@ -380,52 +395,55 @@ def tile_list_rally_shot_scores_kernel(
         nc.sync.dma_start(out=lev_sb[:], in_=lev.partition_broadcast(P))
         products(0, range(HP))
         ends = [psum.tile([P, 2, QUARTER], F32, name=f"end{k}", tag=f"bank{N_TILES + k}") for k in range(4)]
-        end_res = [keep.tile([P, 2, QUARTER], F32, name=f"end_res{k}") for k in range(4)]
+        end_res = [after_h(SLICES - 1, [P, 2, QUARTER], F32, f"end_res{k}", at=4 * HALF * (2 + k)) for k in range(2)]
+        end_res = end_res + [keep.tile([P, 2, QUARTER], F32, name=f"end_res{k}") for k in range(2, 4)]
 
         def end_products(k, b):
             cols = slice(HALF + QUARTER * k, HALF + QUARTER * (k + 1))
             last = b == HP - 1
+            codes = (z_w[0][:, cols], late_w[:, QUARTER * k : QUARTER * (k + 1)], z_w[HP + k][:] if last else None)[b]
             for j in range(N_TILES):
                 nc.tensor.matmul_mx(
                     out=ends[2 * k + j // 2][:, j % 2, :],
                     lhsT=ws_w[b][:, P * j : P * (j + 1)].bitcast(FP8X4),
                     lhsT_scale=ws_s[b][:, P * j : P * (j + 1)],
-                    rhs=(z_w[HP + k][:] if last else z_w[b][:, cols]).bitcast(FP8X4),
+                    rhs=codes.bitcast(FP8X4),
                     rhs_scale=z_s[HP + k][:] if last else z_s[b][:, cols],
                     start=(b == 0 and j % 2 == 0),
                     stop=(last and j % 2 == 1),
                 )
 
-        def end_store(k):
+        def end_store(k, j):
             cols = slice(HALF + QUARTER * k, HALF + QUARTER * (k + 1))
-            for pair in range(2):
-                res = end_res[2 * k + pair]
-                for i in range(2):
-                    j = 2 * pair + i
-                    nc.vector.scalar_tensor_tensor(
-                        out=res[:, i, :],
-                        in0=ends[2 * k + pair][:, i, :],
-                        scalar=per_part[:, SLICES + j : SLICES + j + 1],
-                        in1=lev_sb[:, cols],
-                        op0=ALU.add,
-                        op1=ALU.mult,
-                    )
-                    if k == 1 and pair == 1:
-                        nc.sync.dma_start(out=out[P * j : P * (j + 1), cols], in_=res[:, i, :])
-                if k == 0 or pair == 0:
-                    rows_out = out[2 * P * pair : 2 * P * (pair + 1), cols]
-                    nc.sync.dma_start(out=rows_out.rearrange("(i p) m -> p i m", p=P), in_=res[:])
+            pair, i = divmod(j, 2)
+            res = end_res[2 * k + pair]
+            nc.vector.scalar_tensor_tensor(
+                out=res[:, i, :],
+                in0=ends[2 * k + pair][:, i, :],
+                scalar=per_part[:, j, 1, 0:1],
+                in1=lev_sb[:, cols],
+                op0=ALU.add,
+                op1=ALU.mult,
+            )
+            if k == 1 and pair == 1:
+                nc.sync.dma_start(out=out[P * j : P * (j + 1), cols], in_=res[:, i, :])
+            elif i == 1:
+                rows_out = out[2 * P * pair : 2 * P * (pair + 1), cols]
+                nc.sync.dma_start(out=rows_out.rearrange("(i p) m -> p i m", p=P), in_=res[:])
 
         for k in range(2):
             for b in range(HP - 1):
                 end_products(k, b)
         end_products(0, HP - 1)
         weave_z(4, placed(Z3_WOVEN_AT + 512, [P, QUARTER, PACK], BF16, "z_woven4"))
-        store_beside(0, END_AT)
+        store_beside(0, END_AT + 2048)
         store(0, 1)
         store(0, 2)
+        end_store(0, 0)
         quantize_z(4, keep.tile([P, QUARTER], U32, name="z_w4", align_bytes=64))
         end_products(1, HP - 1)
         store_beside(3, Z3_WOVEN_AT)
-        end_store(0)
-        end_store(1)
+        for j in range(1, N_TILES):
+            end_store(0, j)
+        for j in range(N_TILES):
+            end_store(1, j)

@@ -259,7 +259,8 @@ def tile_list_rally_shot_scores_kernel(
                 out=codes[:].bitcast(FP8X4), scales=scales[:], in_=woven[:].rearrange("p w t -> p (w t)")
             )
 
-        ws_woven = [keep.tile([P, N, PACK], BF16, name=f"ws_woven{b}", align_bytes=64) for b in range(HP)]
+        ws_woven = [keep.tile([P, N, PACK], BF16, name=f"ws_woven{b}", align_bytes=64) for b in range(HP - 1)]
+        ws_woven = ws_woven + [after_h(whole + 2, [P, N, PACK], BF16, "ws_woven2")]
         ws_w = [None] * HP
         ws_s = [keep.tile([P, N], U8, name=f"ws_s{b}", align_bytes=64) for b in range(HP)]
         z_woven = [None] * len(pieces)
@@ -367,9 +368,13 @@ def tile_list_rally_shot_scores_kernel(
             apply_gain(u)
             for work in beside.get(u, []):
                 work()
+            if u == whole - 2:
+                fill_bank(whole + 2, 1)
+                empty_bank(whole + 2, 1, nc.vector.tensor_copy)
         apply_gain(whole)
         weave_z(1, keep.tile([P, M, PACK], BF16, name="z_woven1", align_bytes=64))
-        first_product(whole + 2)
+        fill_bank(whole + 2, 0)
+        empty_bank(whole + 2, 0, nc.scalar.copy)
         pick_follow(whole + 1)
         pick_diff(whole + 1)
         z_w[1] = keep.tile([P, HALF], U32, name="z_w1", align_bytes=64)

@@ -34,18 +34,20 @@ VECTOR_FOLLOWS = 2
 QUARTER = M // 4
 BANKS = 8
 
-TAB1_AT = 0
-WF_LATER_AT = 8192
-TAB0_AT = 16384
-WF_FIRST_AT = TAB0_AT + 8192
+WF01_AT = 0
+PICKED_AT = 512
+TAB1_AT = 1024
+WF_LATER_AT = TAB1_AT + 8192
+TAB0_AT = TAB1_AT + 16384
+LATE_RAW_AT = TAB0_AT + 8192
 WF_RAW_AT = TAB0_AT + 12800
-Z1_WOVEN_AT = 40960
-Z3_WOVEN_AT = 45056
-END_AT = 49152
+Z3_WOVEN_AT = 46080
+END_AT = 50176
 WF_BYTES = 2048
 H_BYTES = 4 * S
 V_SCALES = S // 4
-WF_SCALES = H // 4
+WF_SCALES = PASS // 4
+LATE_SCALES = (H - PASS) // 4
 
 
 def tile_list_rally_shot_scores_kernel(
@@ -72,7 +74,7 @@ def tile_list_rally_shot_scores_kernel(
 
         tab_w = [None] * KP
         tab_s = keep.tile([P, T], U8, name="tab_s", align_bytes=64)
-        picked_s = placed(TAB1_AT, [P, S], U8, "picked_s")
+        picked_s = placed(PICKED_AT, [P, S], U8, "picked_s")
         planes = [keep.tile([P, V_SCALES + WF_SCALES], I32, name=f"plane{a}", align_bytes=64) for a in range(KP)]
         v_w = [[keep.tile([P, BANK], U32, name=f"v_w{a}_{c}", align_bytes=64) for c in range(2)] for a in range(KP)]
         wf_s_raw = keep.tile([KP * BLOCKS, WF_SCALES], I32, name="wf_s_raw")
@@ -106,10 +108,18 @@ def tile_list_rally_shot_scores_kernel(
             entries = offs_sb[:, c * (BANK // GROUP) : (c + 1) * (BANK // GROUP)]
             nc.vector.tensor_copy(v_w[a][c][:], tab_w[a][:].bitcast(U32).indirect(entries))
 
+        def order_first_wf(a, raw):
+            nc.scalar.copy(
+                wf_w[0][:, a, :].bitcast(U32).rearrange("p (t q e) -> p t q e", t=PACK, q=BLOCKS),
+                raw[:].bitcast(U32).rearrange("p (q t e) -> p t q e", t=PACK, q=BLOCKS),
+            )
+
+        def load_first_wf(a, raw):
+            nc.sync.dma_start(out=raw[:], in_=wf_words[a, :, 0 : 2 * PASS].bitcast(I32))
+
         def order_wf(b, raw):
-            offset = WF_LATER_AT + WF_BYTES * (b - 1) if b else WF_FIRST_AT
-            wf_w[b] = placed(offset, [P, KP, PASS // 2], I32, f"wf_w{b}")
-            (nc.gpsimd if b else nc.vector).tensor_copy(
+            wf_w[b] = placed(WF_LATER_AT + WF_BYTES * (b - 1), [P, KP, PASS // 2], I32, f"wf_w{b}")
+            nc.gpsimd.tensor_copy(
                 out=wf_w[b][:].rearrange("p a (t q e) -> p a t q e", t=PACK, q=BLOCKS),
                 in_=raw.rearrange("p a (q t e) -> p a t q e", t=PACK, q=BLOCKS),
             )
@@ -117,14 +127,17 @@ def tile_list_rally_shot_scores_kernel(
         rows32 = slice(0, KP * BLOCKS)
         nc.sync.dma_start(out=tab_s[rows32, :].bitcast(I32), in_=tab_scales.rearrange("a q t -> (a q) t").bitcast(I32))
         nc.sync.dma_start(offs_sb[:], offs)
-        nc.sync.dma_start(out=wf_s_raw[:], in_=wf_scales.rearrange("a q c -> (a q) c").bitcast(I32))
+        nc.sync.dma_start(out=wf_s_raw[:], in_=wf_scales.rearrange("a q c -> (a q) c")[:, 0:PASS].bitcast(I32))
         nc.sync.dma_start(pos3_sb[:], pos3)
+        nc.sync.dma_start(pos2_sb[:], pos2)
+        nc.sync.dma_start(pos1_sb[:], pos1)
         load_words(0, TAB0_AT)
-        wf_first = keep.tile([P, KP, PASS // 2], I32, name="wf_first")
-        load_wf_words(wf_first, 0, 1)
         raw_rows = keep.tile([P, PASS], F32, name="raw_rows")
         nc.sync.dma_start(out=raw_rows[0:HP, :], in_=gain.rearrange("(b r) -> b r", b=HP))
         nc.sync.dma_start(out=raw_rows[32:33, :], in_=bo.rearrange("(o n) -> o n", o=1))
+        wf_w[0] = keep.tile([P, KP, PASS // 2], I32, name="wf_w0", align_bytes=64)
+        wf_00 = keep.tile([P, PASS // 2], I32, name="wf_00")
+        load_first_wf(0, wf_00)
         nc.vector.memset(warm[:, 0:1], 0.0)
         nc.scalar.activation(warm[:, 1:2], warm[:, 0:1], ACT.Sigmoid)
 
@@ -147,24 +160,33 @@ def tile_list_rally_shot_scores_kernel(
 
         nc.vector.tensor_copy(picked_s[:], tab_s[:].indirect(offs_sb[:]))
         nc.vector.tensor_copy(
-            out=planes[0][rows32, V_SCALES:].rearrange("p (b t q e) -> p b t q e", b=HP, t=PACK, q=BLOCKS),
-            in_=wf_s_raw[:].rearrange("p (b q t e) -> p b t q e", b=HP, t=PACK, q=BLOCKS),
+            out=planes[0][rows32, V_SCALES:].rearrange("p (t q e) -> p t q e", t=PACK, q=BLOCKS),
+            in_=wf_s_raw[:].rearrange("p (q t e) -> p t q e", t=PACK, q=BLOCKS),
         )
         nc.vector.tensor_copy(planes[0][rows32, 0:V_SCALES], picked_s[rows32, :].bitcast(I32))
         for quad in range(1, QUADS):
             move_scales(0, quad, nc.sync)
         load_words(1, TAB1_AT)
+        wf_01 = placed(WF01_AT, [P, PASS // 2], I32, "wf_01")
+        load_first_wf(1, wf_01)
         for quad in range(QUADS):
             move_scales(1, quad, nc.sync)
 
         gather_words(0, 0)
         gather_words(0, 1)
-        order_wf(0, wf_first[:])
+        order_first_wf(0, wf_00)
+        order_first_wf(1, wf_01)
 
-        nc.sync.dma_start(pos1_sb[:], pos1)
-        nc.sync.dma_start(pos2_sb[:], pos2)
         wf_later = placed(WF_RAW_AT, [P, KP, PASS], I32, "wf_later")
         load_wf_words(wf_later, 1, HP - 1)
+        late_raw = placed(LATE_RAW_AT, [P, KP, LATE_SCALES], I32, "late_raw")
+        late_s = keep.tile([P, KP, LATE_SCALES], I32, name="late_s", align_bytes=64)
+        nc.vector.memset(late_raw[:], 0)
+        for quad in range(QUADS):
+            nc.sync.dma_start(
+                out=late_raw[32 * quad : 32 * quad + 4],
+                in_=wf_scales[:, 4 * quad : 4 * quad + 4, PASS:].bitcast(I32).rearrange("a i c -> i a c"),
+            )
         load_ws(0, placed(TAB0_AT, [P, PACK, N], F32, "ws_raw0"))
         gather_words(1, 0)
         gather_words(1, 1)
@@ -177,10 +199,14 @@ def tile_list_rally_shot_scores_kernel(
             b, t = divmod(s, PACK)
             if start:
                 acc[s, c] = psum.tile([P, BANK], F32, name="acc", tag=f"bank{(2 * s + c) % BANKS}")
+            if b:
+                wf_plane = late_s[:, a, P // 4 * (s - PACK) : P // 4 * (s - PACK + 1)]
+            else:
+                wf_plane = planes[a][:, V_SCALES + P // 4 * s : V_SCALES + P // 4 * (s + 1)]
             nc.tensor.matmul_mx(
                 out=acc[s, c][:],
                 lhsT=wf_w[b][:, a, P // 2 * t : P // 2 * (t + 1)].bitcast(FP4X4),
-                lhsT_scale=planes[a][:, V_SCALES + P // 4 * s : V_SCALES + P // 4 * (s + 1)].bitcast(U8),
+                lhsT_scale=wf_plane.bitcast(U8),
                 rhs=v_w[a][c][:].bitcast(FP8X4),
                 rhs_scale=planes[a][:, BANK // 4 * c : BANK // 4 * (c + 1)].bitcast(U8),
                 start=start,
@@ -325,8 +351,12 @@ def tile_list_rally_shot_scores_kernel(
             nc.scalar.dma_start(out=out[P * j : P * (j + 1), 0:HALF], in_=res[:])
 
         def order_later_wf():
-            for b in range(1, HP):
-                order_wf(b, wf_later[:, :, PASS // 2 * (b - 1) : PASS // 2 * b])
+            order_wf(1, wf_later[:, :, 0 : PASS // 2])
+            nc.gpsimd.tensor_copy(
+                out=late_s[:].rearrange("p a (b t q e) -> p (a b) t q e", t=PACK, q=BLOCKS, e=2),
+                in_=late_raw[:].rearrange("p a (b q t e) -> p (a b) t q e", t=PACK, q=BLOCKS, e=2),
+            )
+            order_wf(2, wf_later[:, :, PASS // 2 :])
             load_ws(2, placed(WF_RAW_AT, [P, PACK, N], F32, "ws_raw2"))
 
         def products(half, passes):

@@ -33,6 +33,8 @@ HALF = M // 2
 VECTOR_FOLLOWS = 2
 QUARTER = M // 4
 BANKS = 8
+OPEN = BANK // 2
+EARLY = 2048
 
 WF01_AT = 0
 PICKED_AT = 512
@@ -72,7 +74,7 @@ def tile_list_rally_shot_scores_kernel(
         def after_h(s, shape, dtype, name, at=0):
             return rows_of_h.tile(shape, dtype, name=name, tag=name, align_bytes=64, offset=H_BYTES * s + at)
 
-        tab_w = [None] * KP
+        tab_w = [placed(TAB0_AT, [P, T], I32, "tab_w0"), None]
         tab_s = keep.tile([P, T], U8, name="tab_s", align_bytes=64)
         picked_s = placed(PICKED_AT, [P, S], U8, "picked_s")
         planes = [keep.tile([P, V_SCALES + WF_SCALES], I32, name=f"plane{a}", align_bytes=64) for a in range(KP)]
@@ -80,13 +82,12 @@ def tile_list_rally_shot_scores_kernel(
         wf_s_raw = keep.tile([KP * BLOCKS, WF_SCALES], I32, name="wf_s_raw")
         wf_w = [None] * HP
         ident = keep.tile([P, P], F32, name="ident")
-        per_part = keep.tile([P, PACK, 2, HP], F32, name="per_part")
+        gain_sb = keep.tile([P, PACK, HP], F32, name="gain_sb")
         ws_raw = [None] * HP
         warm = keep.tile([P, 2], F32, name="warm")
 
-        def load_words(a, offset):
-            tab_w[a] = placed(offset, [P, T], I32, f"tab_w{a}")
-            nc.sync.dma_start(out=tab_w[a][:], in_=tab_words[a].rearrange("p t i -> p (t i)").bitcast(I32))
+        def load_words(a, dst, cols):
+            nc.sync.dma_start(out=dst, in_=tab_words[a].rearrange("p t i -> p (t i)").bitcast(I32)[:, cols])
 
         def load_wf_words(raw, b, count):
             nc.sync.dma_start(
@@ -104,9 +105,10 @@ def tile_list_rally_shot_scores_kernel(
             row = BLOCKS * a + 4 * quad
             queue.dma_start(out=planes[a][32 * quad : 32 * quad + 4, :], in_=planes[0][row : row + 4, :])
 
-        def gather_words(a, c):
-            entries = offs_sb[:, c * (BANK // GROUP) : (c + 1) * (BANK // GROUP)]
-            nc.vector.tensor_copy(v_w[a][c][:], tab_w[a][:].bitcast(U32).indirect(entries))
+        def gather_words(a, c, first=0, count=BANK):
+            at = (BANK * c + first) // GROUP
+            entries = offs_sb[:, at : at + count // GROUP]
+            nc.vector.tensor_copy(v_w[a][c][:, first : first + count], tab_w[a][:].bitcast(U32).indirect(entries))
 
         def order_first_wf(a, raw):
             nc.scalar.copy(
@@ -131,12 +133,13 @@ def tile_list_rally_shot_scores_kernel(
         nc.sync.dma_start(pos3_sb[:], pos3)
         nc.sync.dma_start(pos2_sb[:], pos2)
         nc.sync.dma_start(pos1_sb[:], pos1)
-        load_words(0, TAB0_AT)
+        load_words(0, tab_w[0][:], slice(0, T))
         raw_rows = keep.tile([P, PASS], F32, name="raw_rows")
         nc.sync.dma_start(out=raw_rows[0:HP, :], in_=gain.rearrange("(b r) -> b r", b=HP))
-        nc.sync.dma_start(out=raw_rows[32:33, :], in_=bo.rearrange("(o n) -> o n", o=1))
         wf_w[0] = keep.tile([P, KP, PASS // 2], I32, name="wf_w0", align_bytes=64)
         wf_00 = keep.tile([P, PASS // 2], I32, name="wf_00")
+        early = keep.tile([P, EARLY], I32, name="early")
+        load_words(1, early[:], slice(0, EARLY))
         load_first_wf(0, wf_00)
         nc.vector.memset(warm[:, 0:1], 0.0)
         nc.scalar.activation(warm[:, 1:2], warm[:, 0:1], ACT.Sigmoid)
@@ -152,11 +155,10 @@ def tile_list_rally_shot_scores_kernel(
             rows[0:HP].rearrange("b t (q e) -> b t q e", e=RUN),
             raw_rows[0:HP, :].rearrange("b (q t e) -> b t q e", t=PACK, e=RUN),
         )
-        nc.gpsimd.tensor_copy(rows[32:33].rearrange("o j p -> o (j p)"), raw_rows[32:33, :])
         turned = psum.tile([P, PACK, P], F32, name="turned", tag=f"bank{BANKS - 1}")
         for t in range(PACK):
             nc.tensor.transpose(turned[:, t, :], rows[:, t, :], ident[:])
-        nc.scalar.copy(per_part[:], turned[:].rearrange("p t (g x) -> p t g x", x=32)[:, :, 0:2, 0:HP])
+        nc.scalar.copy(gain_sb[:], turned[:, :, 0:HP])
 
         nc.vector.tensor_copy(picked_s[:], tab_s[:].indirect(offs_sb[:]))
         nc.vector.tensor_copy(
@@ -166,7 +168,8 @@ def tile_list_rally_shot_scores_kernel(
         nc.vector.tensor_copy(planes[0][rows32, 0:V_SCALES], picked_s[rows32, :].bitcast(I32))
         for quad in range(1, QUADS):
             move_scales(0, quad, nc.sync)
-        load_words(1, TAB1_AT)
+        tab_w[1] = placed(TAB1_AT, [P, T], I32, "tab_w1")
+        load_words(1, tab_w[1][:, EARLY:], slice(EARLY, T))
         wf_01 = placed(WF01_AT, [P, PASS // 2], I32, "wf_01")
         load_first_wf(1, wf_01)
         for quad in range(QUADS):
@@ -174,6 +177,7 @@ def tile_list_rally_shot_scores_kernel(
 
         gather_words(0, 0)
         gather_words(0, 1)
+        nc.vector.tensor_copy(tab_w[1][:, 0:EARLY], early[:])
         order_first_wf(0, wf_00)
         order_first_wf(1, wf_01)
 
@@ -188,7 +192,8 @@ def tile_list_rally_shot_scores_kernel(
                 in_=wf_scales[:, 4 * quad : 4 * quad + 4, PASS:].bitcast(I32).rearrange("a i c -> i a c"),
             )
         load_ws(0, placed(TAB0_AT, [P, PACK, N], F32, "ws_raw0"))
-        gather_words(1, 0)
+        gather_words(1, 0, 0, OPEN)
+        gather_words(1, 0, OPEN, OPEN)
         gather_words(1, 1)
         load_ws(1, placed(TAB1_AT, [P, PACK, N], F32, "ws_raw1"))
 
@@ -198,7 +203,7 @@ def tile_list_rally_shot_scores_kernel(
         def first_pass(s, c, a, start, stop):
             b, t = divmod(s, PACK)
             if start:
-                acc[s, c] = psum.tile([P, BANK], F32, name="acc", tag=f"bank{(2 * s + c) % BANKS}")
+                acc[s, c] = psum.tile([P, BANK], F32, name="acc", tag=f"bank{(2 * s + c) % BANKS if b else PACK + s}")
             if b:
                 wf_plane = late_s[:, a, P // 4 * (s - PACK) : P // 4 * (s - PACK + 1)]
             else:
@@ -261,13 +266,13 @@ def tile_list_rally_shot_scores_kernel(
                 nc.vector.scalar_tensor_tensor(
                     out=z_rows[b][:, t, :],
                     in0=row,
-                    scalar=per_part[:, t, 0, b : b + 1],
+                    scalar=gain_sb[:, t, b : b + 1],
                     in1=gate[s][:],
                     op0=ALU.mult,
                     op1=ALU.mult,
                 )
             else:
-                nc.vector.tensor_scalar(row, row, per_part[:, t, 0, b : b + 1], None, ALU.mult)
+                nc.vector.tensor_scalar(row, row, gain_sb[:, t, b : b + 1], None, ALU.mult)
 
         def make_z(woven, gate4, diff4):
             nc.vector.tensor_tensor(
@@ -336,7 +341,7 @@ def tile_list_rally_shot_scores_kernel(
             nc.vector.scalar_tensor_tensor(
                 out=res[:],
                 in0=scores[half, j][:],
-                scalar=per_part[:, j, 1, 0:1],
+                scalar=bo_sb[:, j : j + 1],
                 in1=lev_sb[:, cols],
                 op0=ALU.add,
                 op1=ALU.mult,
@@ -345,7 +350,7 @@ def tile_list_rally_shot_scores_kernel(
 
         def store_beside(j, offset):
             biased = keep.tile([P, HALF], F32, name=f"biased{j}")
-            nc.scalar.activation(biased[:], scores[0, j][:], ACT.Identity, bias=per_part[:, j, 1, 0:1])
+            nc.scalar.activation(biased[:], scores[0, j][:], ACT.Identity, bias=bo_sb[:, j : j + 1])
             res = placed(offset, [P, HALF], F32, f"res_beside{j}")
             nc.gpsimd.tensor_tensor(res[:], biased[:], lev_sb[:, 0:HALF], ALU.mult)
             nc.scalar.dma_start(out=out[P * j : P * (j + 1), 0:HALF], in_=res[:])
@@ -374,12 +379,33 @@ def tile_list_rally_shot_scores_kernel(
             6: [lambda: quantize_ws(2, 6)],
         }
 
+        pairs = [psum.tile([P, 2, OPEN], F32, name=f"pair{n}", tag=f"bank{n}") for n in range(PACK)]
+
+        def open_pass(k, s, a):
+            nc.tensor.matmul_mx(
+                out=pairs[2 * k + s // 2][:, s % 2, :],
+                lhsT=wf_w[0][:, a, P // 2 * s : P // 2 * (s + 1)].bitcast(FP4X4),
+                lhsT_scale=planes[a][:, V_SCALES + P // 4 * s : V_SCALES + P // 4 * (s + 1)].bitcast(U8),
+                rhs=v_w[a][0][:, OPEN * k : OPEN * (k + 1)].bitcast(FP8X4),
+                rhs_scale=planes[a][:, OPEN // 4 * k : OPEN // 4 * (k + 1)].bitcast(U8),
+                start=(a == 0 and s % 2 == 0),
+                stop=(a == 1 and s % 2 == 1),
+            )
+
+        for k in range(2):
+            for s in range(PACK):
+                open_pass(k, s, 0)
         for s in range(PACK):
-            for c in range(2):
-                first_pass(s, c, 0, True, False)
-        for s, c in ((0, 0), (1, 0), (2, 0), (3, 0), (0, 1), (1, 1)):
-            fill_bank(s, c)
-            empty_bank(s, c, nc.vector.tensor_copy if c or s == 2 else nc.scalar.copy)
+            first_pass(s, 1, 0, True, False)
+        for k in range(2):
+            for s in range(PACK):
+                open_pass(k, s, 1)
+            for s in range(PACK):
+                copy = nc.vector.tensor_copy if k == 1 and s >= 2 else nc.scalar.copy
+                copy(h[s][:, OPEN * k : OPEN * (k + 1)], pairs[2 * k + s // 2][:, s % 2, :])
+        for s in range(2):
+            fill_bank(s, 1)
+            empty_bank(s, 1, nc.vector.tensor_copy)
         order_later_wf()
         pick_follow(0)
         pick_follow(1)
@@ -428,6 +454,9 @@ def tile_list_rally_shot_scores_kernel(
 
         lev_sb = placed(TAB0_AT, [P, M], F32, "lev_sb")
         nc.sync.dma_start(out=lev_sb[:], in_=lev.partition_broadcast(P))
+        bo_sb = placed(TAB0_AT + 2048, [P, N_TILES], F32, "bo_sb")
+        with nc.allow_non_contiguous_dma(reason="bo, one value a partition"):
+            nc.sync.dma_start(out=bo_sb[:], in_=bo.rearrange("(j p) -> p j", p=P))
         products(0, range(HP))
         ends = [psum.tile([P, 2, QUARTER], F32, name=f"end{k}", tag=f"bank{N_TILES + k}") for k in range(4)]
         end_res = [after_h(SLICES - 1, [P, 2, QUARTER], F32, f"end_res{k}", at=4 * HALF * (2 + k)) for k in range(2)]
@@ -455,7 +484,7 @@ def tile_list_rally_shot_scores_kernel(
             nc.vector.scalar_tensor_tensor(
                 out=res[:, i, :],
                 in0=ends[2 * k + pair][:, i, :],
-                scalar=per_part[:, j, 1, 0:1],
+                scalar=bo_sb[:, j : j + 1],
                 in1=lev_sb[:, cols],
                 op0=ALU.add,
                 op1=ALU.mult,

@@ -31,10 +31,12 @@ SLICES = H // P
 N_TILES = N // P
 HALF = M // 2
 VECTOR_FOLLOWS = 2
+SHARED_FOLLOW = 6
+SHARE = 128
 QUARTER = M // 4
 BANKS = 8
 OPEN = BANK // 2
-EARLY = 2048
+EARLY = 1280
 
 WF01_AT = 0
 PICKED_AT = 512
@@ -253,6 +255,10 @@ def tile_list_rally_shot_scores_kernel(
                 follow[s] = keep.tile([P, M], F32, name=f"follow{s}")
             if s < VECTOR_FOLLOWS:
                 nc.vector.tensor_copy(follow[s][:], h[s][:].indirect(pos3_sb[:]))
+            elif s == SHARED_FOLLOW:
+                cut = SHARE // GROUP
+                nc.vector.tensor_copy(follow[s][:, 0:SHARE], h[s][:].indirect(pos3_sb[:, 0:cut]))
+                nc.scalar.activation(follow[s][:, SHARE:], h[s][:].indirect(pos3_sb[:, cut:]), ACT.Copy)
             else:
                 nc.scalar.activation(follow[s][:], h[s][:].indirect(pos3_sb[:]), ACT.Copy)
 
@@ -320,7 +326,7 @@ def tile_list_rally_shot_scores_kernel(
         scores = {}
 
         def second_product(half, j, b):
-            if b == 0:
+            if b == 1:
                 scores[half, j] = psum.tile([P, HALF], F32, name="score", tag=f"bank{N_TILES * half + j}")
             last = b == HP - 1
             i = b + half if last else b
@@ -331,13 +337,13 @@ def tile_list_rally_shot_scores_kernel(
                 lhsT_scale=ws_s[b][:, P * j : P * (j + 1)],
                 rhs=z_w[i][:, cols].bitcast(FP8X4),
                 rhs_scale=z_s[i][:, cols],
-                start=(b == 0),
+                start=(b == 1),
                 stop=last,
             )
 
         def store(half, j):
             cols = slice(HALF * half, HALF * (half + 1))
-            res = after_h(SLICES - 1, [P, HALF], F32, f"res{j}", at=4 * HALF * (j - 1))
+            res = keep.tile([P, HALF], F32, name=f"res{j}")
             nc.vector.scalar_tensor_tensor(
                 out=res[:],
                 in0=scores[half, j][:],
@@ -433,39 +439,43 @@ def tile_list_rally_shot_scores_kernel(
         empty_bank(whole + 2, 0, nc.scalar.copy)
         pick_follow(whole + 1)
         pick_diff(whole + 1)
-        z_w[1] = keep.tile([P, HALF], U32, name="z_w1", align_bytes=64)
-        quantize(z_w[1], z_s[1][:, 0:HALF], z_woven[1][:, 0:HALF, :])
         first_product(whole + 3)
         pick_follow(whole + 2)
         pick_follow(whole + 3)
-        for s in range(whole + 2, SLICES):
-            pick_diff(s)
-            apply_gain(s - 1)
+        pick_diff(whole + 2)
+        apply_gain(whole + 1)
+        z_w[1] = keep.tile([P, HALF], U32, name="z_w1", align_bytes=64)
+        quantize(z_w[1], z_s[1][:, 0:HALF], z_woven[1][:, 0:HALF, :])
+        pick_diff(whole + 3)
+        apply_gain(whole + 2)
         apply_gain(SLICES - 1)
-        late_w = placed(END_AT, [P, HALF], U32, "late_w")
-        quantize(late_w, z_s[1][:, HALF:], z_woven[1][:, HALF:, :])
+        late_w = [placed(END_AT + 4 * QUARTER * k, [P, QUARTER], U32, f"late_w{k}") for k in range(2)]
+
+        def quantize_late(k):
+            cols = slice(HALF + QUARTER * k, HALF + QUARTER * (k + 1))
+            quantize(late_w[k], z_s[1][:, cols], z_woven[1][:, cols, :])
+
+        quantize_late(0)
         for i in range(HP - 1, len(pieces)):
             for t in range(PACK):
                 make_gate(i, t)
         weave_z(2, keep.tile([P, HALF, PACK], BF16, name="z_woven2", align_bytes=64))
-        weave_z(3, placed(Z3_WOVEN_AT + 2048, [P, QUARTER, PACK], BF16, "z_woven3"))
+        quantize_late(1)
         quantize_z(2, keep.tile([P, HALF], U32, name="z_w2", align_bytes=64))
-        quantize_z(3, keep.tile([P, QUARTER], U32, name="z_w3", align_bytes=64))
 
         lev_sb = placed(TAB0_AT, [P, M], F32, "lev_sb")
         nc.sync.dma_start(out=lev_sb[:], in_=lev.partition_broadcast(P))
         bo_sb = placed(TAB0_AT + 2048, [P, N_TILES], F32, "bo_sb")
         with nc.allow_non_contiguous_dma(reason="bo, one value a partition"):
             nc.sync.dma_start(out=bo_sb[:], in_=bo.rearrange("(j p) -> p j", p=P))
-        products(0, range(HP))
-        ends = [psum.tile([P, 2, QUARTER], F32, name=f"end{k}", tag=f"bank{N_TILES + k}") for k in range(4)]
-        end_res = [after_h(SLICES - 1, [P, 2, QUARTER], F32, f"end_res{k}", at=4 * HALF * (2 + k)) for k in range(2)]
-        end_res = end_res + [keep.tile([P, 2, QUARTER], F32, name=f"end_res{k}") for k in range(2, 4)]
+        products(0, (1, 0))
+        ends = [psum.tile([P, 2, QUARTER], F32, name=f"end{k}", tag=f"bank{(4, 5, 1, 2)[k]}") for k in range(4)]
+        end_res = [keep.tile([P, 2, QUARTER], F32, name=f"end_res{k}") for k in range(4)]
 
         def end_products(k, b):
             cols = slice(HALF + QUARTER * k, HALF + QUARTER * (k + 1))
             last = b == HP - 1
-            codes = (z_w[0][:, cols], late_w[:, QUARTER * k : QUARTER * (k + 1)], z_w[HP + k][:] if last else None)[b]
+            codes = (z_w[0][:, cols], late_w[k][:], z_w[HP + k][:] if last else None)[b]
             for j in range(N_TILES):
                 nc.tensor.matmul_mx(
                     out=ends[2 * k + j // 2][:, j % 2, :],
@@ -473,7 +483,7 @@ def tile_list_rally_shot_scores_kernel(
                     lhsT_scale=ws_s[b][:, P * j : P * (j + 1)],
                     rhs=codes.bitcast(FP8X4),
                     rhs_scale=z_s[HP + k][:] if last else z_s[b][:, cols],
-                    start=(b == 0 and j % 2 == 0),
+                    start=(b == 1 and j % 2 == 0),
                     stop=(last and j % 2 == 1),
                 )
 
@@ -495,19 +505,21 @@ def tile_list_rally_shot_scores_kernel(
                 rows_out = out[2 * P * pair : 2 * P * (pair + 1), cols]
                 nc.sync.dma_start(out=rows_out.rearrange("(i p) m -> p i m", p=P), in_=res[:])
 
-        for k in range(2):
-            for b in range(HP - 1):
-                end_products(k, b)
-        end_products(0, HP - 1)
-        weave_z(4, placed(Z3_WOVEN_AT + 512, [P, QUARTER, PACK], BF16, "z_woven4"))
-        store_beside(0, END_AT + 2048)
+        end_products(0, 1)
+        end_products(0, 0)
+        products(0, (HP - 1,))
+        weave_z(3, placed(Z3_WOVEN_AT, [P, QUARTER, PACK], BF16, "z_woven3"))
         store(0, 1)
+        quantize_z(3, keep.tile([P, QUARTER], U32, name="z_w3", align_bytes=64))
+        end_products(0, HP - 1)
         store(0, 2)
-        end_store(0, 0)
+        end_products(1, 1)
+        end_products(1, 0)
+        weave_z(4, placed(Z3_WOVEN_AT, [P, QUARTER, PACK], BF16, "z_woven4"))
+        store(0, 3)
         quantize_z(4, keep.tile([P, QUARTER], U32, name="z_w4", align_bytes=64))
         end_products(1, HP - 1)
-        store_beside(3, Z3_WOVEN_AT)
-        for j in range(1, N_TILES):
-            end_store(0, j)
-        for j in range(N_TILES):
-            end_store(1, j)
+        store_beside(0, Z3_WOVEN_AT)
+        for k in range(2):
+            for j in range(N_TILES):
+                end_store(k, j)

@@ -48,6 +48,7 @@ WF_RAW_AT = TAB0_AT + 12800
 Z3_WOVEN_AT = 46080
 END_AT = 50176
 WF_BYTES = 2048
+EARLY_AT = END_AT + 4096
 H_BYTES = 4 * S
 V_SCALES = S // 4
 WF_SCALES = PASS // 4
@@ -121,9 +122,9 @@ def tile_list_rally_shot_scores_kernel(
         def load_first_wf(a, raw):
             nc.sync.dma_start(out=raw[:], in_=wf_words[a, :, 0 : 2 * PASS].bitcast(I32))
 
-        def order_wf(b, raw):
+        def order_wf(b, raw, copy):
             wf_w[b] = placed(WF_LATER_AT + WF_BYTES * (b - 1), [P, KP, PASS // 2], I32, f"wf_w{b}")
-            nc.gpsimd.tensor_copy(
+            copy(
                 out=wf_w[b][:].rearrange("p a (t q e) -> p a t q e", t=PACK, q=BLOCKS),
                 in_=raw.rearrange("p a (q t e) -> p a t q e", t=PACK, q=BLOCKS),
             )
@@ -140,7 +141,7 @@ def tile_list_rally_shot_scores_kernel(
         nc.sync.dma_start(out=raw_rows[0:HP, :], in_=gain.rearrange("(b r) -> b r", b=HP))
         wf_w[0] = keep.tile([P, KP, PASS // 2], I32, name="wf_w0", align_bytes=64)
         wf_00 = keep.tile([P, PASS // 2], I32, name="wf_00")
-        early = keep.tile([P, EARLY], I32, name="early")
+        early = placed(EARLY_AT, [P, EARLY], I32, "early")
         load_words(1, early[:], slice(0, EARLY))
         load_first_wf(0, wf_00)
         nc.vector.memset(warm[:, 0:1], 0.0)
@@ -362,13 +363,12 @@ def tile_list_rally_shot_scores_kernel(
             nc.scalar.dma_start(out=out[P * j : P * (j + 1), 0:HALF], in_=res[:])
 
         def order_later_wf():
-            order_wf(1, wf_later[:, :, 0 : PASS // 2])
+            order_wf(1, wf_later[:, :, 0 : PASS // 2], nc.gpsimd.tensor_copy)
             nc.gpsimd.tensor_copy(
                 out=late_s[:].rearrange("p a (b t q e) -> p (a b) t q e", t=PACK, q=BLOCKS, e=2),
                 in_=late_raw[:].rearrange("p a (b q t e) -> p (a b) t q e", t=PACK, q=BLOCKS, e=2),
             )
-            order_wf(2, wf_later[:, :, PASS // 2 :])
-            load_ws(2, placed(WF_RAW_AT, [P, PACK, N], F32, "ws_raw2"))
+            load_ws(2, placed(EARLY_AT, [P, PACK, N], F32, "ws_raw2"))
 
         def products(half, passes):
             for b in passes:
@@ -376,13 +376,13 @@ def tile_list_rally_shot_scores_kernel(
                     second_product(half, j, b)
 
         beside = {
-            0: [lambda: weave_ws(0)],
+            0: [lambda: order_wf(2, wf_later[:, :, PASS // 2 :], nc.vector.tensor_copy), lambda: weave_ws(0)],
             1: [lambda: weave_ws(1)],
             2: [lambda: quantize_ws(0, 2), lambda: weave_ws(2)],
             3: [lambda: quantize_ws(1, 3)],
             4: [lambda: weave_z(0, after_h(4, [P, M, PACK], BF16, "z_woven0"))],
-            5: [lambda: quantize_z(0, after_h(5, [P, M], U32, "z_w0"))],
-            6: [lambda: quantize_ws(2, 6)],
+            5: [lambda: quantize_ws(2, 5)],
+            6: [lambda: quantize_z(0, after_h(6, [P, M], U32, "z_w0"))],
         }
 
         pairs = [psum.tile([P, 2, OPEN], F32, name=f"pair{n}", tag=f"bank{n}") for n in range(PACK)]
@@ -409,19 +409,15 @@ def tile_list_rally_shot_scores_kernel(
             for s in range(PACK):
                 copy = nc.vector.tensor_copy if k == 1 and s >= 2 else nc.scalar.copy
                 copy(h[s][:, OPEN * k : OPEN * (k + 1)], pairs[2 * k + s // 2][:, s % 2, :])
-        for s in range(2):
+        for s in range(PACK):
             fill_bank(s, 1)
-            empty_bank(s, 1, nc.vector.tensor_copy)
+            empty_bank(s, 1, nc.vector.tensor_copy if s in (1, 2) else nc.scalar.copy)
         order_later_wf()
         pick_follow(0)
         pick_follow(1)
         pick_diff(0)
         for u in range(whole):
-            if u == 1:
-                for s in (2, 3):
-                    fill_bank(s, 1)
-                    empty_bank(s, 1, nc.scalar.copy)
-            elif u > 1:
+            if u > 1:
                 first_product(u + 2)
             if u > 0:
                 pick_follow(u + 1)

from contextlib import ExitStack

import concourse.mybir as mybir
from concourse.masks import make_identity

T, S, M, K, H, N = 4096, 1024, 512, 1024, 1536, 512
FLOPS = 2 * K * H * S + 2 * H * N * M

F32 = mybir.dt.float32
BF16 = mybir.dt.bfloat16
I32 = mybir.dt.int32
U32 = mybir.dt.uint32
U16 = mybir.dt.uint16
U8 = mybir.dt.uint8
FP8X4 = mybir.dt.float8_e4m3fn_x4
FP4X4 = mybir.dt.float4_e2m1fn_x4
ALU = mybir.AluOpType
ACT = mybir.ActivationFunctionType

P = 128
PACK = 4
PASS = P * PACK
BLOCKS = 16
RUN = 8
QUADS = 4
GROUP = 16
BANK = 512
KP = K // PASS
HP = H // PASS
SLICES = H // P
N_TILES = N // P
HALF = M // 2
VECTOR_FOLLOWS = 2
SHARED_FOLLOW = 6
SHARE = 128
QUARTER = M // 4
BANKS = 8
OPEN = BANK // 2
EARLY = 1280

WF01_AT = 0
PICKED_AT = 512
TAB1_AT = 1024
WF_LATER_AT = TAB1_AT + 8192
TAB0_AT = TAB1_AT + 16384
LATE_RAW_AT = TAB0_AT + 8192
WF_RAW_AT = TAB0_AT + 12800
Z3_WOVEN_AT = 46080
END_AT = 50176
WF_BYTES = 2048
EARLY_AT = END_AT + 4096
H_BYTES = 4 * S
V_SCALES = S // 4
WF_SCALES = PASS // 4
LATE_SCALES = (H - PASS) // 4


def tile_list_rally_shot_scores_kernel(
    tc, tab_words, tab_scales, offs, wf_words, wf_scales, pos1, pos2, pos3, gain, ws, bo, lev, out
):
    nc = tc.nc
    with ExitStack() as ctx:
        lists = ctx.enter_context(tc.tile_pool(name="lists", bufs=1))
        keep = ctx.enter_context(tc.tile_pool(name="keep", bufs=1))
        shared = ctx.enter_context(tc.tile_pool(name="shared", bufs=1))
        rows_of_h = ctx.enter_context(tc.tile_pool(name="rows_of_h", bufs=1))
        psum = ctx.enter_context(tc.psum_pool(name="psum", bufs=1))

        offs_sb = lists.tile([P, S // GROUP], U16, name="offs_sb")
        pos1_sb = lists.tile([P, M // GROUP], U16, name="pos1_sb")
        pos2_sb = lists.tile([P, M // GROUP], U16, name="pos2_sb")
        pos3_sb = lists.tile([P, M // GROUP], U16, name="pos3_sb")

        def placed(offset, shape, dtype, name):
            return shared.tile(shape, dtype, name=name, tag=name, align_bytes=64, offset=offset)

        def after_h(s, shape, dtype, name, at=0):
            return rows_of_h.tile(shape, dtype, name=name, tag=name, align_bytes=64, offset=H_BYTES * s + at)

        tab_w = [placed(TAB0_AT, [P, T], I32, "tab_w0"), None]
        tab_s = keep.tile([P, T], U8, name="tab_s", align_bytes=64)
        picked_s = placed(PICKED_AT, [P, S], U8, "picked_s")
        planes = [keep.tile([P, V_SCALES + WF_SCALES], I32, name=f"plane{a}", align_bytes=64) for a in range(KP)]
        v_w = [[keep.tile([P, BANK], U32, name=f"v_w{a}_{c}", align_bytes=64) for c in range(2)] for a in range(KP)]
        wf_s_raw = keep.tile([KP * BLOCKS, WF_SCALES], I32, name="wf_s_raw")
        wf_w = [None] * HP
        ident = keep.tile([P, P], F32, name="ident")
        gain_sb = keep.tile([P, PACK, HP], F32, name="gain_sb")
        ws_raw = [None] * HP
        warm = keep.tile([P, 2], F32, name="warm")

        def load_words(a, dst, cols):
            nc.sync.dma_start(out=dst, in_=tab_words[a].rearrange("p t i -> p (t i)").bitcast(I32)[:, cols])

        def load_wf_words(raw, b, count):
            nc.sync.dma_start(
                out=raw[:],
                in_=wf_words[:, :, 2 * PASS * b : 2 * PASS * (b + count)].bitcast(I32).rearrange("a p c -> p a c"),
            )

        def load_ws(b, raw):
            ws_raw[b] = raw
            by_code = ws[PASS * b : PASS * (b + 1), :].rearrange("(q t e) n -> t q e n", t=PACK, e=RUN)
            for t in range(PACK):
                nc.sync.dma_start(out=raw[:, t, :], in_=by_code[t])

        def move_scales(a, quad, queue):
            row = BLOCKS * a + 4 * quad
            queue.dma_start(out=planes[a][32 * quad : 32 * quad + 4, :], in_=planes[0][row : row + 4, :])

        def gather_words(a, c, first=0, count=BANK):
            at = (BANK * c + first) // GROUP
            entries = offs_sb[:, at : at + count // GROUP]
            nc.vector.tensor_copy(v_w[a][c][:, first : first + count], tab_w[a][:].bitcast(U32).indirect(entries))

        def order_first_wf(a, raw):
            nc.scalar.copy(
                wf_w[0][:, a, :].bitcast(U32).rearrange("p (t q e) -> p t q e", t=PACK, q=BLOCKS),
                raw[:].bitcast(U32).rearrange("p (q t e) -> p t q e", t=PACK, q=BLOCKS),
            )

        def load_first_wf(a, raw):
            nc.sync.dma_start(out=raw[:], in_=wf_words[a, :, 0 : 2 * PASS].bitcast(I32))

        def order_wf(b, raw, copy):
            wf_w[b] = placed(WF_LATER_AT + WF_BYTES * (b - 1), [P, KP, PASS // 2], I32, f"wf_w{b}")
            copy(
                out=wf_w[b][:].rearrange("p a (t q e) -> p a t q e", t=PACK, q=BLOCKS),
                in_=raw.rearrange("p a (q t e) -> p a t q e", t=PACK, q=BLOCKS),
            )

        rows32 = slice(0, KP * BLOCKS)
        nc.sync.dma_start(out=tab_s[rows32, :].bitcast(I32), in_=tab_scales.rearrange("a q t -> (a q) t").bitcast(I32))
        nc.sync.dma_start(offs_sb[:], offs)
        nc.sync.dma_start(out=wf_s_raw[:], in_=wf_scales.rearrange("a q c -> (a q) c")[:, 0:PASS].bitcast(I32))
        nc.sync.dma_start(pos3_sb[:], pos3)
        nc.sync.dma_start(pos2_sb[:], pos2)
        nc.sync.dma_start(pos1_sb[:], pos1)
        load_words(0, tab_w[0][:], slice(0, T))
        raw_rows = keep.tile([P, PASS], F32, name="raw_rows")
        nc.sync.dma_start(out=raw_rows[0:HP, :], in_=gain.rearrange("(b r) -> b r", b=HP))
        wf_w[0] = keep.tile([P, KP, PASS // 2], I32, name="wf_w0", align_bytes=64)
        wf_00 = keep.tile([P, PASS // 2], I32, name="wf_00")
        early = placed(EARLY_AT, [P, EARLY], I32, "early")
        load_words(1, early[:], slice(0, EARLY))
        load_first_wf(0, wf_00)
        nc.vector.memset(warm[:, 0:1], 0.0)
        nc.scalar.activation(warm[:, 1:2], warm[:, 0:1], ACT.Sigmoid)

        nc.gpsimd.memset(tab_s[64:128, :].bitcast(I32), 0)
        nc.vector.memset(tab_s[32:64, :].bitcast(I32), 0)
        for a in range(KP):
            nc.gpsimd.memset(planes[a][:], 0)
        make_identity(nc, ident[:])
        rows = keep.tile([P, PACK, P], F32, name="rows")
        nc.gpsimd.memset(rows[:], 0.0)
        nc.gpsimd.tensor_copy(
            rows[0:HP].rearrange("b t (q e) -> b t q e", e=RUN),
            raw_rows[0:HP, :].rearrange("b (q t e) -> b t q e", t=PACK, e=RUN),
        )
        turned = psum.tile([P, PACK, P], F32, name="turned", tag=f"bank{BANKS - 1}")
        for t in range(PACK):
            nc.tensor.transpose(turned[:, t, :], rows[:, t, :], ident[:])
        nc.scalar.copy(gain_sb[:], turned[:, :, 0:HP])

        nc.vector.tensor_copy(picked_s[:], tab_s[:].indirect(offs_sb[:]))
        nc.vector.tensor_copy(
            out=planes[0][rows32, V_SCALES:].rearrange("p (t q e) -> p t q e", t=PACK, q=BLOCKS),
            in_=wf_s_raw[:].rearrange("p (q t e) -> p t q e", t=PACK, q=BLOCKS),
        )
        nc.vector.tensor_copy(planes[0][rows32, 0:V_SCALES], picked_s[rows32, :].bitcast(I32))
        for quad in range(1, QUADS):
            move_scales(0, quad, nc.sync)
        tab_w[1] = placed(TAB1_AT, [P, T], I32, "tab_w1")
        load_words(1, tab_w[1][:, EARLY:], slice(EARLY, T))
        wf_01 = placed(WF01_AT, [P, PASS // 2], I32, "wf_01")
        load_first_wf(1, wf_01)
        for quad in range(QUADS):
            move_scales(1, quad, nc.sync)

        gather_words(0, 0)
        gather_words(0, 1)
        nc.vector.tensor_copy(tab_w[1][:, 0:EARLY], early[:])
        order_first_wf(0, wf_00)
        order_first_wf(1, wf_01)

        wf_later = placed(WF_RAW_AT, [P, KP, PASS], I32, "wf_later")
        load_wf_words(wf_later, 1, HP - 1)
        late_raw = placed(LATE_RAW_AT, [P, KP, LATE_SCALES], I32, "late_raw")
        late_s = keep.tile([P, KP, LATE_SCALES], I32, name="late_s", align_bytes=64)
        nc.vector.memset(late_raw[:], 0)
        for quad in range(QUADS):
            nc.sync.dma_start(
                out=late_raw[32 * quad : 32 * quad + 4],
                in_=wf_scales[:, 4 * quad : 4 * quad + 4, PASS:].bitcast(I32).rearrange("a i c -> i a c"),
            )
        load_ws(0, placed(TAB0_AT, [P, PACK, N], F32, "ws_raw0"))
        gather_words(1, 0, 0, OPEN)
        gather_words(1, 0, OPEN, OPEN)
        gather_words(1, 1)
        load_ws(1, placed(TAB1_AT, [P, PACK, N], F32, "ws_raw1"))

        h = [after_h(s, [P, S], F32, f"h{s}") for s in range(SLICES)]
        acc = {}

        def first_pass(s, c, a, start, stop):
            b, t = divmod(s, PACK)
            if start:
                acc[s, c] = psum.tile([P, BANK], F32, name="acc", tag=f"bank{(2 * s + c) % BANKS if b else PACK + s}")
            if b:
                wf_plane = late_s[:, a, P // 4 * (s - PACK) : P // 4 * (s - PACK + 1)]
            else:
                wf_plane = planes[a][:, V_SCALES + P // 4 * s : V_SCALES + P // 4 * (s + 1)]
            nc.tensor.matmul_mx(
                out=acc[s, c][:],
                lhsT=wf_w[b][:, a, P // 2 * t : P // 2 * (t + 1)].bitcast(FP4X4),
                lhsT_scale=wf_plane.bitcast(U8),
                rhs=v_w[a][c][:].bitcast(FP8X4),
                rhs_scale=planes[a][:, BANK // 4 * c : BANK // 4 * (c + 1)].bitcast(U8),
                start=start,
                stop=stop,
            )

        def fill_bank(s, c):
            if s >= PACK:
                first_pass(s, c, 0, True, False)
            first_pass(s, c, 1, False, True)

        def empty_bank(s, c, copy):
            copy(h[s][:, BANK * c : BANK * (c + 1)], acc[s, c][:])

        def first_product(s):
            for c in range(2):
                fill_bank(s, c)
                empty_bank(s, c, nc.scalar.copy)

        whole = SLICES - PACK
        pieces = [(0, 0, M), (1, 0, M), (2, 0, HALF), (2, HALF, QUARTER), (2, HALF + QUARTER, QUARTER)]
        gate = [keep.tile([P, M], F32, name=f"gate{s}") for s in range(whole)]
        gates = {i: keep.tile([P, PACK, pieces[i][2]], F32, name=f"gates{i}") for i in (2, 3)}
        gates[4] = placed(END_AT + 2048, [P, PACK, QUARTER], F32, "gates4")
        diffs = [keep.tile([P, PACK, M], F32, name=f"diffs{b}") for b in range(HP)]
        z_rows = [keep.tile([P, PACK, M], BF16, name=f"z_rows{b}") for b in range(HP - 1)]
        follow = [None] * SLICES

        def make_gate(i, t):
            b, m0, w = pieces[i]
            entries = pos1_sb[:, m0 // GROUP : (m0 + w) // GROUP]
            dst = gate[PACK * b + t][:] if b < HP - 1 else gates[i][:, t, :]
            nc.scalar.activation(dst, h[PACK * b + t][:].indirect(entries), ACT.Sigmoid)

        def pick_follow(s):
            if s == SLICES - 1:
                follow[s] = placed(END_AT, [P, M], F32, f"follow{s}")
            else:
                follow[s] = keep.tile([P, M], F32, name=f"follow{s}")
            if s < VECTOR_FOLLOWS:
                nc.vector.tensor_copy(follow[s][:], h[s][:].indirect(pos3_sb[:]))
            elif s == SHARED_FOLLOW:
                cut = SHARE // GROUP
                nc.vector.tensor_copy(follow[s][:, 0:SHARE], h[s][:].indirect(pos3_sb[:, 0:cut]))
                nc.scalar.activation(follow[s][:, SHARE:], h[s][:].indirect(pos3_sb[:, cut:]), ACT.Copy)
            else:
                nc.scalar.activation(follow[s][:], h[s][:].indirect(pos3_sb[:]), ACT.Copy)

        def pick_diff(s):
            nc.vector.tensor_tensor(diffs[s // PACK][:, s % PACK, :], h[s][:].indirect(pos2_sb[:]), follow[s][:], ALU.subtract)

        def apply_gain(s):
            b, t = divmod(s, PACK)
            row = diffs[b][:, t, :]
            if s < whole:
                nc.vector.scalar_tensor_tensor(
                    out=z_rows[b][:, t, :],
                    in0=row,
                    scalar=gain_sb[:, t, b : b + 1],
                    in1=gate[s][:],
                    op0=ALU.mult,
                    op1=ALU.mult,
                )
            else:
                nc.vector.tensor_scalar(row, row, gain_sb[:, t, b : b + 1], None, ALU.mult)

        def make_z(woven, gate4, diff4):
            nc.vector.tensor_tensor(
                woven.rearrange("p (c i) t -> p c t i", i=2),
                diff4.rearrange("p t (c i) -> p c t i", i=2),
                gate4.rearrange("p t (c i) -> p c t i", i=2),
                ALU.mult,
            )

        def weave(woven, src, copy=nc.vector.tensor_copy):
            copy(woven.rearrange("p (c i) t -> p c t i", i=4), src.rearrange("p t (c i) -> p c t i", i=4))

        def quantize(codes, scales, woven):
            nc.vector.quantize_mx(
                out=codes[:].bitcast(FP8X4), scales=scales[:], in_=woven[:].rearrange("p w t -> p (w t)")
            )

        ws_woven = [keep.tile([P, N, PACK], BF16, name=f"ws_woven{b}", align_bytes=64) for b in range(HP - 1)]
        ws_woven = ws_woven + [after_h(whole + 2, [P, N, PACK], BF16, "ws_woven2")]
        ws_w = [None] * HP
        ws_s = [keep.tile([P, N], U8, name=f"ws_s{b}", align_bytes=64) for b in range(HP)]
        z_woven = [None] * len(pieces)
        z_w = [None] * len(pieces)
        z_s = [keep.tile([P, w], U8, name=f"z_s{i}", align_bytes=64) for i, (b, m0, w) in enumerate(pieces)]

        def weave_ws(b):
            weave(ws_woven[b][:], ws_raw[b][:])

        def quantize_ws(b, s):
            ws_w[b] = after_h(s, [P, N], U32, f"ws_w{b}")
            quantize(ws_w[b], ws_s[b], ws_woven[b])

        def weave_z(i, woven):
            z_woven[i] = woven
            b, m0, w = pieces[i]
            if b < HP - 1:
                weave(woven[:], z_rows[b][:])
            else:
                make_z(woven[:], gates[i][:], diffs[b][:, :, m0 : m0 + w])

        def quantize_z(i, codes):
            z_w[i] = codes
            quantize(codes, z_s[i], z_woven[i])

        scores = {}

        def second_product(half, j, b):
            if b == 1:
                scores[half, j] = psum.tile([P, HALF], F32, name="score", tag=f"bank{N_TILES * half + j}")
            last = b == HP - 1
            i = b + half if last else b
            cols = slice(0, HALF) if last else slice(HALF * half, HALF * (half + 1))
            nc.tensor.matmul_mx(
                out=scores[half, j][:],
                lhsT=ws_w[b][:, P * j : P * (j + 1)].bitcast(FP8X4),
                lhsT_scale=ws_s[b][:, P * j : P * (j + 1)],
                rhs=z_w[i][:, cols].bitcast(FP8X4),
                rhs_scale=z_s[i][:, cols],
                start=(b == 1),
                stop=last,
            )

        def store(half, j):
            cols = slice(HALF * half, HALF * (half + 1))
            res = keep.tile([P, HALF], F32, name=f"res{j}")
            nc.vector.scalar_tensor_tensor(
                out=res[:],
                in0=scores[half, j][:],
                scalar=bo_sb[:, j : j + 1],
                in1=lev_sb[:, cols],
                op0=ALU.add,
                op1=ALU.mult,
            )
            nc.sync.dma_start(out=out[P * j : P * (j + 1), cols], in_=res[:])

        def store_beside(j, offset):
            biased = keep.tile([P, HALF], F32, name=f"biased{j}")
            nc.scalar.activation(biased[:], scores[0, j][:], ACT.Identity, bias=bo_sb[:, j : j + 1])
            res = placed(offset, [P, HALF], F32, f"res_beside{j}")
            nc.gpsimd.tensor_tensor(res[:], biased[:], lev_sb[:, 0:HALF], ALU.mult)
            nc.scalar.dma_start(out=out[P * j : P * (j + 1), 0:HALF], in_=res[:])

        def order_later_wf():
            order_wf(1, wf_later[:, :, 0 : PASS // 2], nc.gpsimd.tensor_copy)
            nc.gpsimd.tensor_copy(
                out=late_s[:].rearrange("p a (b t q e) -> p (a b) t q e", t=PACK, q=BLOCKS, e=2),
                in_=late_raw[:].rearrange("p a (b q t e) -> p (a b) t q e", t=PACK, q=BLOCKS, e=2),
            )
            load_ws(2, placed(EARLY_AT, [P, PACK, N], F32, "ws_raw2"))

        def products(half, passes):
            for b in passes:
                for j in range(N_TILES):
                    second_product(half, j, b)

        beside = {
            0: [lambda: order_wf(2, wf_later[:, :, PASS // 2 :], nc.vector.tensor_copy), lambda: weave_ws(0)],
            1: [lambda: weave_ws(1)],
            2: [lambda: quantize_ws(0, 2), lambda: weave_ws(2)],
            3: [lambda: quantize_ws(1, 3)],
            4: [lambda: weave_z(0, after_h(4, [P, M, PACK], BF16, "z_woven0"))],
            5: [lambda: quantize_ws(2, 5)],
            6: [lambda: quantize_z(0, after_h(6, [P, M], U32, "z_w0"))],
        }

        pairs = [psum.tile([P, 2, OPEN], F32, name=f"pair{n}", tag=f"bank{n}") for n in range(PACK)]

        def open_pass(k, s, a):
            nc.tensor.matmul_mx(
                out=pairs[2 * k + s // 2][:, s % 2, :],
                lhsT=wf_w[0][:, a, P // 2 * s : P // 2 * (s + 1)].bitcast(FP4X4),
                lhsT_scale=planes[a][:, V_SCALES + P // 4 * s : V_SCALES + P // 4 * (s + 1)].bitcast(U8),
                rhs=v_w[a][0][:, OPEN * k : OPEN * (k + 1)].bitcast(FP8X4),
                rhs_scale=planes[a][:, OPEN // 4 * k : OPEN // 4 * (k + 1)].bitcast(U8),
                start=(a == 0 and s % 2 == 0),
                stop=(a == 1 and s % 2 == 1),
            )

        for k in range(2):
            for s in range(PACK):
                open_pass(k, s, 0)
        for s in range(PACK):
            first_pass(s, 1, 0, True, False)
        for k in range(2):
            for s in range(PACK):
                open_pass(k, s, 1)
            for s in range(PACK):
                copy = nc.vector.tensor_copy if k == 1 and s >= 2 else nc.scalar.copy
                copy(h[s][:, OPEN * k : OPEN * (k + 1)], pairs[2 * k + s // 2][:, s % 2, :])
        for s in range(PACK):
            fill_bank(s, 1)
            empty_bank(s, 1, nc.vector.tensor_copy if s in (1, 2) else nc.scalar.copy)
        order_later_wf()
        pick_follow(0)
        pick_follow(1)
        pick_diff(0)
        for u in range(whole):
            if u > 1:
                first_product(u + 2)
            if u > 0:
                pick_follow(u + 1)
            make_gate(*divmod(u, PACK))
            pick_diff(u + 1)
            apply_gain(u)
            for work in beside.get(u, []):
                work()
            if u == whole - 2:
                fill_bank(whole + 2, 1)
                empty_bank(whole + 2, 1, nc.vector.tensor_copy)
        apply_gain(whole)
        weave_z(1, keep.tile([P, M, PACK], BF16, name="z_woven1", align_bytes=64))
        fill_bank(whole + 2, 0)
        empty_bank(whole + 2, 0, nc.scalar.copy)
        pick_follow(whole + 1)
        pick_diff(whole + 1)
        first_product(whole + 3)
        pick_follow(whole + 2)
        pick_follow(whole + 3)
        pick_diff(whole + 2)
        apply_gain(whole + 1)
        z_w[1] = keep.tile([P, HALF], U32, name="z_w1", align_bytes=64)
        quantize(z_w[1], z_s[1][:, 0:HALF], z_woven[1][:, 0:HALF, :])
        pick_diff(whole + 3)
        apply_gain(whole + 2)
        apply_gain(SLICES - 1)
        late_w = [placed(END_AT + 4 * QUARTER * k, [P, QUARTER], U32, f"late_w{k}") for k in range(2)]

        def quantize_late(k):
            cols = slice(HALF + QUARTER * k, HALF + QUARTER * (k + 1))
            quantize(late_w[k], z_s[1][:, cols], z_woven[1][:, cols, :])

        quantize_late(0)
        for i in range(HP - 1, len(pieces)):
            for t in range(PACK):
                make_gate(i, t)
        weave_z(2, keep.tile([P, HALF, PACK], BF16, name="z_woven2", align_bytes=64))
        quantize_late(1)
        quantize_z(2, keep.tile([P, HALF], U32, name="z_w2", align_bytes=64))

        lev_sb = placed(TAB0_AT, [P, M], F32, "lev_sb")
        nc.sync.dma_start(out=lev_sb[:], in_=lev.partition_broadcast(P))
        bo_sb = placed(TAB0_AT + 2048, [P, N_TILES], F32, "bo_sb")
        with nc.allow_non_contiguous_dma(reason="bo, one value a partition"):
            nc.sync.dma_start(out=bo_sb[:], in_=bo.rearrange("(j p) -> p j", p=P))
        products(0, (1, 0))
        ends = [psum.tile([P, 2, QUARTER], F32, name=f"end{k}", tag=f"bank{(4, 5, 1, 2)[k]}") for k in range(4)]
        end_res = [keep.tile([P, 2, QUARTER], F32, name=f"end_res{k}") for k in range(4)]

        def end_products(k, b):
            cols = slice(HALF + QUARTER * k, HALF + QUARTER * (k + 1))
            last = b == HP - 1
            codes = (z_w[0][:, cols], late_w[k][:], z_w[HP + k][:] if last else None)[b]
            for j in range(N_TILES):
                nc.tensor.matmul_mx(
                    out=ends[2 * k + j // 2][:, j % 2, :],
                    lhsT=ws_w[b][:, P * j : P * (j + 1)].bitcast(FP8X4),
                    lhsT_scale=ws_s[b][:, P * j : P * (j + 1)],
                    rhs=codes.bitcast(FP8X4),
                    rhs_scale=z_s[HP + k][:] if last else z_s[b][:, cols],
                    start=(b == 1 and j % 2 == 0),
                    stop=(last and j % 2 == 1),
                )

        def end_store(k, j):
            cols = slice(HALF + QUARTER * k, HALF + QUARTER * (k + 1))
            pair, i = divmod(j, 2)
            res = end_res[2 * k + pair]
            nc.vector.scalar_tensor_tensor(
                out=res[:, i, :],
                in0=ends[2 * k + pair][:, i, :],
                scalar=bo_sb[:, j : j + 1],
                in1=lev_sb[:, cols],
                op0=ALU.add,
                op1=ALU.mult,
            )
            if k == 1 and pair == 1:
                nc.sync.dma_start(out=out[P * j : P * (j + 1), cols], in_=res[:, i, :])
            elif i == 1:
                rows_out = out[2 * P * pair : 2 * P * (pair + 1), cols]
                nc.sync.dma_start(out=rows_out.rearrange("(i p) m -> p i m", p=P), in_=res[:])

        end_products(0, 1)
        end_products(0, 0)
        products(0, (HP - 1,))
        weave_z(3, placed(Z3_WOVEN_AT, [P, QUARTER, PACK], BF16, "z_woven3"))
        store(0, 1)
        quantize_z(3, keep.tile([P, QUARTER], U32, name="z_w3", align_bytes=64))
        end_products(0, HP - 1)
        store(0, 2)
        end_products(1, 1)
        end_products(1, 0)
        weave_z(4, placed(Z3_WOVEN_AT, [P, QUARTER, PACK], BF16, "z_woven4"))
        store(0, 3)
        quantize_z(4, keep.tile([P, QUARTER], U32, name="z_w4", align_bytes=64))
        end_products(1, HP - 1)
        store_beside(0, Z3_WOVEN_AT)
        for k in range(2):
            for j in range(N_TILES):
                end_store(k, j)
